import numpy as np
import ml_dtypes


def mxq(x, axis, fmt="e4m3"):
    dtype, down = {"e4m3": (ml_dtypes.float8_e4m3fn, 7), "e5m2": (ml_dtypes.float8_e5m2, 14)}[fmt]
    v = np.moveaxis(np.asarray(x, np.float32).astype(ml_dtypes.bfloat16).astype(np.float64), axis, -1)
    blocks = v.reshape(v.shape[:-1] + (-1, 32))
    amax = np.abs(blocks).max(-1, keepdims=True)
    byte = np.maximum(np.where(amax > 0, np.frexp(amax)[1] - 1 + 127, 0) - down, 1)
    scale = np.exp2(byte - 127.0)
    codes = (blocks / scale).astype(np.float32).astype(dtype).astype(np.float64)
    return np.moveaxis((codes * scale).reshape(v.shape), -1, axis)


WIDE = False


def mx_kscale(k):
    if not WIDE:
        return np.ones(k)
    levels = np.array([18, -18])
    if k % 512:
        return np.exp2(np.random.permutation(np.resize(levels, k // 32))).repeat(32)
    a = np.empty((k // 512, 16))
    for p in range(k // 512):
        a[p, :8] = np.random.permutation(np.resize(levels, 8))
        for g in range(8):
            far = levels[np.abs(levels - a[p, g]) >= 10]
            a[p, g + 8] = far[np.random.randint(len(far))]
    return np.exp2(a.ravel()).repeat(32)


def f64(x):
    return np.asarray(x).astype(np.float64)


def striped(idx):
    return np.tile(np.asarray(idx).reshape(-1, 16).T, (8, 1)).astype(np.uint16)


def unstriped(offs):
    return offs[:16].T.reshape(-1).astype(np.int64)


B, N, T, D, DV, R = 2, 512, 2048, 512, 512, 512


def setup_inputs():
    n = np.random.standard_normal
    idx = np.random.permutation(T)[:B * N]
    s = mx_kscale(D)[:, None]
    z = mx_kscale(R)[:, None]
    q = n((B, D, R))
    do = n((B, DV, R))
    return {
        "qT": (q * s).astype(np.float32),
        "kT": (n((D, T)) * (1.00 / np.sqrt(D)) / s).astype(np.float32),
        "rw": (np.random.uniform(0.5, 1.5, (B, R, 1)) * 1.0 / np.sqrt(R) * z).astype(np.float32),
        "dom": (do.transpose(0, 2, 1) / z).astype(np.float32),
        "offs": striped(idx),
    }


def reference(qT, kT, rw, dom, offs):
    idx = unstriped(offs)
    pick = lambda x: x[:, idx].reshape(x.shape[0], B, N).transpose(1, 0, 2)
    a = mxq(f64(qT), 1, "e4m3").transpose(0, 2, 1) @ mxq(pick(f64(kT)), 1, "e4m3")
    p = 1.0 / (1.0 + np.exp(-a))
    dv = mxq(f64(dom), 1, "e5m2").transpose(0, 2, 1) @ mxq(f64(rw) * p, 1, "e4m3")
    gv = np.zeros((DV, T))
    gv[:, idx] = dv.transpose(1, 0, 2).reshape(DV, B * N)
    return gv

@@ -1,0 +1,179 @@
+from contextlib import ExitStack
+
+import concourse.mybir as mybir
+
+B, N, T, D, DV, R = 2, 512, 2048, 512, 512, 512
+FLOPS = 2 * B * R * N * D + 2 * B * DV * N * R
+
+F32 = mybir.dt.float32
+BF16 = mybir.dt.bfloat16
+U32 = mybir.dt.uint32
+U16 = mybir.dt.uint16
+U8 = mybir.dt.uint8
+E4M3 = mybir.dt.float8_e4m3fn_x4
+E5M2 = mybir.dt.float8_e5m2_x4
+COPY = mybir.ActivationFunctionType.Copy
+SIGMOID = mybir.ActivationFunctionType.Sigmoid
+MULT = mybir.AluOpType.mult
+
+P = 128
+PACK = 4
+LIST_COLS = N // 16
+KEY_CHUNKS = (((512, 512), (512, 512), (512, 256), (512, 256)), ((512, 512), (512, 512), (512, 256), (256, 128), (256, 96)))
+
+
+def tile_attend_gat_sig_v_kernel(tc, qT, kT, rw, dom, offs, out):
+    nc = tc.nc
+    with ExitStack() as ctx:
+        keep = ctx.enter_context(tc.tile_pool(name="keep", bufs=1))
+        psum = ctx.enter_context(tc.psum_pool(name="psum", bufs=4))
+
+        def tile(name, shape, dtype):
+            return keep.tile(shape, dtype, name=name, align_bytes=64)
+
+        def scalar_cast(dst, src):
+            nc.scalar.activation(out=dst, in_=src, func=COPY)
+
+        def vector_cast(dst, src):
+            nc.vector.tensor_copy(out=dst, in_=src)
+
+        offsets = keep.tile([P, B * LIST_COLS], U16, name="offsets")
+        nc.sync.dma_start(offsets[:], offs)
+
+        gate = [tile("gate%d" % b, [P, 1, PACK], F32) for b in range(B)]
+        for b in range(B):
+            nc.scalar.dma_start(out=gate[b][:, 0, :], in_=rw[b].rearrange("(p t) o -> p (t o)", t=PACK))
+
+        warm_in = tile("warm_in", [P, 1], F32)
+        warm_out = tile("warm_out", [P, 1], F32)
+        nc.gpsimd.memset(warm_in[:], 0.0)
+        nc.scalar.activation(out=warm_out[:], in_=warm_in[:], func=SIGMOID)
+
+        window = [tile("window%d" % m, [P, T], F32) for m in range(DV // P)]
+
+        def seq_offsets(b, lo=0, hi=N):
+            return offsets[:, b * LIST_COLS + lo // 16 : b * LIST_COLS + hi // 16]
+
+        key_rows = kT.rearrange("(p u e) t -> u p e t", u=2, e=2)
+        key_pairs = [tile("key_pairs%d" % u, [P, T], U32) for u in range(2)]
+        picked = [tile("picked%d" % b, [P, N, 2], U32) for b in range(B)]
+
+        def gather(b, u, lo=0, hi=N):
+            nc.vector.tensor_copy(picked[b][:, lo:hi, u], key_pairs[u][:].indirect(seq_offsets(b, lo, hi)))
+
+        for u in range(2):
+            pairs = key_pairs[u][:].bitcast(BF16).rearrange("p (t e) -> p t e", e=2)
+            t0 = 0
+            for i, (w, h) in enumerate(KEY_CHUNKS[u]):
+                raw = tile("key_raw%d_%d" % (u, i), [P, 2, w], F32)
+                nc.sync.dma_start(out=raw[:], in_=key_rows[u][:, :, t0 : t0 + w])
+                scalar_cast(pairs[:, t0 : t0 + h, :], raw[:, :, 0:h].rearrange("p e t -> p t e"))
+                if h < w:
+                    vector_cast(pairs[:, t0 + h : t0 + w, :], raw[:, :, h:w].rearrange("p e t -> p t e"))
+                t0 += w
+            if u == 0:
+                for b in range(B):
+                    gather(b, 0)
+
+        def load_rows(name, src, c0, w):
+            raw = tile(name, [P, PACK, w], F32)
+            nc.sync.dma_start(out=raw[:], in_=src.rearrange("(p j) c -> p j c", j=PACK)[:, :, c0 : c0 + w])
+            return raw
+
+        H = 256
+        q_raw = {}
+        dom_raw = {}
+        for b in range(B):
+            for h in range(2):
+                q_raw[b, h] = load_rows("q_raw%d_%d" % (b, h), qT[b], h * H, H)
+            for h in range(2):
+                dom_raw[b, h] = load_rows("dom_raw%d_%d" % (b, h), dom[b], h * H, H)
+
+        def quantise(name, src, words, fmt):
+            codes = tile(name + "_codes", [P, words], U32)
+            scales = tile(name + "_scales", [P, words], U8)
+            nc.vector.quantize_mx(out=codes[:].bitcast(fmt), scales=scales[:], in_=src)
+            return codes, scales
+
+        def front(b):
+            keys = []
+            for h in range(2):
+                gather(b, 1, h * H, (h + 1) * H)
+            for h in range(2):
+                src = picked[b][:, h * H : (h + 1) * H, :].rearrange("p n u -> p (n u)").bitcast(BF16)
+                keys.append(quantise("key%d_%d" % (b, h), src, H, E4M3))
+            q_grouped = tile("q_grouped%d" % b, [P, PACK, P, PACK], BF16)
+            q_view = q_grouped[:].rearrange("p t m j -> p m t j")
+            for h in range(2):
+                src = q_raw[b, h][:].rearrange("p j (m t) -> p m t j", t=PACK)
+                if b == 0 and h == 1:
+                    scalar_cast(q_view[:, 64:88], src[:, 0:24])
+                    vector_cast(q_view[:, 88:128], src[:, 24:64])
+                else:
+                    scalar_cast(q_view[:, 64 * h : 64 * h + 32], src[:, 0:32])
+                    scalar_cast(q_view[:, 64 * h + 32 : 64 * h + 64], src[:, 32:64])
+            q_codes, q_scales = quantise("q%d" % b, q_grouped[:].rearrange("p t m j -> p (t m j)"), R, E4M3)
+            pw_codes = tile("pw_codes%d" % b, [P, N], U32)
+            pw_scales = tile("pw_scales%d" % b, [P, N], U8)
+            for c in range(N // P):
+                scores = psum.tile([P, PACK, P], F32, name="scores")
+                k_codes, k_scales = keys[c // 2]
+                cols = slice((c % 2) * P, (c % 2 + 1) * P)
+                for t in range(PACK):
+                    nc.tensor.matmul_mx(
+                        out=scores[:, t, :],
+                        lhsT=q_codes[:, t * P : (t + 1) * P].bitcast(E4M3),
+                        lhsT_scale=q_scales[:, t * P : (t + 1) * P],
+                        rhs=k_codes[:, cols].bitcast(E4M3),
+                        rhs_scale=k_scales[:, cols],
+                        start=True,
+                        stop=True,
+                    )
+                prob = tile("prob%d_%d" % (b, c), [P, P, PACK], F32)
+                nc.scalar.activation(out=prob[:], in_=scores[:].rearrange("p t n -> p n t"), func=SIGMOID)
+                pw = tile("pw%d_%d" % (b, c), [P, P, PACK], BF16)
+                nc.vector.tensor_tensor(out=pw[:], in0=prob[:], in1=gate[b][:].broadcast_to([P, P, PACK]), op=MULT)
+                nc.vector.quantize_mx(
+                    out=pw_codes[:, c * P : (c + 1) * P].bitcast(E4M3),
+                    scales=pw_scales[:, c * P : (c + 1) * P],
+                    in_=pw[:].rearrange("p n t -> p (n t)"),
+                )
+            return pw_codes, pw_scales
+
+        def dom_block(b, m, cast):
+            grouped = tile("dom_grouped%d_%d" % (b, m), [P, P, PACK], BF16)
+            cast(grouped[:], dom_raw[b, m // 2][:, :, (m % 2) * P : (m % 2 + 1) * P].rearrange("p j e -> p e j"))
+            return quantise("dom%d_%d" % (b, m), grouped[:].rearrange("p e j -> p (e j)"), P, E5M2)
+
+        def product(b, m, dom_q, pw_q):
+            acc = psum.tile([P, N], F32, name="acc")
+            nc.tensor.matmul_mx(
+                out=acc[:],
+                lhsT=dom_q[0][:].bitcast(E5M2),
+                lhsT_scale=dom_q[1][:],
+                rhs=pw_q[0][:].bitcast(E4M3),
+                rhs_scale=pw_q[1][:],
+                start=True,
+                stop=True,
+            )
+            dense = tile("dense%d_%d" % (b, m), [P, N], F32)
+            scalar_cast(dense[:], acc[:])
+            return dense
+
+        dense = {}
+        for b in range(B):
+            first = dom_block(b, 0, vector_cast if b == 0 else scalar_cast)
+            pw_q = front(b)
+            for m in range(DV // P):
+                dom_q = first if m == 0 else dom_block(b, m, scalar_cast)
+                dense[b, m] = product(b, m, dom_q, pw_q)
+
+        for m in range(DV // P):
+            for h in range(2):
+                nc.vector.memset(window[m][:, h * T // 2 : (h + 1) * T // 2], 0.0)
+
+        for b in range(B):
+            for m in range(DV // P):
+                nc.vector.tensor_copy(window[m][:].indirect(seq_offsets(b)), dense[b, m][:])
+                if b == B - 1:
+                    nc.sync.dma_start(out=out[m * P : (m + 1) * P, :], in_=window[m][:])

@@ -19,7 +19,7 @@ MULT = mybir.AluOpType.mult
 P = 128
 PACK = 4
 LIST_COLS = N // 16
-KEY_CHUNKS = (((512, 512), (512, 512), (512, 256), (512, 256)), ((512, 512), (512, 512), (512, 256), (256, 128), (256, 96)))
+KEY_CHUNKS = (((1024, 1024), (1024, 512)), ((1024, 640), (512, 256), (512, 192)))
 
 
 def tile_attend_gat_sig_v_kernel(tc, qT, kT, rw, dom, offs, out):
@@ -50,6 +50,11 @@ def tile_attend_gat_sig_v_kernel(tc, qT, kT, rw, dom, offs, out):
         nc.scalar.activation(out=warm_out[:], in_=warm_in[:], func=SIGMOID)
 
         window = [tile("window%d" % m, [P, T], F32) for m in range(DV // P)]
+
+        for m in range(2):
+            nc.vector.memset(window[m][:, 0:1023], 0.0)
+            nc.vector.memset(window[m][:, 1023:T], 0.0)
+            nc.gpsimd.memset(window[2 + m][:], 0.0)
 
         def seq_offsets(b, lo=0, hi=N):
             return offsets[:, b * LIST_COLS + lo // 16 : b * LIST_COLS + hi // 16]
@@ -89,91 +94,137 @@ def tile_attend_gat_sig_v_kernel(tc, qT, kT, rw, dom, offs, out):
             for h in range(2):
                 dom_raw[b, h] = load_rows("dom_raw%d_%d" % (b, h), dom[b], h * H, H)
 
-        def quantise(name, src, words, fmt):
-            codes = tile(name + "_codes", [P, words], U32)
-            scales = tile(name + "_scales", [P, words], U8)
-            nc.vector.quantize_mx(out=codes[:].bitcast(fmt), scales=scales[:], in_=src)
-            return codes, scales
+        def operand(name, words):
+            return tile(name + "_codes", [P, words], U32), tile(name + "_scales", [P, words], U8)
 
-        def front(b):
-            keys = []
-            for h in range(2):
-                gather(b, 1, h * H, (h + 1) * H)
-            for h in range(2):
-                src = picked[b][:, h * H : (h + 1) * H, :].rearrange("p n u -> p (n u)").bitcast(BF16)
-                keys.append(quantise("key%d_%d" % (b, h), src, H, E4M3))
-            q_grouped = tile("q_grouped%d" % b, [P, PACK, P, PACK], BF16)
-            q_view = q_grouped[:].rearrange("p t m j -> p m t j")
-            for h in range(2):
-                src = q_raw[b, h][:].rearrange("p j (m t) -> p m t j", t=PACK)
-                if b == 0 and h == 1:
-                    scalar_cast(q_view[:, 64:88], src[:, 0:24])
-                    vector_cast(q_view[:, 88:128], src[:, 24:64])
-                else:
-                    scalar_cast(q_view[:, 64 * h : 64 * h + 32], src[:, 0:32])
-                    scalar_cast(q_view[:, 64 * h + 32 : 64 * h + 64], src[:, 32:64])
-            q_codes, q_scales = quantise("q%d" % b, q_grouped[:].rearrange("p t m j -> p (t m j)"), R, E4M3)
-            pw_codes = tile("pw_codes%d" % b, [P, N], U32)
-            pw_scales = tile("pw_scales%d" % b, [P, N], U8)
-            for c in range(N // P):
-                scores = psum.tile([P, PACK, P], F32, name="scores")
-                k_codes, k_scales = keys[c // 2]
-                cols = slice((c % 2) * P, (c % 2 + 1) * P)
-                for t in range(PACK):
-                    nc.tensor.matmul_mx(
-                        out=scores[:, t, :],
-                        lhsT=q_codes[:, t * P : (t + 1) * P].bitcast(E4M3),
-                        lhsT_scale=q_scales[:, t * P : (t + 1) * P],
-                        rhs=k_codes[:, cols].bitcast(E4M3),
-                        rhs_scale=k_scales[:, cols],
-                        start=True,
-                        stop=True,
-                    )
-                prob = tile("prob%d_%d" % (b, c), [P, P, PACK], F32)
-                nc.scalar.activation(out=prob[:], in_=scores[:].rearrange("p t n -> p n t"), func=SIGMOID)
-                pw = tile("pw%d_%d" % (b, c), [P, P, PACK], BF16)
-                nc.vector.tensor_tensor(out=pw[:], in0=prob[:], in1=gate[b][:].broadcast_to([P, P, PACK]), op=MULT)
-                nc.vector.quantize_mx(
-                    out=pw_codes[:, c * P : (c + 1) * P].bitcast(E4M3),
-                    scales=pw_scales[:, c * P : (c + 1) * P],
-                    in_=pw[:].rearrange("p n t -> p (n t)"),
-                )
-            return pw_codes, pw_scales
+        def quantise(dst, cols, src, fmt):
+            nc.vector.quantize_mx(out=dst[0][:, cols].bitcast(fmt), scales=dst[1][:, cols], in_=src)
 
-        def dom_block(b, m, cast):
-            grouped = tile("dom_grouped%d_%d" % (b, m), [P, P, PACK], BF16)
-            cast(grouped[:], dom_raw[b, m // 2][:, :, (m % 2) * P : (m % 2 + 1) * P].rearrange("p j e -> p e j"))
-            return quantise("dom%d_%d" % (b, m), grouped[:].rearrange("p e j -> p (e j)"), P, E5M2)
-
-        def product(b, m, dom_q, pw_q):
-            acc = psum.tile([P, N], F32, name="acc")
+        def multiply(acc, lhs, lhs_cols, lhs_fmt, rhs, rhs_cols):
             nc.tensor.matmul_mx(
-                out=acc[:],
-                lhsT=dom_q[0][:].bitcast(E5M2),
-                lhsT_scale=dom_q[1][:],
-                rhs=pw_q[0][:].bitcast(E4M3),
-                rhs_scale=pw_q[1][:],
+                out=acc,
+                lhsT=lhs[0][:, lhs_cols].bitcast(lhs_fmt),
+                lhsT_scale=lhs[1][:, lhs_cols],
+                rhs=rhs[0][:, rhs_cols].bitcast(E4M3),
+                rhs_scale=rhs[1][:, rhs_cols],
                 start=True,
                 stop=True,
             )
-            dense = tile("dense%d_%d" % (b, m), [P, N], F32)
-            scalar_cast(dense[:], acc[:])
-            return dense
 
-        dense = {}
-        for b in range(B):
-            first = dom_block(b, 0, vector_cast if b == 0 else scalar_cast)
-            pw_q = front(b)
-            for m in range(DV // P):
-                dom_q = first if m == 0 else dom_block(b, m, scalar_cast)
-                dense[b, m] = product(b, m, dom_q, pw_q)
+        def half(h):
+            return slice(h * H, (h + 1) * H)
 
-        for m in range(DV // P):
+        def block(c):
+            return slice(c * P, (c + 1) * P)
+
+        q_grouped = [tile("q_grouped%d" % b, [P, PACK, P, PACK], BF16) for b in range(B)]
+        keys = [operand("key", N)] * B
+        queries = [operand("query%d" % b, R) for b in range(B)]
+        weights = [operand("weight%d" % b, N) for b in range(B)]
+        grads = [operand("grad%d" % b, DV) for b in range(B)]
+
+        def gather_last(b):
             for h in range(2):
-                nc.vector.memset(window[m][:, h * T // 2 : (h + 1) * T // 2], 0.0)
+                gather(b, 1, h * H, (h + 1) * H)
 
-        for b in range(B):
-            for m in range(DV // P):
-                nc.vector.tensor_copy(window[m][:].indirect(seq_offsets(b)), dense[b, m][:])
-                if b == B - 1:
-                    nc.sync.dma_start(out=out[m * P : (m + 1) * P, :], in_=window[m][:])
+        def quantise_keys(b):
+            for h in range(2):
+                quantise(keys[b], half(h), picked[b][:, half(h), :].rearrange("p n u -> p (n u)").bitcast(BF16), E4M3)
+
+        def quantise_queries(b):
+            grouped = q_grouped[b]
+            view = grouped[:].rearrange("p t m j -> p m j t")
+            for h in range(2):
+                src = q_raw[b, h][:].rearrange("p j (m t) -> p m j t", t=PACK)
+                scalar_cast(view[:, 64 * h : 64 * h + 64], src)
+            if b == 0:
+                for t in range(PACK):
+                    quantise(queries[b], block(t), grouped[:, t].rearrange("p m j -> p (m j)"), E4M3)
+            else:
+                quantise(queries[b], slice(0, R), grouped[:].rearrange("p t m j -> p (t m j)"), E4M3)
+
+        def quantise_grad(b, lo, hi):
+            grouped = tile("dom_grouped%d_%d" % (b, lo), [P, hi - lo, PACK], BF16)
+            scalar_cast(
+                grouped[:].rearrange("p (c i) j -> p c j i", i=4),
+                dom_raw[b, lo // H][:, :, lo % H : lo % H + hi - lo].rearrange("p j (c i) -> p c j i", i=4),
+            )
+            quantise(grads[b], slice(lo, hi), grouped[:].rearrange("p e j -> p (e j)"), E5M2)
+
+        def score(b, c):
+            scores = psum.tile([P, PACK, P], F32, name="scores")
+            for t in range(PACK):
+                multiply(scores[:, t, :], queries[b], block(t), E4M3, keys[b], block(c))
+            return scores
+
+        def weigh_on_vector(b, c):
+            scores = score(b, c)
+            prob = tile("prob%d_%d" % (b, c), [P, P, PACK], F32)
+            nc.scalar.activation(out=prob[:], in_=scores[:].rearrange("p t n -> p n t"), func=SIGMOID)
+            pw = tile("pw%d_%d" % (b, c), [P, P, PACK], BF16)
+            nc.vector.tensor_tensor(out=pw[:], in0=prob[:], in1=gate[b][:].broadcast_to([P, P, PACK]), op=MULT)
+            quantise(weights[b], block(c), pw[:].rearrange("p n t -> p (n t)"), E4M3)
+
+        def weigh_on_scalar(b, h):
+            prob = tile("prob%d_%d" % (b, h), [P, PACK, H], F32)
+            for c in range(2):
+                nc.scalar.activation(out=prob[:, :, block(c)], in_=score(b, 2 * h + c)[:], func=SIGMOID)
+            planes = tile("planes%d_%d" % (b, h), [P, PACK, H], BF16)
+            for t in range(PACK):
+                nc.scalar.activation(out=planes[:, t, :], in_=prob[:, t, :], func=COPY, scale=gate[b][:, 0, t : t + 1])
+            pw = tile("pw%d_%d" % (b, h), [P, H, PACK], BF16)
+            nc.scalar.copy(
+                out=pw[:].rearrange("p (c i) t -> p c t i", i=4),
+                in_=planes[:].rearrange("p t (c i) -> p c t i", i=4),
+            )
+            quantise(weights[b], half(h), pw[:].rearrange("p n t -> p (n t)"), E4M3)
+            return planes[:].rearrange("p t c -> p (t c)").bitcast(F32)
+
+        def product(b, m):
+            acc = psum.tile([P, N], F32, name="acc")
+            multiply(acc[:], grads[b], block(m), E5M2, weights[b], slice(0, N))
+            return acc
+
+        pieces = []
+
+        def copy_out(b, m, acc, lo, hi, dense):
+            scalar_cast(dense, acc[:, lo:hi])
+            pieces.append((b, m, lo, hi, dense))
+
+        gather_last(0)
+        quantise_keys(0)
+        quantise_queries(0)
+        quantise_grad(0, 0, P)
+        for c in range(N // P):
+            weigh_on_vector(0, c)
+        gather_last(1)
+        acc = product(0, 0)
+        first = tile("dense0_0", [P, N], F32)
+        for h in range(2):
+            copy_out(0, 0, acc, h * H, (h + 1) * H, first[:, half(h)])
+        for m in range(1, DV // P):
+            quantise_grad(0, m * P, (m + 1) * P)
+        quantise_keys(1)
+        quantise_queries(1)
+        for m in (1, 2):
+            acc = product(0, m)
+            dense = q_raw[1, 1][:, 2 * m - 2 : 2 * m, :].rearrange("p j c -> p (j c)")
+            scalar_cast(dense, acc[:])
+            for h in range(2):
+                pieces.append((0, m, h * H, (h + 1) * H, dense[:, half(h)]))
+        quantise_grad(1, 0, P)
+        acc = product(0, 3)
+        for h in range(2):
+            spent = weigh_on_scalar(1, h)
+            copy_out(0, 3, acc, h * H, (h + 1) * H, spent[:, 0:H])
+        for m in range(DV // P):
+            if m > 0:
+                quantise_grad(1, m * P, (m + 1) * P)
+            acc = product(1, m)
+            copy_out(1, m, acc, 0, N, tile("dense1_%d" % m, [P, N], F32)[:])
+
+        for b, m, lo, hi, dense in pieces:
+            nc.vector.tensor_copy(window[m][:].indirect(seq_offsets(b, lo, hi)), dense)
+            if b == B - 1:
+                for queue, cols in ((nc.sync, slice(0, T // 2)), (nc.scalar, slice(T // 2, T))):
+                    queue.dma_start(out=out[block(m), cols], in_=window[m][:, cols])

@@ -8,6 +8,7 @@ FLOPS = 2 * B * R * N * D + 2 * B * DV * N * R
 F32 = mybir.dt.float32
 BF16 = mybir.dt.bfloat16
 U32 = mybir.dt.uint32
+I32 = mybir.dt.int32
 U16 = mybir.dt.uint16
 U8 = mybir.dt.uint8
 E4M3 = mybir.dt.float8_e4m3fn_x4
@@ -19,7 +20,7 @@ MULT = mybir.AluOpType.mult
 P = 128
 PACK = 4
 LIST_COLS = N // 16
-KEY_CHUNKS = (((1024, 1024), (1024, 512)), ((1024, 640), (512, 256), (512, 192)))
+KEY_CHUNKS = (((1024, 1024), (1024, 640)), ((1024, 896), (512, 320), (512, 192)))
 
 
 def tile_attend_gat_sig_v_kernel(tc, qT, kT, rw, dom, offs, out):
@@ -61,10 +62,17 @@ def tile_attend_gat_sig_v_kernel(tc, qT, kT, rw, dom, offs, out):
 
         key_rows = kT.rearrange("(p u e) t -> u p e t", u=2, e=2)
         key_pairs = [tile("key_pairs%d" % u, [P, T], U32) for u in range(2)]
-        picked = [tile("picked%d" % b, [P, N, 2], U32) for b in range(B)]
+        pw_room = tile("pw_room", [P, 7 * N], BF16)
+        picked = [
+            tile("picked0", [P, N, 2], U32)[:],
+            pw_room[:, 3 * N : 7 * N].bitcast(U32).rearrange("p (n u) -> p n u", u=2),
+        ]
+        shared = tile("shared", [P, 3, N], F32)
+        planes1 = shared[:, 0:2, :].rearrange("p u n -> p (u n)").bitcast(U32).rearrange("p (u n) -> p u n", u=2)
 
-        def gather(b, u, lo=0, hi=N):
-            nc.vector.tensor_copy(picked[b][:, lo:hi, u], key_pairs[u][:].indirect(seq_offsets(b, lo, hi)))
+        def gather(b, u):
+            dst = picked[0][:, :, u] if b == 0 else planes1[:, u, :]
+            nc.vector.tensor_copy(dst, key_pairs[u][:].indirect(seq_offsets(b)))
 
         for u in range(2):
             pairs = key_pairs[u][:].bitcast(BF16).rearrange("p (t e) -> p t e", e=2)
@@ -81,8 +89,11 @@ def tile_attend_gat_sig_v_kernel(tc, qT, kT, rw, dom, offs, out):
                     gather(b, 0)
 
         def load_rows(name, src, c0, w):
-            raw = tile(name, [P, PACK, w], F32)
-            nc.sync.dma_start(out=raw[:], in_=src.rearrange("(p j) c -> p j c", j=PACK)[:, :, c0 : c0 + w])
+            if name == "q_raw0_1":
+                raw = shared[:, 1:3, :].rearrange("p a (j c) -> p (a j) c", j=2)
+            else:
+                raw = tile(name, [P, PACK, w], F32)[:]
+            nc.sync.dma_start(out=raw, in_=src.rearrange("(p j) c -> p j c", j=PACK)[:, :, c0 : c0 + w])
             return raw
 
         H = 256
@@ -117,39 +128,54 @@ def tile_attend_gat_sig_v_kernel(tc, qT, kT, rw, dom, offs, out):
         def block(c):
             return slice(c * P, (c + 1) * P)
 
-        q_grouped = [tile("q_grouped%d" % b, [P, PACK, P, PACK], BF16) for b in range(B)]
+        probs = tile("probs0", [P, 4 * N + 3 * H], F32)
+        prob_at = (0, N, 3 * N, 2 * N)
+        q_grouped = [
+            tile("q_grouped0", [P, PACK, P, PACK], BF16)[:],
+            probs[:, 3 * N + H : 5 * N + H].bitcast(BF16).rearrange("p (t m j) -> p t m j", t=PACK, j=PACK),
+        ]
         keys = [operand("key", N)] * B
         queries = [operand("query%d" % b, R) for b in range(B)]
         weights = [operand("weight%d" % b, N) for b in range(B)]
         grads = [operand("grad%d" % b, DV) for b in range(B)]
 
-        def gather_last(b):
-            for h in range(2):
-                gather(b, 1, h * H, (h + 1) * H)
-
         def quantise_keys(b):
-            for h in range(2):
-                quantise(keys[b], half(h), picked[b][:, half(h), :].rearrange("p n u -> p (n u)").bitcast(BF16), E4M3)
+            quantise(keys[b], slice(0, N), picked[b].rearrange("p n u -> p (n u)").bitcast(BF16), E4M3)
+
+        def interleave_keys():
+            src = shared[:, 0:2, :].rearrange("p u n -> p (u n)").bitcast(I32).rearrange("p (u n) -> p n u", u=2)
+            dst = picked[1].rearrange("p n u -> p (n u)").bitcast(I32).rearrange("p (n u) -> p n u", u=2)
+            nc.vector.tensor_copy(out=dst, in_=src)
 
         def quantise_queries(b):
             grouped = q_grouped[b]
-            view = grouped[:].rearrange("p t m j -> p m j t")
+            view = grouped.rearrange("p t m j -> p m j t")
             for h in range(2):
-                src = q_raw[b, h][:].rearrange("p j (m t) -> p m j t", t=PACK)
-                scalar_cast(view[:, 64 * h : 64 * h + 64], src)
+                src = q_raw[b, h].rearrange("p j (m t) -> p m j t", t=PACK)
+                if (b, h) == (0, 1):
+                    scalar_cast(view[:, 64:92], src[:, 0:28])
+                    vector_cast(view[:, 92:128], src[:, 28:64])
+                elif b == 0:
+                    scalar_cast(view[:, 0:64], src)
+                else:
+                    for i in range(2):
+                        scalar_cast(view[:, 64 * h + 32 * i : 64 * h + 32 * i + 32], src[:, 32 * i : 32 * i + 32])
             if b == 0:
                 for t in range(PACK):
                     quantise(queries[b], block(t), grouped[:, t].rearrange("p m j -> p (m j)"), E4M3)
             else:
-                quantise(queries[b], slice(0, R), grouped[:].rearrange("p t m j -> p (t m j)"), E4M3)
+                quantise(queries[b], slice(0, R), grouped.rearrange("p t m j -> p (t m j)"), E4M3)
 
-        def quantise_grad(b, lo, hi):
-            grouped = tile("dom_grouped%d_%d" % (b, lo), [P, hi - lo, PACK], BF16)
+        def quantise_grad(b, m, room):
             scalar_cast(
-                grouped[:].rearrange("p (c i) j -> p c j i", i=4),
-                dom_raw[b, lo // H][:, :, lo % H : lo % H + hi - lo].rearrange("p j (c i) -> p c j i", i=4),
+                room.rearrange("p (c i j) -> p c j i", i=4, j=PACK),
+                dom_raw[b, m // 2][:, :, block(m % 2)].rearrange("p j (c i) -> p c j i", i=4),
             )
-            quantise(grads[b], slice(lo, hi), grouped[:].rearrange("p e j -> p (e j)"), E5M2)
+            quantise(grads[b], block(m), room, E5M2)
+
+        def rooms(spent):
+            flat = spent.bitcast(BF16)
+            return [flat[:, i * N : (i + 1) * N] for i in range(flat.shape[1] // N)]
 
         def score(b, c):
             scores = psum.tile([P, PACK, P], F32, name="scores")
@@ -157,13 +183,11 @@ def tile_attend_gat_sig_v_kernel(tc, qT, kT, rw, dom, offs, out):
                 multiply(scores[:, t, :], queries[b], block(t), E4M3, keys[b], block(c))
             return scores
 
-        def weigh_on_vector(b, c):
+        def weigh_on_vector(b, c, pw):
             scores = score(b, c)
-            prob = tile("prob%d_%d" % (b, c), [P, P, PACK], F32)
-            nc.scalar.activation(out=prob[:], in_=scores[:].rearrange("p t n -> p n t"), func=SIGMOID)
-            pw = tile("pw%d_%d" % (b, c), [P, P, PACK], BF16)
-            nc.vector.tensor_tensor(out=pw[:], in0=prob[:], in1=gate[b][:].broadcast_to([P, P, PACK]), op=MULT)
-            quantise(weights[b], block(c), pw[:].rearrange("p n t -> p (n t)"), E4M3)
+            prob = probs[:, prob_at[c] : prob_at[c] + N].rearrange("p (n t) -> p n t", t=PACK)
+            nc.scalar.activation(out=prob, in_=scores[:].rearrange("p t n -> p n t"), func=SIGMOID)
+            nc.vector.tensor_tensor(out=pw[:, block(c), :], in0=prob, in1=gate[b][:].broadcast_to([P, P, PACK]), op=MULT)
 
         def weigh_on_scalar(b, h):
             prob = tile("prob%d_%d" % (b, h), [P, PACK, H], F32)
@@ -178,7 +202,7 @@ def tile_attend_gat_sig_v_kernel(tc, qT, kT, rw, dom, offs, out):
                 in_=planes[:].rearrange("p t (c i) -> p c t i", i=4),
             )
             quantise(weights[b], half(h), pw[:].rearrange("p n t -> p (n t)"), E4M3)
-            return planes[:].rearrange("p t c -> p (t c)").bitcast(F32)
+            return planes[:].rearrange("p t c -> p (t c)").bitcast(F32), prob[:].rearrange("p t c -> p (t c)")
 
         def product(b, m):
             acc = psum.tile([P, N], F32, name="acc")
@@ -191,40 +215,46 @@ def tile_attend_gat_sig_v_kernel(tc, qT, kT, rw, dom, offs, out):
             scalar_cast(dense, acc[:, lo:hi])
             pieces.append((b, m, lo, hi, dense))
 
-        gather_last(0)
+        def scatter(count):
+            for b, m, lo, hi, dense in pieces[:count]:
+                nc.vector.tensor_copy(window[m][:].indirect(seq_offsets(b, lo, hi)), dense)
+                if b == B - 1:
+                    for queue, cols in ((nc.sync, slice(0, T // 2)), (nc.scalar, slice(T // 2, T))):
+                        queue.dma_start(out=out[block(m), cols], in_=window[m][:, cols])
+            pieces[:count] = []
+
+        gather(0, 1)
         quantise_keys(0)
         quantise_queries(0)
-        quantise_grad(0, 0, P)
+        gather(1, 1)
+        quantise_grad(0, 0, tile("grad_room", [P, N], BF16)[:])
+        pw = pw_room[:, 0 : PACK * N].rearrange("p (n t) -> p n t", t=PACK)
         for c in range(N // P):
-            weigh_on_vector(0, c)
-        gather_last(1)
+            weigh_on_vector(0, c, pw)
+        quantise(weights[0], slice(0, N), pw_room[:, 0 : PACK * N], E4M3)
+        quantise_grad(0, 1, probs[:, 3 * N : 3 * N + H].bitcast(BF16))
         acc = product(0, 0)
         first = tile("dense0_0", [P, N], F32)
         for h in range(2):
             copy_out(0, 0, acc, h * H, (h + 1) * H, first[:, half(h)])
-        for m in range(1, DV // P):
-            quantise_grad(0, m * P, (m + 1) * P)
+        for m in (2, 3):
+            quantise_grad(0, m, rooms(probs[:, 2 * N : 3 * N])[m - 2])
+        interleave_keys()
         quantise_keys(1)
         quantise_queries(1)
         for m in (1, 2):
-            acc = product(0, m)
-            dense = q_raw[1, 1][:, 2 * m - 2 : 2 * m, :].rearrange("p j c -> p (j c)")
-            scalar_cast(dense, acc[:])
-            for h in range(2):
-                pieces.append((0, m, h * H, (h + 1) * H, dense[:, half(h)]))
-        quantise_grad(1, 0, P)
+            copy_out(0, m, product(0, m), 0, N, q_raw[1, 1][:, 2 * m - 2 : 2 * m, :].rearrange("p j c -> p (j c)"))
+        scatter(2)
+        for m in (0, 1):
+            quantise_grad(1, m, rooms(first[:])[m])
         acc = product(0, 3)
         for h in range(2):
-            spent = weigh_on_scalar(1, h)
+            spent, spent_prob = weigh_on_scalar(1, h)
             copy_out(0, 3, acc, h * H, (h + 1) * H, spent[:, 0:H])
         for m in range(DV // P):
-            if m > 0:
-                quantise_grad(1, m * P, (m + 1) * P)
+            if m > 1:
+                quantise_grad(1, m, rooms(spent_prob)[m])
             acc = product(1, m)
             copy_out(1, m, acc, 0, N, tile("dense1_%d" % m, [P, N], F32)[:])
 
-        for b, m, lo, hi, dense in pieces:
-            nc.vector.tensor_copy(window[m][:].indirect(seq_offsets(b, lo, hi)), dense)
-            if b == B - 1:
-                for queue, cols in ((nc.sync, slice(0, T // 2)), (nc.scalar, slice(T // 2, T))):
-                    queue.dma_start(out=out[block(m), cols], in_=window[m][:, cols])
+        scatter(len(pieces))

@@ -42,6 +42,7 @@ def tile_attend_gat_sig_v_kernel(tc, qT, kT, rw, dom, offs, out):
         nc.sync.dma_start(offsets[:], offs)
 
         gate = [tile("gate%d" % b, [P, 1, PACK], F32) for b in range(B)]
+
         for b in range(B):
             nc.scalar.dma_start(out=gate[b][:, 0, :], in_=rw[b].rearrange("(p t) o -> p (t o)", t=PACK))
 
@@ -62,17 +63,17 @@ def tile_attend_gat_sig_v_kernel(tc, qT, kT, rw, dom, offs, out):
 
         key_rows = kT.rearrange("(p u e) t -> u p e t", u=2, e=2)
         key_pairs = [tile("key_pairs%d" % u, [P, T], U32) for u in range(2)]
-        pw_room = tile("pw_room", [P, 7 * N], BF16)
+        pw_room = tile("pw_room", [P, 5 * N], BF16)
         picked = [
             tile("picked0", [P, N, 2], U32)[:],
-            pw_room[:, 3 * N : 7 * N].bitcast(U32).rearrange("p (n u) -> p n u", u=2),
+            pw_room[:, N : 5 * N].bitcast(U32).rearrange("p (n u) -> p n u", u=2),
         ]
         shared = tile("shared", [P, 3, N], F32)
         planes1 = shared[:, 0:2, :].rearrange("p u n -> p (u n)").bitcast(U32).rearrange("p (u n) -> p u n", u=2)
 
-        def gather(b, u):
-            dst = picked[0][:, :, u] if b == 0 else planes1[:, u, :]
-            nc.vector.tensor_copy(dst, key_pairs[u][:].indirect(seq_offsets(b)))
+        def gather(b, u, lo=0, hi=N):
+            dst = picked[0][:, lo:hi, u] if b == 0 else planes1[:, u, lo:hi]
+            nc.vector.tensor_copy(dst, key_pairs[u][:].indirect(seq_offsets(b, lo, hi)))
 
         for u in range(2):
             pairs = key_pairs[u][:].bitcast(BF16).rearrange("p (t e) -> p t e", e=2)
@@ -88,9 +89,13 @@ def tile_attend_gat_sig_v_kernel(tc, qT, kT, rw, dom, offs, out):
                 for b in range(B):
                     gather(b, 0)
 
+        late = tile("late", [P, 2 * N + 256], F32)
+
         def load_rows(name, src, c0, w):
             if name == "q_raw0_1":
                 raw = shared[:, 1:3, :].rearrange("p a (j c) -> p (a j) c", j=2)
+            elif name == "q_raw1_1":
+                raw = late[:, 0 : 2 * N].rearrange("p (j c) -> p j c", j=PACK)
             else:
                 raw = tile(name, [P, PACK, w], F32)[:]
             nc.sync.dma_start(out=raw, in_=src.rearrange("(p j) c -> p j c", j=PACK)[:, :, c0 : c0 + w])
@@ -128,11 +133,11 @@ def tile_attend_gat_sig_v_kernel(tc, qT, kT, rw, dom, offs, out):
         def block(c):
             return slice(c * P, (c + 1) * P)
 
-        probs = tile("probs0", [P, 4 * N + 3 * H], F32)
-        prob_at = (0, N, 3 * N, 2 * N)
+        probs = tile("probs0", [P, 6 * N], F32)
+        prob_at = (0, N, 3 * N + H, 2 * N + P)
         q_grouped = [
             tile("q_grouped0", [P, PACK, P, PACK], BF16)[:],
-            probs[:, 3 * N + H : 5 * N + H].bitcast(BF16).rearrange("p (t m j) -> p t m j", t=PACK, j=PACK),
+            probs[:, 4 * N : 6 * N].bitcast(BF16).rearrange("p (t m j) -> p t m j", t=PACK, j=PACK),
         ]
         keys = [operand("key", N)] * B
         queries = [operand("query%d" % b, R) for b in range(B)]
@@ -140,12 +145,14 @@ def tile_attend_gat_sig_v_kernel(tc, qT, kT, rw, dom, offs, out):
         grads = [operand("grad%d" % b, DV) for b in range(B)]
 
         def quantise_keys(b):
-            quantise(keys[b], slice(0, N), picked[b].rearrange("p n u -> p (n u)").bitcast(BF16), E4M3)
+            for h in range(2):
+                quantise(keys[b], half(h), picked[b][:, half(h), :].rearrange("p n u -> p (n u)").bitcast(BF16), E4M3)
 
         def interleave_keys():
             src = shared[:, 0:2, :].rearrange("p u n -> p (u n)").bitcast(I32).rearrange("p (u n) -> p n u", u=2)
             dst = picked[1].rearrange("p n u -> p (n u)").bitcast(I32).rearrange("p (n u) -> p n u", u=2)
-            nc.vector.tensor_copy(out=dst, in_=src)
+            for h in range(2):
+                nc.vector.tensor_copy(out=dst[:, half(h)], in_=src[:, half(h)])
 
         def quantise_queries(b):
             grouped = q_grouped[b]
@@ -223,37 +230,38 @@ def tile_attend_gat_sig_v_kernel(tc, qT, kT, rw, dom, offs, out):
                         queue.dma_start(out=out[block(m), cols], in_=window[m][:, cols])
             pieces[:count] = []
 
-        gather(0, 1)
+        for h in range(2):
+            gather(0, 1, h * H, (h + 1) * H)
         quantise_keys(0)
         quantise_queries(0)
         gather(1, 1)
-        quantise_grad(0, 0, tile("grad_room", [P, N], BF16)[:])
         pw = pw_room[:, 0 : PACK * N].rearrange("p (n t) -> p n t", t=PACK)
         for c in range(N // P):
             weigh_on_vector(0, c, pw)
+        quantise_grad(0, 0, probs[:, 3 * N + H : 4 * N].bitcast(BF16))
         quantise(weights[0], slice(0, N), pw_room[:, 0 : PACK * N], E4M3)
-        quantise_grad(0, 1, probs[:, 3 * N : 3 * N + H].bitcast(BF16))
         acc = product(0, 0)
-        first = tile("dense0_0", [P, N], F32)
-        for h in range(2):
-            copy_out(0, 0, acc, h * H, (h + 1) * H, first[:, half(h)])
-        for m in (2, 3):
-            quantise_grad(0, m, rooms(probs[:, 2 * N : 3 * N])[m - 2])
+        first = tile("dense0_0", [P, H], F32)
+        copy_out(0, 0, acc, 0, H, first[:])
+        for m in (1, 2, 3):
+            quantise_grad(0, m, rooms(probs[:, 2 * N : 3 * N + H])[m - 1])
         interleave_keys()
         quantise_keys(1)
         quantise_queries(1)
+        copy_out(0, 0, acc, H, N, late[:, 0:H])
         for m in (1, 2):
-            copy_out(0, m, product(0, m), 0, N, q_raw[1, 1][:, 2 * m - 2 : 2 * m, :].rearrange("p j c -> p (j c)"))
-        scatter(2)
-        for m in (0, 1):
-            quantise_grad(1, m, rooms(first[:])[m])
+            copy_out(0, m, product(0, m), 0, N, late[:, m * N - H : (m + 1) * N - H])
+        scatter(1)
+        quantise_grad(1, 0, rooms(first[:])[0])
         acc = product(0, 3)
+        spent_prob = []
         for h in range(2):
-            spent, spent_prob = weigh_on_scalar(1, h)
+            spent, prob = weigh_on_scalar(1, h)
+            spent_prob.append(prob)
             copy_out(0, 3, acc, h * H, (h + 1) * H, spent[:, 0:H])
         for m in range(DV // P):
-            if m > 1:
-                quantise_grad(1, m, rooms(spent_prob)[m])
+            if m > 0:
+                quantise_grad(1, m, rooms(spent_prob[m // 2])[m])
             acc = product(1, m)
             copy_out(1, m, acc, 0, N, tile("dense1_%d" % m, [P, N], F32)[:])
 

@@ -196,20 +196,18 @@ def tile_attend_gat_sig_v_kernel(tc, qT, kT, rw, dom, offs, out):
             nc.scalar.activation(out=prob, in_=scores[:].rearrange("p t n -> p n t"), func=SIGMOID)
             nc.vector.tensor_tensor(out=pw[:, block(c), :], in0=prob, in1=gate[b][:].broadcast_to([P, P, PACK]), op=MULT)
 
-        def weigh_on_scalar(b, h):
-            prob = tile("prob%d_%d" % (b, h), [P, PACK, H], F32)
-            for c in range(2):
-                nc.scalar.activation(out=prob[:, :, block(c)], in_=score(b, 2 * h + c)[:], func=SIGMOID)
-            planes = tile("planes%d_%d" % (b, h), [P, PACK, H], BF16)
-            for t in range(PACK):
-                nc.scalar.activation(out=planes[:, t, :], in_=prob[:, t, :], func=COPY, scale=gate[b][:, 0, t : t + 1])
+        def weigh_on_gpsimd(b, h):
+            prob = tile("prob%d_%d" % (b, h), [P, H, PACK], F32)
             pw = tile("pw%d_%d" % (b, h), [P, H, PACK], BF16)
-            nc.scalar.copy(
-                out=pw[:].rearrange("p (c i) t -> p c t i", i=4),
-                in_=planes[:].rearrange("p t (c i) -> p c t i", i=4),
-            )
+            for c in range(2):
+                scores = score(b, 2 * h + c)
+                nc.scalar.activation(out=prob[:, block(c), :], in_=scores[:].rearrange("p t n -> p n t"), func=SIGMOID)
+                nc.gpsimd.tensor_tensor(
+                    out=pw[:, block(c), :], in0=prob[:, block(c), :], in1=gate[b][:].broadcast_to([P, P, PACK]), op=MULT
+                )
             quantise(weights[b], half(h), pw[:].rearrange("p n t -> p (n t)"), E4M3)
-            return planes[:].rearrange("p t c -> p (t c)").bitcast(F32), prob[:].rearrange("p t c -> p (t c)")
+            flat = prob[:].rearrange("p n t -> p (n t)")
+            return flat[:, 3 * H : 4 * H], flat[:, 0 : 3 * H]
 
         def product(b, m):
             acc = psum.tile([P, N], F32, name="acc")
@@ -256,12 +254,12 @@ def tile_attend_gat_sig_v_kernel(tc, qT, kT, rw, dom, offs, out):
         acc = product(0, 3)
         spent_prob = []
         for h in range(2):
-            spent, prob = weigh_on_scalar(1, h)
+            spent, prob = weigh_on_gpsimd(1, h)
             spent_prob.append(prob)
             copy_out(0, 3, acc, h * H, (h + 1) * H, spent[:, 0:H])
         for m in range(DV // P):
             if m > 0:
-                quantise_grad(1, m, rooms(spent_prob[m // 2])[m])
+                quantise_grad(1, m, rooms(spent_prob[m // 2])[m % 2 + 1])
             acc = product(1, m)
             copy_out(1, m, acc, 0, N, tile("dense1_%d" % m, [P, N], F32)[:])
 

@@ -16,6 +16,7 @@ E5M2 = mybir.dt.float8_e5m2_x4
 COPY = mybir.ActivationFunctionType.Copy
 SIGMOID = mybir.ActivationFunctionType.Sigmoid
 MULT = mybir.AluOpType.mult
+ADD = mybir.AluOpType.add
 
 P = 128
 PACK = 4
@@ -37,6 +38,9 @@ def tile_attend_gat_sig_v_kernel(tc, qT, kT, rw, dom, offs, out):
 
         def vector_cast(dst, src):
             nc.vector.tensor_copy(out=dst, in_=src)
+
+        def gpsimd_cast(dst, src):
+            nc.gpsimd.tensor_scalar(out=dst, in0=src, scalar1=1.0, scalar2=0.0, op0=MULT, op1=ADD)
 
         offsets = keep.tile([P, B * LIST_COLS], U16, name="offsets")
         nc.sync.dma_start(offsets[:], offs)
@@ -63,11 +67,12 @@ def tile_attend_gat_sig_v_kernel(tc, qT, kT, rw, dom, offs, out):
 
         key_rows = kT.rearrange("(p u e) t -> u p e t", u=2, e=2)
         key_pairs = [tile("key_pairs%d" % u, [P, T], U32) for u in range(2)]
-        pw_room = tile("pw_room", [P, 5 * N], BF16)
+        early = tile("early", [P, 2 * N + 256], F32)
         picked = [
             tile("picked0", [P, N, 2], U32)[:],
-            pw_room[:, N : 5 * N].bitcast(U32).rearrange("p (n u) -> p n u", u=2),
+            early[:, 256 : 2 * N + 256].bitcast(U32).rearrange("p (n u) -> p n u", u=2),
         ]
+        room = tile("room", [P, 7 * N], BF16)
         shared = tile("shared", [P, 3, N], F32)
         planes1 = shared[:, 0:2, :].rearrange("p u n -> p (u n)").bitcast(U32).rearrange("p (u n) -> p u n", u=2)
 
@@ -133,15 +138,19 @@ def tile_attend_gat_sig_v_kernel(tc, qT, kT, rw, dom, offs, out):
         def block(c):
             return slice(c * P, (c + 1) * P)
 
-        probs = tile("probs0", [P, 6 * N], F32)
-        prob_at = (0, N, 3 * N + H, 2 * N + P)
+        probs = [
+            [early[:, 0:N], early[:, N : 2 * N]] + [tile("prob0_%d" % c, [P, N], F32)[:] for c in (2, 3)],
+            [tile("prob1_%d" % c, [P, N], F32)[:] for c in range(PACK)],
+        ]
         q_grouped = [
             tile("q_grouped0", [P, PACK, P, PACK], BF16)[:],
-            probs[:, 4 * N : 6 * N].bitcast(BF16).rearrange("p (t m j) -> p t m j", t=PACK, j=PACK),
+            room[:, 0 : 4 * N].rearrange("p (t m j) -> p t m j", t=PACK, j=PACK),
         ]
-        keys = [operand("key", N)] * B
+        keys = [operand("key%d" % b, N) for b in range(B)]
         queries = [operand("query%d" % b, R) for b in range(B)]
-        weights = [operand("weight%d" % b, N) for b in range(B)]
+        weights = [operand("weight0", H + N), operand("weight1", N)]
+        nc.gpsimd.memset(weights[0][0][:, 0:H], 0)
+        nc.gpsimd.memset(weights[0][1][:, 0:H], 0)
         grads = [operand("grad%d" % b, DV) for b in range(B)]
 
         def quantise_keys(b):
@@ -149,10 +158,9 @@ def tile_attend_gat_sig_v_kernel(tc, qT, kT, rw, dom, offs, out):
                 quantise(keys[b], half(h), picked[b][:, half(h), :].rearrange("p n u -> p (n u)").bitcast(BF16), E4M3)
 
         def interleave_keys():
-            src = shared[:, 0:2, :].rearrange("p u n -> p (u n)").bitcast(I32).rearrange("p (u n) -> p n u", u=2)
-            dst = picked[1].rearrange("p n u -> p (n u)").bitcast(I32).rearrange("p (n u) -> p n u", u=2)
+            src = shared[:, 0:2, :].rearrange("p u n -> p (u n)").bitcast(U32).rearrange("p (u n) -> p n u", u=2)
             for h in range(2):
-                nc.vector.tensor_copy(out=dst[:, half(h)], in_=src[:, half(h)])
+                nc.scalar.copy(out=picked[1][:, half(h)], in_=src[:, half(h)])
 
         def quantise_queries(b):
             grouped = q_grouped[b]
@@ -165,19 +173,22 @@ def tile_attend_gat_sig_v_kernel(tc, qT, kT, rw, dom, offs, out):
                 elif b == 0:
                     scalar_cast(view[:, 0:64], src)
                 else:
-                    for i in range(2):
-                        scalar_cast(view[:, 64 * h + 32 * i : 64 * h + 32 * i + 32], src[:, 32 * i : 32 * i + 32])
+                    for i in range(4):
+                        scalar_cast(view[:, 64 * h + 16 * i : 64 * h + 16 * i + 16], src[:, 16 * i : 16 * i + 16])
             if b == 0:
                 for t in range(PACK):
                     quantise(queries[b], block(t), grouped[:, t].rearrange("p m j -> p (m j)"), E4M3)
             else:
                 quantise(queries[b], slice(0, R), grouped.rearrange("p t m j -> p (t m j)"), E4M3)
 
-        def quantise_grad(b, m, room):
-            scalar_cast(
+        def cast_grad(b, m, room, cast=scalar_cast):
+            cast(
                 room.rearrange("p (c i j) -> p c j i", i=4, j=PACK),
                 dom_raw[b, m // 2][:, :, block(m % 2)].rearrange("p j (c i) -> p c j i", i=4),
             )
+
+        def quantise_grad(b, m, room):
+            cast_grad(b, m, room)
             quantise(grads[b], block(m), room, E5M2)
 
         def rooms(spent):
@@ -185,39 +196,48 @@ def tile_attend_gat_sig_v_kernel(tc, qT, kT, rw, dom, offs, out):
             return [flat[:, i * N : (i + 1) * N] for i in range(flat.shape[1] // N)]
 
         def score(b, c):
-            scores = psum.tile([P, PACK, P], F32, name="scores")
+            if (b, c) == (0, 3):
+                scores = psum.tile([P, PACK, P], F32, name="first", bufs=1)
+            else:
+                scores = psum.tile([P, PACK, P], F32, name="scores", bufs=3)
             for t in range(PACK):
                 multiply(scores[:, t, :], queries[b], block(t), E4M3, keys[b], block(c))
             return scores
 
-        def weigh_on_vector(b, c, pw):
+        def sigmoid(b, c):
             scores = score(b, c)
-            prob = probs[:, prob_at[c] : prob_at[c] + N].rearrange("p (n t) -> p n t", t=PACK)
+            prob = probs[b][c].rearrange("p (n t) -> p n t", t=PACK)
             nc.scalar.activation(out=prob, in_=scores[:].rearrange("p t n -> p n t"), func=SIGMOID)
-            nc.vector.tensor_tensor(out=pw[:, block(c), :], in0=prob, in1=gate[b][:].broadcast_to([P, P, PACK]), op=MULT)
 
-        def weigh_on_gpsimd(b, h):
-            prob = tile("prob%d_%d" % (b, h), [P, H, PACK], F32)
-            pw = tile("pw%d_%d" % (b, h), [P, H, PACK], BF16)
-            for c in range(2):
-                scores = score(b, 2 * h + c)
-                nc.scalar.activation(out=prob[:, block(c), :], in_=scores[:].rearrange("p t n -> p n t"), func=SIGMOID)
-                nc.gpsimd.tensor_tensor(
-                    out=pw[:, block(c), :], in0=prob[:, block(c), :], in1=gate[b][:].broadcast_to([P, P, PACK]), op=MULT
-                )
-            quantise(weights[b], half(h), pw[:].rearrange("p n t -> p (n t)"), E4M3)
-            flat = prob[:].rearrange("p n t -> p (n t)")
-            return flat[:, 3 * H : 4 * H], flat[:, 0 : 3 * H]
+        def weigh(engine, b, c, pw):
+            prob = probs[b][c].rearrange("p (n t) -> p n t", t=PACK)
+            engine.tensor_tensor(
+                out=pw.rearrange("p (n t) -> p n t", t=PACK), in0=prob, in1=gate[b][:].broadcast_to([P, P, PACK]), op=MULT
+            )
 
-        def product(b, m):
-            acc = psum.tile([P, N], F32, name="acc")
-            multiply(acc[:], grads[b], block(m), E5M2, weights[b], slice(0, N))
+        def weigh_on_scalar(b, c, pw):
+            prob = probs[b][c].rearrange("p (t n) -> p t n", t=PACK)
+            nc.scalar.activation(out=prob, in_=score(b, c)[:], func=SIGMOID)
+            planes = tile("planes", [P, PACK, P], BF16)
+            for t in range(PACK):
+                nc.scalar.activation(out=planes[:, t, :], in_=prob[:, t, :], func=COPY, scale=gate[b][:, 0, t : t + 1])
+            nc.scalar.copy(
+                out=pw.rearrange("p (c i t) -> p c t i", i=4, t=PACK),
+                in_=planes[:].rearrange("p t (c i) -> p c t i", i=4),
+            )
+
+        def product(b, m, first=0):
+            if (b, m, first) == (0, 0, 0):
+                acc = psum.tile([P, N], F32, name="first", bufs=1)
+            else:
+                acc = psum.tile([P, N], F32, name="acc")
+            multiply(acc[:], grads[b], block(m), E5M2, weights[b], slice(first, first + N))
             return acc
 
         pieces = []
 
         def copy_out(b, m, acc, lo, hi, dense):
-            scalar_cast(dense, acc[:, lo:hi])
+            scalar_cast(dense, acc)
             pieces.append((b, m, lo, hi, dense))
 
         def scatter(count):
@@ -232,35 +252,44 @@ def tile_attend_gat_sig_v_kernel(tc, qT, kT, rw, dom, offs, out):
             gather(0, 1, h * H, (h + 1) * H)
         quantise_keys(0)
         quantise_queries(0)
+        for m in range(2):
+            quantise_grad(0, m, tile("grad_room%d" % m, [P, N], BF16)[:])
         gather(1, 1)
-        pw = pw_room[:, 0 : PACK * N].rearrange("p (n t) -> p n t", t=PACK)
-        for c in range(N // P):
-            weigh_on_vector(0, c, pw)
-        quantise_grad(0, 0, probs[:, 3 * N + H : 4 * N].bitcast(BF16))
-        quantise(weights[0], slice(0, N), pw_room[:, 0 : PACK * N], E4M3)
-        acc = product(0, 0)
-        first = tile("dense0_0", [P, H], F32)
-        copy_out(0, 0, acc, 0, H, first[:])
-        for m in (1, 2, 3):
-            quantise_grad(0, m, rooms(probs[:, 2 * N : 3 * N + H])[m - 1])
+        for c in range(2):
+            sigmoid(0, c)
+            weigh(nc.vector, 0, c, room[:, (3 + c) * N : (4 + c) * N])
+        quantise(weights[0], slice(H, N), room[:, 3 * N : 5 * N], E4M3)
+        quantise_grad(0, 2, rooms(early[:, 0:H])[0])
+        copy_out(0, 0, product(0, 0)[:, H:N], 0, H, tile("dense0_0a", [P, H], F32)[:])
         interleave_keys()
         quantise_keys(1)
+        for c in range(2, 4):
+            sigmoid(0, c)
+        copy_out(0, 1, product(0, 1)[:, H:N], 0, H, tile("dense0_1a", [P, H], F32)[:])
+        scatter(2)
+        gated = picked[1].rearrange("p n u -> p (n u)").bitcast(BF16)
+        for c in range(2, 4):
+            weigh(nc.gpsimd, 0, c, gated[:, c * N : (c + 1) * N])
+        quantise(weights[0], slice(N, N + H), gated[:, 2 * N : 4 * N], E4M3)
         quantise_queries(1)
-        copy_out(0, 0, acc, H, N, late[:, 0:H])
-        for m in (1, 2):
-            copy_out(0, m, product(0, m), 0, N, late[:, m * N - H : (m + 1) * N - H])
-        scatter(1)
-        quantise_grad(1, 0, rooms(first[:])[0])
-        acc = product(0, 3)
-        spent_prob = []
-        for h in range(2):
-            spent, prob = weigh_on_gpsimd(1, h)
-            spent_prob.append(prob)
-            copy_out(0, 3, acc, h * H, (h + 1) * H, spent[:, 0:H])
+        copy_out(0, 2, product(0, 2)[:, H:N], 0, H, probs[0][3][:, 0:H])
+        quantise_grad(0, 3, rooms(probs[0][3][:, H:N])[0])
+        for m in range(3):
+            copy_out(0, m, product(0, m, H)[:, H:N], H, N, late[:, m * H : (m + 1) * H])
+        scatter(4)
+        for m in range(2):
+            cast_grad(1, m, room[:, m * N : (m + 1) * N], gpsimd_cast)
+        pw = tile("pw1", [P, PACK * N], BF16)
+        for c in range(3):
+            sigmoid(1, c)
+            weigh(nc.gpsimd, 1, c, pw[:, c * N : (c + 1) * N])
+        weigh_on_scalar(1, 3, pw[:, 3 * N : 4 * N])
+        for m in range(2, 4):
+            cast_grad(1, m, room[:, m * N : (m + 1) * N])
+        quantise(grads[1], slice(0, DV), room[:, 0 : 4 * N], E5M2)
+        quantise(weights[1], slice(0, N), pw[:], E4M3)
+        copy_out(0, 3, product(0, 3, H)[:], 0, N, probs[1][2])
         for m in range(DV // P):
-            if m > 0:
-                quantise_grad(1, m, rooms(spent_prob[m // 2])[m % 2 + 1])
-            acc = product(1, m)
-            copy_out(1, m, acc, 0, N, tile("dense1_%d" % m, [P, N], F32)[:])
+            copy_out(1, m, product(1, m)[:], 0, N, tile("dense1_%d" % m, [P, N], F32)[:])
 
         scatter(len(pieces))

@@ -21,7 +21,7 @@ ADD = mybir.AluOpType.add
 P = 128
 PACK = 4
 LIST_COLS = N // 16
-KEY_CHUNKS = (((1024, 1024), (1024, 640)), ((1024, 896), (512, 320), (512, 192)))
+KEY_CHUNKS = (((1024, 1024), (1024, 640)), ((1024, 768), (768, 256), (256, 96)))
 
 
 def tile_attend_gat_sig_v_kernel(tc, qT, kT, rw, dom, offs, out):
@@ -43,7 +43,6 @@ def tile_attend_gat_sig_v_kernel(tc, qT, kT, rw, dom, offs, out):
             nc.gpsimd.tensor_scalar(out=dst, in0=src, scalar1=1.0, scalar2=0.0, op0=MULT, op1=ADD)
 
         offsets = keep.tile([P, B * LIST_COLS], U16, name="offsets")
-        nc.sync.dma_start(offsets[:], offs)
 
         gate = [tile("gate%d" % b, [P, 1, PACK], F32) for b in range(B)]
 
@@ -67,10 +66,10 @@ def tile_attend_gat_sig_v_kernel(tc, qT, kT, rw, dom, offs, out):
 
         key_rows = kT.rearrange("(p u e) t -> u p e t", u=2, e=2)
         key_pairs = [tile("key_pairs%d" % u, [P, T], U32) for u in range(2)]
-        early = tile("early", [P, 2 * N + 256], F32)
+        early = tile("early", [P, 3 * N], F32)
         picked = [
             tile("picked0", [P, N, 2], U32)[:],
-            early[:, 256 : 2 * N + 256].bitcast(U32).rearrange("p (n u) -> p n u", u=2),
+            early[:, N : 3 * N].bitcast(U32).rearrange("p (n u) -> p n u", u=2),
         ]
         room = tile("room", [P, 7 * N], BF16)
         shared = tile("shared", [P, 3, N], F32)
@@ -86,6 +85,8 @@ def tile_attend_gat_sig_v_kernel(tc, qT, kT, rw, dom, offs, out):
             for i, (w, h) in enumerate(KEY_CHUNKS[u]):
                 raw = tile("key_raw%d_%d" % (u, i), [P, 2, w], F32)
                 nc.sync.dma_start(out=raw[:], in_=key_rows[u][:, :, t0 : t0 + w])
+                if (u, i) == (0, 0):
+                    nc.sync.dma_start(offsets[:], offs)
                 scalar_cast(pairs[:, t0 : t0 + h, :], raw[:, :, 0:h].rearrange("p e t -> p t e"))
                 if h < w:
                     vector_cast(pairs[:, t0 + h : t0 + w, :], raw[:, :, h:w].rearrange("p e t -> p t e"))
@@ -139,7 +140,7 @@ def tile_attend_gat_sig_v_kernel(tc, qT, kT, rw, dom, offs, out):
             return slice(c * P, (c + 1) * P)
 
         probs = [
-            [early[:, 0:N], early[:, N : 2 * N]] + [tile("prob0_%d" % c, [P, N], F32)[:] for c in (2, 3)],
+            [early[:, H : H + N], early[:, H + N : H + 2 * N]] + [tile("prob0_%d" % c, [P, N], F32)[:] for c in (2, 3)],
             [tile("prob1_%d" % c, [P, N], F32)[:] for c in range(PACK)],
         ]
         q_grouped = [
@@ -252,14 +253,16 @@ def tile_attend_gat_sig_v_kernel(tc, qT, kT, rw, dom, offs, out):
             gather(0, 1, h * H, (h + 1) * H)
         quantise_keys(0)
         quantise_queries(0)
-        for m in range(2):
-            quantise_grad(0, m, tile("grad_room%d" % m, [P, N], BF16)[:])
+        quantise_grad(0, 0, tile("grad_room0", [P, N], BF16)[:])
+        cast_grad(0, 1, rooms(early[:, 0:N])[0])
         gather(1, 1)
         for c in range(2):
             sigmoid(0, c)
             weigh(nc.vector, 0, c, room[:, (3 + c) * N : (4 + c) * N])
-        quantise(weights[0], slice(H, N), room[:, 3 * N : 5 * N], E4M3)
-        quantise_grad(0, 2, rooms(early[:, 0:H])[0])
+        for c in range(2):
+            quantise(weights[0], block(2 + c), room[:, (3 + c) * N : (4 + c) * N], E4M3)
+        cast_grad(0, 2, rooms(early[:, 0:N])[1])
+        quantise(grads[0], slice(P, 3 * P), early[:, 0:N].bitcast(BF16), E5M2)
         copy_out(0, 0, product(0, 0)[:, H:N], 0, H, tile("dense0_0a", [P, H], F32)[:])
         interleave_keys()
         quantise_keys(1)
@@ -277,14 +280,13 @@ def tile_attend_gat_sig_v_kernel(tc, qT, kT, rw, dom, offs, out):
         for m in range(3):
             copy_out(0, m, product(0, m, H)[:, H:N], H, N, late[:, m * H : (m + 1) * H])
         scatter(4)
-        for m in range(2):
-            cast_grad(1, m, room[:, m * N : (m + 1) * N], gpsimd_cast)
+        cast_grad(1, 0, room[:, 0:N], gpsimd_cast)
         pw = tile("pw1", [P, PACK * N], BF16)
         for c in range(3):
             sigmoid(1, c)
             weigh(nc.gpsimd, 1, c, pw[:, c * N : (c + 1) * N])
         weigh_on_scalar(1, 3, pw[:, 3 * N : 4 * N])
-        for m in range(2, 4):
+        for m in range(1, 4):
             cast_grad(1, m, room[:, m * N : (m + 1) * N])
         quantise(grads[1], slice(0, DV), room[:, 0 : 4 * N], E5M2)
         quantise(weights[1], slice(0, N), pw[:], E4M3)

@@ -21,7 +21,7 @@ ADD = mybir.AluOpType.add
 P = 128
 PACK = 4
 LIST_COLS = N // 16
-KEY_CHUNKS = (((1024, 1024), (1024, 640)), ((1024, 768), (768, 256), (256, 96)))
+KEY_CHUNKS = (((1024, 1024), (1024, 320)), ((1024, 768), (768, 256), (256, 96)))
 
 
 def tile_attend_gat_sig_v_kernel(tc, qT, kT, rw, dom, offs, out):
@@ -56,10 +56,9 @@ def tile_attend_gat_sig_v_kernel(tc, qT, kT, rw, dom, offs, out):
 
         window = [tile("window%d" % m, [P, T], F32) for m in range(DV // P)]
 
-        for m in range(2):
-            nc.vector.memset(window[m][:, 0:1023], 0.0)
-            nc.vector.memset(window[m][:, 1023:T], 0.0)
-            nc.gpsimd.memset(window[2 + m][:], 0.0)
+        for m in range(3):
+            nc.vector.memset(window[m][:].bitcast(I32), 0)
+        nc.gpsimd.memset(window[3][:], 0.0)
 
         def seq_offsets(b, lo=0, hi=N):
             return offsets[:, b * LIST_COLS + lo // 16 : b * LIST_COLS + hi // 16]

@@ -20,8 +20,14 @@ ADD = mybir.AluOpType.add
 
 P = 128
 PACK = 4
+H = N // 2
+BLOCKS = DV // P
 LIST_COLS = N // 16
-KEY_CHUNKS = (((1024, 1024), (1024, 320)), ((1024, 768), (768, 256), (256, 96)))
+
+KEY_LOADS = (((1024, 1024), (1024, 320)), ((1024, 768), (768, 256), (256, 96)))
+GROUPS = H // PACK
+SCALAR_GROUPS = 28
+PIECE_GROUPS = 16
 
 
 def tile_attend_gat_sig_v_kernel(tc, qT, kT, rw, dom, offs, out):
@@ -42,10 +48,21 @@ def tile_attend_gat_sig_v_kernel(tc, qT, kT, rw, dom, offs, out):
         def gpsimd_cast(dst, src):
             nc.gpsimd.tensor_scalar(out=dst, in0=src, scalar1=1.0, scalar2=0.0, op0=MULT, op1=ADD)
 
+        def half(h):
+            return slice(h * H, (h + 1) * H)
+
+        def block(c):
+            return slice(c * P, (c + 1) * P)
+
+        def chunk(wide, c):
+            return wide[:, c * N : (c + 1) * N]
+
         offsets = keep.tile([P, B * LIST_COLS], U16, name="offsets")
 
-        gate = [tile("gate%d" % b, [P, 1, PACK], F32) for b in range(B)]
+        def seq_offsets(b, lo, hi):
+            return offsets[:, b * LIST_COLS + lo // 16 : b * LIST_COLS + hi // 16]
 
+        gate = [tile("gate%d" % b, [P, 1, PACK], F32) for b in range(B)]
         for b in range(B):
             nc.scalar.dma_start(out=gate[b][:, 0, :], in_=rw[b].rearrange("(p t) o -> p (t o)", t=PACK))
 
@@ -54,66 +71,61 @@ def tile_attend_gat_sig_v_kernel(tc, qT, kT, rw, dom, offs, out):
         nc.gpsimd.memset(warm_in[:], 0.0)
         nc.scalar.activation(out=warm_out[:], in_=warm_in[:], func=SIGMOID)
 
-        window = [tile("window%d" % m, [P, T], F32) for m in range(DV // P)]
-
-        for m in range(3):
+        window = [tile("window%d" % m, [P, T], F32) for m in range(BLOCKS)]
+        for m in range(BLOCKS - 1):
             nc.vector.memset(window[m][:].bitcast(I32), 0)
-        nc.gpsimd.memset(window[3][:], 0.0)
-
-        def seq_offsets(b, lo=0, hi=N):
-            return offsets[:, b * LIST_COLS + lo // 16 : b * LIST_COLS + hi // 16]
+        nc.gpsimd.memset(window[BLOCKS - 1][:], 0.0)
 
         key_rows = kT.rearrange("(p u e) t -> u p e t", u=2, e=2)
         key_pairs = [tile("key_pairs%d" % u, [P, T], U32) for u in range(2)]
+
         early = tile("early", [P, 3 * N], F32)
         picked = [
             tile("picked0", [P, N, 2], U32)[:],
             early[:, N : 3 * N].bitcast(U32).rearrange("p (n u) -> p n u", u=2),
         ]
-        room = tile("room", [P, 7 * N], BF16)
+        room = tile("room", [P, 5 * N], BF16)
         shared = tile("shared", [P, 3, N], F32)
-        planes1 = shared[:, 0:2, :].rearrange("p u n -> p (u n)").bitcast(U32).rearrange("p (u n) -> p u n", u=2)
+        pair_rows = shared[:, 0:2, :].rearrange("p u n -> p (u n)").bitcast(U32).rearrange("p (u n) -> p u n", u=2)
 
-        def gather(b, u, lo=0, hi=N):
-            dst = picked[0][:, lo:hi, u] if b == 0 else planes1[:, u, lo:hi]
+        def gather(b, u, lo, hi):
+            dst = picked[0][:, lo:hi, u] if b == 0 else pair_rows[:, u, lo:hi]
             nc.vector.tensor_copy(dst, key_pairs[u][:].indirect(seq_offsets(b, lo, hi)))
 
         for u in range(2):
             pairs = key_pairs[u][:].bitcast(BF16).rearrange("p (t e) -> p t e", e=2)
             t0 = 0
-            for i, (w, h) in enumerate(KEY_CHUNKS[u]):
-                raw = tile("key_raw%d_%d" % (u, i), [P, 2, w], F32)
-                nc.sync.dma_start(out=raw[:], in_=key_rows[u][:, :, t0 : t0 + w])
+            for i, (width, on_scalar) in enumerate(KEY_LOADS[u]):
+                raw = tile("key_raw%d_%d" % (u, i), [P, 2, width], F32)
+                nc.sync.dma_start(out=raw[:], in_=key_rows[u][:, :, t0 : t0 + width])
                 if (u, i) == (0, 0):
                     nc.sync.dma_start(offsets[:], offs)
-                scalar_cast(pairs[:, t0 : t0 + h, :], raw[:, :, 0:h].rearrange("p e t -> p t e"))
-                if h < w:
-                    vector_cast(pairs[:, t0 + h : t0 + w, :], raw[:, :, h:w].rearrange("p e t -> p t e"))
-                t0 += w
+                by_token = raw[:].rearrange("p e t -> p t e")
+                scalar_cast(pairs[:, t0 : t0 + on_scalar, :], by_token[:, 0:on_scalar])
+                if on_scalar < width:
+                    vector_cast(pairs[:, t0 + on_scalar : t0 + width, :], by_token[:, on_scalar:width])
+                t0 += width
             if u == 0:
                 for b in range(B):
-                    gather(b, 0)
+                    gather(b, 0, 0, N)
 
-        late = tile("late", [P, 2 * N + 256], F32)
+        late = tile("late", [P, PACK * H], F32)
 
-        def load_rows(name, src, c0, w):
-            if name == "q_raw0_1":
-                raw = shared[:, 1:3, :].rearrange("p a (j c) -> p (a j) c", j=2)
-            elif name == "q_raw1_1":
-                raw = late[:, 0 : 2 * N].rearrange("p (j c) -> p j c", j=PACK)
-            else:
-                raw = tile(name, [P, PACK, w], F32)[:]
-            nc.sync.dma_start(out=raw, in_=src.rearrange("(p j) c -> p j c", j=PACK)[:, :, c0 : c0 + w])
+        def load_half(raw, src, h):
+            nc.sync.dma_start(out=raw, in_=src.rearrange("(p j) c -> p j c", j=PACK)[:, :, half(h)])
             return raw
 
-        H = 256
+        last_half = [
+            shared[:, 1:3, :].rearrange("p a (j c) -> p (a j) c", j=2),
+            late[:].rearrange("p (j c) -> p j c", j=PACK),
+        ]
         q_raw = {}
         dom_raw = {}
         for b in range(B):
+            q_raw[b, 0] = load_half(tile("q_raw%d_0" % b, [P, PACK, H], F32)[:], qT[b], 0)
+            q_raw[b, 1] = load_half(last_half[b], qT[b], 1)
             for h in range(2):
-                q_raw[b, h] = load_rows("q_raw%d_%d" % (b, h), qT[b], h * H, H)
-            for h in range(2):
-                dom_raw[b, h] = load_rows("dom_raw%d_%d" % (b, h), dom[b], h * H, H)
+                dom_raw[b, h] = load_half(tile("dom_raw%d_%d" % (b, h), [P, PACK, H], F32)[:], dom[b], h)
 
         def operand(name, words):
             return tile(name + "_codes", [P, words], U32), tile(name + "_scales", [P, words], U8)
@@ -131,12 +143,6 @@ def tile_attend_gat_sig_v_kernel(tc, qT, kT, rw, dom, offs, out):
                 start=True,
                 stop=True,
             )
-
-        def half(h):
-            return slice(h * H, (h + 1) * H)
-
-        def block(c):
-            return slice(c * P, (c + 1) * P)
 
         probs = [
             [early[:, H : H + N], early[:, H + N : H + 2 * N]] + [tile("prob0_%d" % c, [P, N], F32)[:] for c in (2, 3)],
@@ -158,45 +164,26 @@ def tile_attend_gat_sig_v_kernel(tc, qT, kT, rw, dom, offs, out):
                 quantise(keys[b], half(h), picked[b][:, half(h), :].rearrange("p n u -> p (n u)").bitcast(BF16), E4M3)
 
         def interleave_keys():
-            src = shared[:, 0:2, :].rearrange("p u n -> p (u n)").bitcast(U32).rearrange("p (u n) -> p n u", u=2)
+            by_slot = pair_rows.rearrange("p u n -> p n u")
             for h in range(2):
-                nc.scalar.copy(out=picked[1][:, half(h)], in_=src[:, half(h)])
+                nc.scalar.copy(out=picked[1][:, half(h)], in_=by_slot[:, half(h)])
 
-        def quantise_queries(b):
-            grouped = q_grouped[b]
-            view = grouped.rearrange("p t m j -> p m j t")
-            for h in range(2):
-                src = q_raw[b, h].rearrange("p j (m t) -> p m j t", t=PACK)
-                if (b, h) == (0, 1):
-                    scalar_cast(view[:, 64:92], src[:, 0:28])
-                    vector_cast(view[:, 92:128], src[:, 28:64])
-                elif b == 0:
-                    scalar_cast(view[:, 0:64], src)
-                else:
-                    for i in range(4):
-                        scalar_cast(view[:, 64 * h + 16 * i : 64 * h + 16 * i + 16], src[:, 16 * i : 16 * i + 16])
-            if b == 0:
-                for t in range(PACK):
-                    quantise(queries[b], block(t), grouped[:, t].rearrange("p m j -> p (m j)"), E4M3)
-            else:
-                quantise(queries[b], slice(0, R), grouped.rearrange("p t m j -> p (t m j)"), E4M3)
+        def cast_queries(cast, b, h, lo, hi):
+            dst = q_grouped[b].rearrange("p t m j -> p m j t")[:, GROUPS * h + lo : GROUPS * h + hi]
+            cast(dst, q_raw[b, h].rearrange("p j (m t) -> p m j t", t=PACK)[:, lo:hi])
 
-        def cast_grad(b, m, room, cast=scalar_cast):
+        def cast_grad(cast, b, m, dst):
             cast(
-                room.rearrange("p (c i j) -> p c j i", i=4, j=PACK),
+                dst.rearrange("p (c i j) -> p c j i", i=4, j=PACK),
                 dom_raw[b, m // 2][:, :, block(m % 2)].rearrange("p j (c i) -> p c j i", i=4),
             )
 
-        def quantise_grad(b, m, room):
-            cast_grad(b, m, room)
-            quantise(grads[b], block(m), room, E5M2)
-
-        def rooms(spent):
-            flat = spent.bitcast(BF16)
-            return [flat[:, i * N : (i + 1) * N] for i in range(flat.shape[1] // N)]
+        def quantise_grad(b, m, dst):
+            cast_grad(scalar_cast, b, m, dst)
+            quantise(grads[b], block(m), dst, E5M2)
 
         def score(b, c):
-            if (b, c) == (0, 3):
+            if (b, c) == (0, PACK - 1):
                 scores = psum.tile([P, PACK, P], F32, name="first", bufs=1)
             else:
                 scores = psum.tile([P, PACK, P], F32, name="scores", bufs=3)
@@ -215,18 +202,18 @@ def tile_attend_gat_sig_v_kernel(tc, qT, kT, rw, dom, offs, out):
                 out=pw.rearrange("p (n t) -> p n t", t=PACK), in0=prob, in1=gate[b][:].broadcast_to([P, P, PACK]), op=MULT
             )
 
-        def weigh_on_scalar(b, c, pw):
+        def sigmoid_and_weigh_on_scalar(b, c, pw):
             prob = probs[b][c].rearrange("p (t n) -> p t n", t=PACK)
             nc.scalar.activation(out=prob, in_=score(b, c)[:], func=SIGMOID)
-            planes = tile("planes", [P, PACK, P], BF16)
+            by_tile = tile("by_tile", [P, PACK, P], BF16)
             for t in range(PACK):
-                nc.scalar.activation(out=planes[:, t, :], in_=prob[:, t, :], func=COPY, scale=gate[b][:, 0, t : t + 1])
+                nc.scalar.activation(out=by_tile[:, t, :], in_=prob[:, t, :], func=COPY, scale=gate[b][:, 0, t : t + 1])
             nc.scalar.copy(
                 out=pw.rearrange("p (c i t) -> p c t i", i=4, t=PACK),
-                in_=planes[:].rearrange("p t (c i) -> p c t i", i=4),
+                in_=by_tile[:].rearrange("p t (c i) -> p c t i", i=4),
             )
 
-        def product(b, m, first=0):
+        def product(b, m, first):
             if (b, m, first) == (0, 0, 0):
                 acc = psum.tile([P, N], F32, name="first", bufs=1)
             else:
@@ -234,63 +221,74 @@ def tile_attend_gat_sig_v_kernel(tc, qT, kT, rw, dom, offs, out):
             multiply(acc[:], grads[b], block(m), E5M2, weights[b], slice(first, first + N))
             return acc
 
-        pieces = []
+        waiting = []
 
         def copy_out(b, m, acc, lo, hi, dense):
             scalar_cast(dense, acc)
-            pieces.append((b, m, lo, hi, dense))
+            waiting.append((b, m, lo, hi, dense))
 
-        def scatter(count):
-            for b, m, lo, hi, dense in pieces[:count]:
+        def scatter_waiting():
+            for b, m, lo, hi, dense in waiting:
                 nc.vector.tensor_copy(window[m][:].indirect(seq_offsets(b, lo, hi)), dense)
                 if b == B - 1:
                     for queue, cols in ((nc.sync, slice(0, T // 2)), (nc.scalar, slice(T // 2, T))):
                         queue.dma_start(out=out[block(m), cols], in_=window[m][:, cols])
-            pieces[:count] = []
+            waiting.clear()
 
         for h in range(2):
             gather(0, 1, h * H, (h + 1) * H)
         quantise_keys(0)
-        quantise_queries(0)
+        cast_queries(scalar_cast, 0, 0, 0, GROUPS)
+        cast_queries(scalar_cast, 0, 1, 0, SCALAR_GROUPS)
+        cast_queries(vector_cast, 0, 1, SCALAR_GROUPS, GROUPS)
+        for t in range(PACK):
+            quantise(queries[0], block(t), q_grouped[0][:, t].rearrange("p m j -> p (m j)"), E4M3)
         quantise_grad(0, 0, tile("grad_room0", [P, N], BF16)[:])
-        cast_grad(0, 1, rooms(early[:, 0:N])[0])
-        gather(1, 1)
+        middle_blocks = early[:, 0:N].bitcast(BF16)
+        cast_grad(scalar_cast, 0, 1, chunk(middle_blocks, 0))
+        gather(1, 1, 0, N)
+
         for c in range(2):
             sigmoid(0, c)
-            weigh(nc.vector, 0, c, room[:, (3 + c) * N : (4 + c) * N])
+            weigh(nc.vector, 0, c, chunk(room, 3 + c))
         for c in range(2):
-            quantise(weights[0], block(2 + c), room[:, (3 + c) * N : (4 + c) * N], E4M3)
-        cast_grad(0, 2, rooms(early[:, 0:N])[1])
-        quantise(grads[0], slice(P, 3 * P), early[:, 0:N].bitcast(BF16), E5M2)
-        copy_out(0, 0, product(0, 0)[:, H:N], 0, H, tile("dense0_0a", [P, H], F32)[:])
+            quantise(weights[0], block(2 + c), chunk(room, 3 + c), E4M3)
+        cast_grad(scalar_cast, 0, 2, chunk(middle_blocks, 1))
+        quantise(grads[0], slice(P, 3 * P), middle_blocks, E5M2)
+        copy_out(0, 0, product(0, 0, 0)[:, H:N], 0, H, tile("dense0_0a", [P, H], F32)[:])
         interleave_keys()
         quantise_keys(1)
         for c in range(2, 4):
             sigmoid(0, c)
-        copy_out(0, 1, product(0, 1)[:, H:N], 0, H, tile("dense0_1a", [P, H], F32)[:])
-        scatter(2)
-        gated = picked[1].rearrange("p n u -> p (n u)").bitcast(BF16)
+        copy_out(0, 1, product(0, 1, 0)[:, H:N], 0, H, tile("dense0_1a", [P, H], F32)[:])
+        scatter_waiting()
+
+        spent_keys = picked[1].rearrange("p n u -> p (n u)").bitcast(BF16)
         for c in range(2, 4):
-            weigh(nc.gpsimd, 0, c, gated[:, c * N : (c + 1) * N])
-        quantise(weights[0], slice(N, N + H), gated[:, 2 * N : 4 * N], E4M3)
-        quantise_queries(1)
-        copy_out(0, 2, product(0, 2)[:, H:N], 0, H, probs[0][3][:, 0:H])
-        quantise_grad(0, 3, rooms(probs[0][3][:, H:N])[0])
-        for m in range(3):
+            weigh(nc.gpsimd, 0, c, chunk(spent_keys, c))
+        quantise(weights[0], slice(N, N + H), spent_keys[:, 2 * N : 4 * N], E4M3)
+        for h in range(2):
+            for lo in range(0, GROUPS, PIECE_GROUPS):
+                cast_queries(scalar_cast, 1, h, lo, lo + PIECE_GROUPS)
+        quantise(queries[1], slice(0, R), q_grouped[1].rearrange("p t m j -> p (t m j)"), E4M3)
+        copy_out(0, 2, product(0, 2, 0)[:, H:N], 0, H, probs[0][3][:, 0:H])
+        quantise_grad(0, 3, probs[0][3][:, H:N].bitcast(BF16))
+        for m in range(BLOCKS - 1):
             copy_out(0, m, product(0, m, H)[:, H:N], H, N, late[:, m * H : (m + 1) * H])
-        scatter(4)
-        cast_grad(1, 0, room[:, 0:N], gpsimd_cast)
+        scatter_waiting()
+
+        cast_grad(gpsimd_cast, 1, 0, chunk(room, 0))
         pw = tile("pw1", [P, PACK * N], BF16)
-        for c in range(3):
+        for c in range(PACK - 1):
             sigmoid(1, c)
-            weigh(nc.gpsimd, 1, c, pw[:, c * N : (c + 1) * N])
-        weigh_on_scalar(1, 3, pw[:, 3 * N : 4 * N])
-        for m in range(1, 4):
-            cast_grad(1, m, room[:, m * N : (m + 1) * N])
+            weigh(nc.gpsimd, 1, c, chunk(pw, c))
+        sigmoid_and_weigh_on_scalar(1, PACK - 1, chunk(pw, PACK - 1))
+        for m in range(1, BLOCKS):
+            cast_grad(scalar_cast, 1, m, chunk(room, m))
         quantise(grads[1], slice(0, DV), room[:, 0 : 4 * N], E5M2)
         quantise(weights[1], slice(0, N), pw[:], E4M3)
-        copy_out(0, 3, product(0, 3, H)[:], 0, N, probs[1][2])
-        for m in range(DV // P):
-            copy_out(1, m, product(1, m)[:], 0, N, tile("dense1_%d" % m, [P, N], F32)[:])
 
-        scatter(len(pieces))
+        copy_out(0, BLOCKS - 1, product(0, BLOCKS - 1, H)[:], 0, N, probs[1][2])
+        for m in range(BLOCKS):
+            copy_out(1, m, product(1, m, 0)[:], 0, N, tile("dense1_%d" % m, [P, N], F32)[:])
+        scatter_waiting()

@@ -24,7 +24,7 @@ H = N // 2
 BLOCKS = DV // P
 LIST_COLS = N // 16
 
-KEY_LOADS = (((1024, 1024), (1024, 320)), ((1024, 768), (768, 256), (256, 96)))
+KEY_LOADS = (((1536, 704), (512, 128)), ((1024, 768), (768, 256), (256, 96)))
 GROUPS = H // PACK
 SCALAR_GROUPS = 28
 PIECE_GROUPS = 16
@@ -34,6 +34,7 @@ def tile_attend_gat_sig_v_kernel(tc, qT, kT, rw, dom, offs, out):
     nc = tc.nc
     with ExitStack() as ctx:
         keep = ctx.enter_context(tc.tile_pool(name="keep", bufs=1))
+        placed = ctx.enter_context(tc.tile_pool(name="placed", bufs=1))
         psum = ctx.enter_context(tc.psum_pool(name="psum", bufs=4))
 
         def tile(name, shape, dtype):
@@ -71,10 +72,9 @@ def tile_attend_gat_sig_v_kernel(tc, qT, kT, rw, dom, offs, out):
         nc.gpsimd.memset(warm_in[:], 0.0)
         nc.scalar.activation(out=warm_out[:], in_=warm_in[:], func=SIGMOID)
 
-        window = [tile("window%d" % m, [P, T], F32) for m in range(BLOCKS)]
+        window = [tile("window%d" % m, [P, T], F32) for m in range(BLOCKS - 1)]
         for m in range(BLOCKS - 1):
             nc.vector.memset(window[m][:].bitcast(I32), 0)
-        nc.gpsimd.memset(window[BLOCKS - 1][:], 0.0)
 
         key_rows = kT.rearrange("(p u e) t -> u p e t", u=2, e=2)
         key_pairs = [tile("key_pairs%d" % u, [P, T], U32) for u in range(2)]
@@ -96,7 +96,10 @@ def tile_attend_gat_sig_v_kernel(tc, qT, kT, rw, dom, offs, out):
             pairs = key_pairs[u][:].bitcast(BF16).rearrange("p (t e) -> p t e", e=2)
             t0 = 0
             for i, (width, on_scalar) in enumerate(KEY_LOADS[u]):
-                raw = tile("key_raw%d_%d" % (u, i), [P, 2, width], F32)
+                if (u, i) == (0, 1):
+                    raw = placed.tile([P, 2, width], F32, name="key_raw0_1", offset=0)
+                else:
+                    raw = tile("key_raw%d_%d" % (u, i), [P, 2, width], F32)
                 nc.sync.dma_start(out=raw[:], in_=key_rows[u][:, :, t0 : t0 + width])
                 if (u, i) == (0, 0):
                     nc.sync.dma_start(offsets[:], offs)
@@ -106,6 +109,8 @@ def tile_attend_gat_sig_v_kernel(tc, qT, kT, rw, dom, offs, out):
                     vector_cast(pairs[:, t0 + on_scalar : t0 + width, :], by_token[:, on_scalar:width])
                 t0 += width
             if u == 0:
+                window.append(placed.tile([P, T], F32, name="last_window", offset=0))
+                nc.gpsimd.memset(window[BLOCKS - 1][:], 0.0)
                 for b in range(B):
                     gather(b, 0, 0, N)
 

@@ -135,6 +135,12 @@ def tile_attend_gat_sig_v_kernel(tc, qT, kT, rw, dom, offs, out):
         def operand(name, words):
             return tile(name + "_codes", [P, words], U32), tile(name + "_scales", [P, words], U8)
 
+        def query_tile(b, t):
+            codes, scales = queries[b]
+            if (b, t) == (0, PACK - 1):
+                return codes[:, block(t)], planes[:, 3 * P // 2 : 5 * P // 2]
+            return codes[:, block(t)], scales[:, block(t)]
+
         def quantise(dst, cols, src, fmt):
             nc.vector.quantize_mx(out=dst[0][:, cols].bitcast(fmt), scales=dst[1][:, cols], in_=src)
 
@@ -157,7 +163,8 @@ def tile_attend_gat_sig_v_kernel(tc, qT, kT, rw, dom, offs, out):
             tile("q_grouped0", [P, PACK, P, PACK], BF16)[:],
             room[:, 0 : 4 * N].rearrange("p (t m j) -> p t m j", t=PACK, j=PACK),
         ]
-        keys = [operand("key%d" % b, N) for b in range(B)]
+        planes = tile("planes", [P, N], U8)
+        keys = [(tile("key0_codes", [P, N], U32), planes[4:P, :]), operand("key1", N)]
         queries = [operand("query%d" % b, R) for b in range(B)]
         weights = [operand("weight0", H + N), operand("weight1", N)]
         nc.gpsimd.memset(weights[0][0][:, 0:H], 0)
@@ -193,7 +200,7 @@ def tile_attend_gat_sig_v_kernel(tc, qT, kT, rw, dom, offs, out):
             else:
                 scores = psum.tile([P, PACK, P], F32, name="scores", bufs=3)
             for t in range(PACK):
-                multiply(scores[:, t, :], queries[b], block(t), E4M3, keys[b], block(c))
+                multiply(scores[:, t, :], query_tile(b, t), block(0), E4M3, keys[b], block(c))
             return scores
 
         def sigmoid(b, c):
@@ -247,7 +254,7 @@ def tile_attend_gat_sig_v_kernel(tc, qT, kT, rw, dom, offs, out):
         cast_queries(scalar_cast, 0, 1, 0, SCALAR_GROUPS)
         cast_queries(vector_cast, 0, 1, SCALAR_GROUPS, GROUPS)
         for t in range(PACK):
-            quantise(queries[0], block(t), q_grouped[0][:, t].rearrange("p m j -> p (m j)"), E4M3)
+            quantise(query_tile(0, t), block(0), q_grouped[0][:, t].rearrange("p m j -> p (m j)"), E4M3)
         quantise_grad(0, 0, tile("grad_room0", [P, N], BF16)[:])
         middle_blocks = early[:, 0:N].bitcast(BF16)
         cast_grad(scalar_cast, 0, 1, chunk(middle_blocks, 0))

@@ -16,18 +16,16 @@ E5M2 = mybir.dt.float8_e5m2_x4
 COPY = mybir.ActivationFunctionType.Copy
 SIGMOID = mybir.ActivationFunctionType.Sigmoid
 MULT = mybir.AluOpType.mult
-ADD = mybir.AluOpType.add
 
 P = 128
 PACK = 4
 H = N // 2
 BLOCKS = DV // P
-LIST_COLS = N // 16
+SLOTS = B * N
 
 KEY_LOADS = (((1536, 704), (512, 128)), ((1024, 768), (768, 256), (256, 96)))
 GROUPS = H // PACK
 SCALAR_GROUPS = 28
-PIECE_GROUPS = 16
 
 
 def tile_attend_gat_sig_v_kernel(tc, qT, kT, rw, dom, offs, out):
@@ -35,19 +33,19 @@ def tile_attend_gat_sig_v_kernel(tc, qT, kT, rw, dom, offs, out):
     with ExitStack() as ctx:
         keep = ctx.enter_context(tc.tile_pool(name="keep", bufs=1))
         placed = ctx.enter_context(tc.tile_pool(name="placed", bufs=1))
-        psum = ctx.enter_context(tc.psum_pool(name="psum", bufs=4))
+        psum = ctx.enter_context(tc.psum_pool(name="psum", bufs=1))
 
         def tile(name, shape, dtype):
             return keep.tile(shape, dtype, name=name, align_bytes=64)
+
+        def bank(i):
+            return psum.tile([P, N], F32, name="bank%d" % i)
 
         def scalar_cast(dst, src):
             nc.scalar.activation(out=dst, in_=src, func=COPY)
 
         def vector_cast(dst, src):
             nc.vector.tensor_copy(out=dst, in_=src)
-
-        def gpsimd_cast(dst, src):
-            nc.gpsimd.tensor_scalar(out=dst, in0=src, scalar1=1.0, scalar2=0.0, op0=MULT, op1=ADD)
 
         def half(h):
             return slice(h * H, (h + 1) * H)
@@ -58,10 +56,10 @@ def tile_attend_gat_sig_v_kernel(tc, qT, kT, rw, dom, offs, out):
         def chunk(wide, c):
             return wide[:, c * N : (c + 1) * N]
 
-        offsets = keep.tile([P, B * LIST_COLS], U16, name="offsets")
+        offsets = keep.tile([P, SLOTS // 16], U16, name="offsets")
 
-        def seq_offsets(b, lo, hi):
-            return offsets[:, b * LIST_COLS + lo // 16 : b * LIST_COLS + hi // 16]
+        def listed(window, lo, hi):
+            return window[:].indirect(offsets[:, lo // 16 : hi // 16])
 
         gate = [tile("gate%d" % b, [P, 1, PACK], F32) for b in range(B)]
         for b in range(B):
@@ -79,18 +77,13 @@ def tile_attend_gat_sig_v_kernel(tc, qT, kT, rw, dom, offs, out):
         key_rows = kT.rearrange("(p u e) t -> u p e t", u=2, e=2)
         key_pairs = [tile("key_pairs%d" % u, [P, T], U32) for u in range(2)]
 
-        early = tile("early", [P, 3 * N], F32)
-        picked = [
-            tile("picked0", [P, N, 2], U32)[:],
-            early[:, N : 3 * N].bitcast(U32).rearrange("p (n u) -> p n u", u=2),
-        ]
-        room = tile("room", [P, 5 * N], BF16)
+        picked = [tile("picked%d" % b, [P, N, 2], U32)[:] for b in range(B)]
         shared = tile("shared", [P, 3, N], F32)
         pair_rows = shared[:, 0:2, :].rearrange("p u n -> p (u n)").bitcast(U32).rearrange("p (u n) -> p u n", u=2)
 
         def gather(b, u, lo, hi):
             dst = picked[0][:, lo:hi, u] if b == 0 else pair_rows[:, u, lo:hi]
-            nc.vector.tensor_copy(dst, key_pairs[u][:].indirect(seq_offsets(b, lo, hi)))
+            nc.vector.tensor_copy(dst, listed(key_pairs[u], b * N + lo, b * N + hi))
 
         for u in range(2):
             pairs = key_pairs[u][:].bitcast(BF16).rearrange("p (t e) -> p t e", e=2)
@@ -114,26 +107,34 @@ def tile_attend_gat_sig_v_kernel(tc, qT, kT, rw, dom, offs, out):
                 for b in range(B):
                     gather(b, 0, 0, N)
 
-        late = tile("late", [P, PACK * H], F32)
-
         def load_half(raw, src, h):
             nc.sync.dma_start(out=raw, in_=src.rearrange("(p j) c -> p j c", j=PACK)[:, :, half(h)])
             return raw
 
-        last_half = [
-            shared[:, 1:3, :].rearrange("p a (j c) -> p (a j) c", j=2),
-            late[:].rearrange("p (j c) -> p j c", j=PACK),
-        ]
         q_raw = {}
         dom_raw = {}
         for b in range(B):
-            q_raw[b, 0] = load_half(tile("q_raw%d_0" % b, [P, PACK, H], F32)[:], qT[b], 0)
-            q_raw[b, 1] = load_half(last_half[b], qT[b], 1)
+            for h in range(2):
+                if (b, h) == (0, 1):
+                    raw = shared[:, 1:3, :].rearrange("p a (j c) -> p (a j) c", j=2)
+                else:
+                    raw = tile("q_raw%d_%d" % (b, h), [P, PACK, H], F32)[:]
+                q_raw[b, h] = load_half(raw, qT[b], h)
             for h in range(2):
                 dom_raw[b, h] = load_half(tile("dom_raw%d_%d" % (b, h), [P, PACK, H], F32)[:], dom[b], h)
 
         def operand(name, words):
             return tile(name + "_codes", [P, words], U32), tile(name + "_scales", [P, words], U8)
+
+        planes = tile("planes", [P, N], U8)
+        keys = [(tile("key0_codes", [P, N], U32), planes[4:P, :]), operand("key1", N)]
+        queries = [operand("query%d" % b, R) for b in range(B)]
+        weights = [operand("weight%d" % b, N) for b in range(B)]
+        grads = [operand("grad%d" % b, DV) for b in range(B)]
+        q_grouped = [tile("q_grouped%d" % b, [P, PACK, P, PACK], BF16)[:] for b in range(B)]
+        dom_grouped = [tile("dom_grouped%d" % b, [P, PACK * DV], BF16)[:] for b in range(B)]
+        probs = [[tile("prob%d_%d" % (b, c), [P, N], F32)[:] for c in range(PACK)] for b in range(B)]
+        pw = [tile("pw%d" % b, [P, PACK * N], BF16)[:] for b in range(B)]
 
         def query_tile(b, t):
             codes, scales = queries[b]
@@ -155,152 +156,146 @@ def tile_attend_gat_sig_v_kernel(tc, qT, kT, rw, dom, offs, out):
                 stop=True,
             )
 
-        probs = [
-            [early[:, H : H + N], early[:, H + N : H + 2 * N]] + [tile("prob0_%d" % c, [P, N], F32)[:] for c in (2, 3)],
-            [tile("prob1_%d" % c, [P, N], F32)[:] for c in range(PACK)],
-        ]
-        q_grouped = [
-            tile("q_grouped0", [P, PACK, P, PACK], BF16)[:],
-            room[:, 0 : 4 * N].rearrange("p (t m j) -> p t m j", t=PACK, j=PACK),
-        ]
-        planes = tile("planes", [P, N], U8)
-        keys = [(tile("key0_codes", [P, N], U32), planes[4:P, :]), operand("key1", N)]
-        queries = [operand("query%d" % b, R) for b in range(B)]
-        weights = [operand("weight0", H + N), operand("weight1", N)]
-        nc.gpsimd.memset(weights[0][0][:, 0:H], 0)
-        nc.gpsimd.memset(weights[0][1][:, 0:H], 0)
-        grads = [operand("grad%d" % b, DV) for b in range(B)]
-
-        def quantise_keys(b):
-            for h in range(2):
-                quantise(keys[b], half(h), picked[b][:, half(h), :].rearrange("p n u -> p (n u)").bitcast(BF16), E4M3)
-
-        def interleave_keys():
-            by_slot = pair_rows.rearrange("p u n -> p n u")
-            for h in range(2):
-                nc.scalar.copy(out=picked[1][:, half(h)], in_=by_slot[:, half(h)])
+        def quantise_keys(b, lo, hi):
+            quantise(keys[b], slice(lo, hi), picked[b][:, lo:hi, :].rearrange("p n u -> p (n u)").bitcast(BF16), E4M3)
 
         def cast_queries(cast, b, h, lo, hi):
             dst = q_grouped[b].rearrange("p t m j -> p m j t")[:, GROUPS * h + lo : GROUPS * h + hi]
             cast(dst, q_raw[b, h].rearrange("p j (m t) -> p m j t", t=PACK)[:, lo:hi])
 
-        def cast_grad(cast, b, m, dst):
+        def cast_grad(cast, b, m):
             cast(
-                dst.rearrange("p (c i j) -> p c j i", i=4, j=PACK),
+                chunk(dom_grouped[b], m).rearrange("p (c i j) -> p c j i", i=4, j=PACK),
                 dom_raw[b, m // 2][:, :, block(m % 2)].rearrange("p j (c i) -> p c j i", i=4),
             )
 
-        def quantise_grad(b, m, dst):
-            cast_grad(scalar_cast, b, m, dst)
-            quantise(grads[b], block(m), dst, E5M2)
+        def quantise_grads(b, lo, hi):
+            quantise(grads[b], slice(lo * P, hi * P), dom_grouped[b][:, lo * N : hi * N], E5M2)
 
-        def score(b, c):
-            if (b, c) == (0, PACK - 1):
-                scores = psum.tile([P, PACK, P], F32, name="first", bufs=1)
-            else:
-                scores = psum.tile([P, PACK, P], F32, name="scores", bufs=3)
+        def sigmoid(b, c, where):
+            scores = bank(where)[:].rearrange("p (t n) -> p t n", t=PACK)
             for t in range(PACK):
                 multiply(scores[:, t, :], query_tile(b, t), block(0), E4M3, keys[b], block(c))
-            return scores
-
-        def sigmoid(b, c):
-            scores = score(b, c)
-            prob = probs[b][c].rearrange("p (n t) -> p n t", t=PACK)
-            nc.scalar.activation(out=prob, in_=scores[:].rearrange("p t n -> p n t"), func=SIGMOID)
-
-        def weigh(engine, b, c, pw):
-            prob = probs[b][c].rearrange("p (n t) -> p n t", t=PACK)
-            engine.tensor_tensor(
-                out=pw.rearrange("p (n t) -> p n t", t=PACK), in0=prob, in1=gate[b][:].broadcast_to([P, P, PACK]), op=MULT
+            nc.scalar.activation(
+                out=probs[b][c].rearrange("p (n t) -> p n t", t=PACK), in_=scores.rearrange("p t n -> p n t"), func=SIGMOID
             )
 
-        def sigmoid_and_weigh_on_scalar(b, c, pw):
-            prob = probs[b][c].rearrange("p (t n) -> p t n", t=PACK)
-            nc.scalar.activation(out=prob, in_=score(b, c)[:], func=SIGMOID)
-            by_tile = tile("by_tile", [P, PACK, P], BF16)
-            for t in range(PACK):
-                nc.scalar.activation(out=by_tile[:, t, :], in_=prob[:, t, :], func=COPY, scale=gate[b][:, 0, t : t + 1])
-            nc.scalar.copy(
-                out=pw.rearrange("p (c i t) -> p c t i", i=4, t=PACK),
-                in_=by_tile[:].rearrange("p t (c i) -> p c t i", i=4),
+        def weigh(b, c):
+            nc.vector.tensor_tensor(
+                out=chunk(pw[b], c).rearrange("p (n t) -> p n t", t=PACK),
+                in0=probs[b][c].rearrange("p (n t) -> p n t", t=PACK),
+                in1=gate[b][:].broadcast_to([P, P, PACK]),
+                op=MULT,
             )
 
-        def product(b, m, first):
-            if (b, m, first) == (0, 0, 0):
-                acc = psum.tile([P, N], F32, name="first", bufs=1)
-            else:
-                acc = psum.tile([P, N], F32, name="acc")
-            multiply(acc[:], grads[b], block(m), E5M2, weights[b], slice(first, first + N))
-            return acc
+        def quantise_weights(b, h):
+            quantise(weights[b], half(h), pw[b][:, 2 * h * N : 2 * (h + 1) * N], E4M3)
 
-        waiting = []
+        def product(acc, b, m, cols):
+            multiply(acc, grads[b], block(m), E5M2, weights[b], cols)
 
-        def copy_out(b, m, acc, lo, hi, dense):
-            scalar_cast(dense, acc)
-            waiting.append((b, m, lo, hi, dense))
+        def vector_scatter(m, lo, hi, dense):
+            nc.vector.tensor_copy(listed(window[m], lo, hi), dense)
 
-        def scatter_waiting():
-            for b, m, lo, hi, dense in waiting:
-                nc.vector.tensor_copy(window[m][:].indirect(seq_offsets(b, lo, hi)), dense)
-                if b == B - 1:
-                    for queue, cols in ((nc.sync, slice(0, T // 2)), (nc.scalar, slice(T // 2, T))):
-                        queue.dma_start(out=out[block(m), cols], in_=window[m][:, cols])
-            waiting.clear()
+        def scalar_scatter(m, lo, hi, dense):
+            nc.scalar.activation(out=listed(window[m], lo, hi), in_=dense, func=COPY)
 
         for h in range(2):
             gather(0, 1, h * H, (h + 1) * H)
-        quantise_keys(0)
+        for h in range(2):
+            quantise_keys(0, h * H, (h + 1) * H)
         cast_queries(scalar_cast, 0, 0, 0, GROUPS)
         cast_queries(scalar_cast, 0, 1, 0, SCALAR_GROUPS)
         cast_queries(vector_cast, 0, 1, SCALAR_GROUPS, GROUPS)
         for t in range(PACK):
             quantise(query_tile(0, t), block(0), q_grouped[0][:, t].rearrange("p m j -> p (m j)"), E4M3)
-        quantise_grad(0, 0, tile("grad_room0", [P, N], BF16)[:])
-        middle_blocks = early[:, 0:N].bitcast(BF16)
-        cast_grad(scalar_cast, 0, 1, chunk(middle_blocks, 0))
+        for m in range(2):
+            cast_grad(scalar_cast, 0, m)
         gather(1, 1, 0, N)
+        quantise_grads(0, 0, 2)
 
+        for c in range(PACK):
+            sigmoid(0, c, c % 3)
         for c in range(2):
-            sigmoid(0, c)
-            weigh(nc.vector, 0, c, chunk(room, 3 + c))
-        for c in range(2):
-            quantise(weights[0], block(2 + c), chunk(room, 3 + c), E4M3)
-        cast_grad(scalar_cast, 0, 2, chunk(middle_blocks, 1))
-        quantise(grads[0], slice(P, 3 * P), middle_blocks, E5M2)
-        copy_out(0, 0, product(0, 0, 0)[:, H:N], 0, H, tile("dense0_0a", [P, H], F32)[:])
-        interleave_keys()
-        quantise_keys(1)
-        for c in range(2, 4):
-            sigmoid(0, c)
-        copy_out(0, 1, product(0, 1, 0)[:, H:N], 0, H, tile("dense0_1a", [P, H], F32)[:])
-        scatter_waiting()
+            weigh(0, c)
+        quantise_weights(0, 0)
+        first = tile("first", [P, 2, H], F32)
+        acc = bank(4)
+        for m in range(2):
+            product(acc[:, half(m)], 0, m, half(0))
+        scalar_cast(first[:].rearrange("p m n -> p (m n)"), acc[:])
+        for m in range(2):
+            scalar_scatter(m, 0, H, first[:, m, :])
 
-        spent_keys = picked[1].rearrange("p n u -> p (n u)").bitcast(BF16)
-        for c in range(2, 4):
-            weigh(nc.gpsimd, 0, c, chunk(spent_keys, c))
-        quantise(weights[0], slice(N, N + H), spent_keys[:, 2 * N : 4 * N], E4M3)
+        vector_cast(picked[1], pair_rows.rearrange("p u n -> p n u"))
+        for c in range(2, PACK):
+            weigh(0, c)
+        quantise_weights(0, 1)
+        second = tile("second", [P, 2, H], F32)
+        acc = bank(5)
+        product(acc[:, 0:H], 0, 0, half(1))
+        scalar_cast(second[:, 0, :], acc[:, 0:H])
+        scalar_scatter(0, H, N, second[:, 0, :])
+
+        quantise_keys(1, 0, N)
         for h in range(2):
-            for lo in range(0, GROUPS, PIECE_GROUPS):
-                cast_queries(scalar_cast, 1, h, lo, lo + PIECE_GROUPS)
+            cast_queries(vector_cast, 1, h, 0, GROUPS)
         quantise(queries[1], slice(0, R), q_grouped[1].rearrange("p t m j -> p (t m j)"), E4M3)
-        copy_out(0, 2, product(0, 2, 0)[:, H:N], 0, H, probs[0][3][:, 0:H])
-        quantise_grad(0, 3, probs[0][3][:, H:N].bitcast(BF16))
-        for m in range(BLOCKS - 1):
-            copy_out(0, m, product(0, m, H)[:, H:N], H, N, late[:, m * H : (m + 1) * H])
-        scatter_waiting()
-
-        cast_grad(gpsimd_cast, 1, 0, chunk(room, 0))
-        pw = tile("pw1", [P, PACK * N], BF16)
-        for c in range(PACK - 1):
-            sigmoid(1, c)
-            weigh(nc.gpsimd, 1, c, chunk(pw, c))
-        sigmoid_and_weigh_on_scalar(1, PACK - 1, chunk(pw, PACK - 1))
-        for m in range(1, BLOCKS):
-            cast_grad(scalar_cast, 1, m, chunk(room, m))
-        quantise(grads[1], slice(0, DV), room[:, 0 : 4 * N], E5M2)
-        quantise(weights[1], slice(0, N), pw[:], E4M3)
-
-        copy_out(0, BLOCKS - 1, product(0, BLOCKS - 1, H)[:], 0, N, probs[1][2])
+        for c in range(PACK):
+            sigmoid(1, c, c)
+        acc = bank(2)
+        product(acc[:, 0:H], 0, 1, half(1))
+        scalar_cast(second[:, 1, :], acc[:, 0:H])
         for m in range(BLOCKS):
-            copy_out(1, m, product(1, m, 0)[:], 0, N, tile("dense1_%d" % m, [P, N], F32)[:])
-        scatter_waiting()
+            cast_grad(vector_cast, 1, m)
+        quantise_grads(1, 0, BLOCKS)
+        for m in range(2, BLOCKS):
+            cast_grad(vector_cast, 0, m)
+        quantise_grads(0, 2, BLOCKS)
+        dense = {m: tile("dense%d" % m, [P, SLOTS], F32) for m in range(1, BLOCKS)}
+        for m in range(2, BLOCKS):
+            acc = bank(4 + m)
+            product(acc[:], 0, m, slice(0, N))
+            scalar_cast(dense[m][:, 0:N], acc[:])
+        scalar_scatter(1, H, N, second[:, 1, :])
+
+        for c in range(2):
+            weigh(1, c)
+        quantise_weights(1, 0)
+        for c in range(2, PACK):
+            weigh(1, c)
+        third = bank(4)
+        product(third[:, 0:H], 1, 0, half(0))
+        vector_cast(probs[1][PACK - 1][:, 0:H], third[:, 0:H])
+        quantise_weights(1, 1)
+        acc = bank(5)
+        product(acc[:, 0:H], 1, 1, half(0))
+        scalar_cast(dense[1][:, N : N + H], acc[:, 0:H])
+        scalar_scatter(1, N, N + H, dense[1][:, N : N + H])
+
+        vector_scatter(0, N, N + H, probs[1][PACK - 1][:, 0:H])
+        acc = bank(3)
+        product(acc[:, 0:H], 1, 0, half(1))
+        vector_cast(dense[1][:, 0:H], acc[:, 0:H])
+        vector_scatter(0, N + H, SLOTS, dense[1][:, 0:H])
+        nc.sync.dma_start(out=out[block(0), :], in_=window[0][:])
+
+        acc = bank(0)
+        product(acc[:], 1, 2, slice(0, N))
+        scalar_cast(probs[1][PACK - 1], acc[:])
+        acc = bank(6)
+        product(acc[:, 0:H], 1, 1, half(1))
+        scalar_cast(dense[1][:, N + H : SLOTS], acc[:, 0:H])
+        acc = bank(1)
+        product(acc[:], 1, 3, slice(0, N))
+        scalar_cast(dense[3][:, N:SLOTS], acc[:])
+        scalar_scatter(1, N + H, SLOTS, dense[1][:, N + H : SLOTS])
+        nc.scalar.dma_start(out=out[block(1), :], in_=window[1][:])
+
+        vector_scatter(2, N, SLOTS, probs[1][PACK - 1])
+        vector_scatter(2, 0, N, dense[2][:, 0:N])
+        nc.sync.dma_start(out=out[block(2), :], in_=window[2][:])
+
+        for lo, hi in ((640, SLOTS), (H, 640), (0, H)):
+            scalar_scatter(3, lo, hi, dense[3][:, lo:hi])
+        nc.scalar.dma_start(out=out[block(3), :], in_=window[3][:])

@@ -77,7 +77,11 @@ def tile_attend_gat_sig_v_kernel(tc, qT, kT, rw, dom, offs, out):
         key_rows = kT.rearrange("(p u e) t -> u p e t", u=2, e=2)
         key_pairs = [tile("key_pairs%d" % u, [P, T], U32) for u in range(2)]
 
-        picked = [tile("picked%d" % b, [P, N, 2], U32)[:] for b in range(B)]
+        lane = tile("lane", [P, 6 * N], BF16)
+        picked = [
+            tile("picked0", [P, N, 2], U32)[:],
+            lane[:, 0 : 4 * N].bitcast(U32).rearrange("p (n u) -> p n u", u=2),
+        ]
         shared = tile("shared", [P, 3, N], F32)
         pair_rows = shared[:, 0:2, :].rearrange("p u n -> p (u n)").bitcast(U32).rearrange("p (u n) -> p u n", u=2)
 
@@ -131,10 +135,26 @@ def tile_attend_gat_sig_v_kernel(tc, qT, kT, rw, dom, offs, out):
         queries = [operand("query%d" % b, R) for b in range(B)]
         weights = [operand("weight%d" % b, N) for b in range(B)]
         grads = [operand("grad%d" % b, DV) for b in range(B)]
-        q_grouped = [tile("q_grouped%d" % b, [P, PACK, P, PACK], BF16)[:] for b in range(B)]
-        dom_grouped = [tile("dom_grouped%d" % b, [P, PACK * DV], BF16)[:] for b in range(B)]
+        room = tile("room", [P, 2 * N], F32)
         probs = [[tile("prob%d_%d" % (b, c), [P, N], F32)[:] for c in range(PACK)] for b in range(B)]
-        pw = [tile("pw%d" % b, [P, PACK * N], BF16)[:] for b in range(B)]
+        probs[0][2] = room[:, 0:N]
+        q_grouped = [
+            tile("q_grouped0", [P, PACK, P, PACK], BF16)[:],
+            room[:].bitcast(BF16).rearrange("p (t m j) -> p t m j", t=PACK, j=PACK),
+        ]
+        dom_grouped = {
+            (0, 0): tile("dom_grouped0", [P, 2 * N], BF16)[:],
+            (0, 1): probs[0][1].bitcast(BF16),
+            (1, 0): room[:, 0:N].bitcast(BF16),
+            (1, 1): room[:, N : 2 * N].bitcast(BF16),
+        }
+        pw1 = tile("pw1", [P, PACK * N], BF16)
+        pw = {
+            (0, 0): lane[:, 3 * N : 5 * N],
+            (0, 1): lane[:, 4 * N : 6 * N],
+            (1, 0): pw1[:, 0 : 2 * N],
+            (1, 1): pw1[:, 2 * N : 4 * N],
+        }
 
         def query_tile(b, t):
             codes, scales = queries[b]
@@ -165,12 +185,12 @@ def tile_attend_gat_sig_v_kernel(tc, qT, kT, rw, dom, offs, out):
 
         def cast_grad(cast, b, m):
             cast(
-                chunk(dom_grouped[b], m).rearrange("p (c i j) -> p c j i", i=4, j=PACK),
+                chunk(dom_grouped[b, m // 2], m % 2).rearrange("p (c i j) -> p c j i", i=4, j=PACK),
                 dom_raw[b, m // 2][:, :, block(m % 2)].rearrange("p j (c i) -> p c j i", i=4),
             )
 
-        def quantise_grads(b, lo, hi):
-            quantise(grads[b], slice(lo * P, hi * P), dom_grouped[b][:, lo * N : hi * N], E5M2)
+        def quantise_grads(b, h):
+            quantise(grads[b], half(h), dom_grouped[b, h], E5M2)
 
         def sigmoid(b, c, where):
             scores = bank(where)[:].rearrange("p (t n) -> p t n", t=PACK)
@@ -182,14 +202,14 @@ def tile_attend_gat_sig_v_kernel(tc, qT, kT, rw, dom, offs, out):
 
         def weigh(b, c):
             nc.vector.tensor_tensor(
-                out=chunk(pw[b], c).rearrange("p (n t) -> p n t", t=PACK),
+                out=chunk(pw[b, c // 2], c % 2).rearrange("p (n t) -> p n t", t=PACK),
                 in0=probs[b][c].rearrange("p (n t) -> p n t", t=PACK),
                 in1=gate[b][:].broadcast_to([P, P, PACK]),
                 op=MULT,
             )
 
         def quantise_weights(b, h):
-            quantise(weights[b], half(h), pw[b][:, 2 * h * N : 2 * (h + 1) * N], E4M3)
+            quantise(weights[b], half(h), pw[b, h], E4M3)
 
         def product(acc, b, m, cols):
             multiply(acc, grads[b], block(m), E5M2, weights[b], cols)
@@ -212,90 +232,83 @@ def tile_attend_gat_sig_v_kernel(tc, qT, kT, rw, dom, offs, out):
         for m in range(2):
             cast_grad(scalar_cast, 0, m)
         gather(1, 1, 0, N)
-        quantise_grads(0, 0, 2)
+        quantise_grads(0, 0)
 
         for c in range(PACK):
             sigmoid(0, c, c % 3)
         for c in range(2):
             weigh(0, c)
         quantise_weights(0, 0)
-        first = tile("first", [P, 2, H], F32)
-        acc = bank(4)
-        for m in range(2):
-            product(acc[:, half(m)], 0, m, half(0))
-        scalar_cast(first[:].rearrange("p m n -> p (m n)"), acc[:])
-        for m in range(2):
-            scalar_scatter(m, 0, H, first[:, m, :])
+        for m in range(2, BLOCKS):
+            cast_grad(scalar_cast, 0, m)
 
-        vector_cast(picked[1], pair_rows.rearrange("p u n -> p n u"))
+        def pair_of_products(where, h, dense):
+            acc = bank(where)
+            for m in range(2):
+                product(acc[:, half(m)], 0, m, half(h))
+            scalar_cast(dense, acc[:])
+
+        def whole_product(where, b, m, cast, dense):
+            acc = bank(where)
+            product(acc[:], b, m, slice(0, N))
+            cast(dense, acc[:])
+
+        def half_product(where, h, dense):
+            acc = bank(where)
+            product(acc[:, 0:H], 1, 0, half(h))
+            vector_cast(dense, acc[:, 0:H])
+
+        first = tile("first", [P, N], F32)
+        pair_of_products(4, 0, first[:])
+        for m in range(2):
+            scalar_scatter(m, 0, H, first[:, half(m)])
+
         for c in range(2, PACK):
             weigh(0, c)
         quantise_weights(0, 1)
-        second = tile("second", [P, 2, H], F32)
-        acc = bank(5)
-        product(acc[:, 0:H], 0, 0, half(1))
-        scalar_cast(second[:, 0, :], acc[:, 0:H])
-        scalar_scatter(0, H, N, second[:, 0, :])
-
+        vector_cast(picked[1], pair_rows.rearrange("p u n -> p n u"))
         quantise_keys(1, 0, N)
+        quantise_grads(0, 1)
         for h in range(2):
             cast_queries(vector_cast, 1, h, 0, GROUPS)
         quantise(queries[1], slice(0, R), q_grouped[1].rearrange("p t m j -> p (t m j)"), E4M3)
         for c in range(PACK):
             sigmoid(1, c, c)
-        acc = bank(2)
-        product(acc[:, 0:H], 0, 1, half(1))
-        scalar_cast(second[:, 1, :], acc[:, 0:H])
+        dense3 = tile("dense3", [P, SLOTS], F32)
+        whole_product(7, 0, 3, scalar_cast, dense3[:, 0:N])
         for m in range(BLOCKS):
             cast_grad(vector_cast, 1, m)
-        quantise_grads(1, 0, BLOCKS)
-        for m in range(2, BLOCKS):
-            cast_grad(vector_cast, 0, m)
-        quantise_grads(0, 2, BLOCKS)
-        dense = {m: tile("dense%d" % m, [P, SLOTS], F32) for m in range(1, BLOCKS)}
-        for m in range(2, BLOCKS):
-            acc = bank(4 + m)
-            product(acc[:], 0, m, slice(0, N))
-            scalar_cast(dense[m][:, 0:N], acc[:])
-        scalar_scatter(1, H, N, second[:, 1, :])
+        quantise(grads[1], slice(0, DV), room[:].bitcast(BF16), E5M2)
+        spent_dom = dom_raw[1, 1].rearrange("p j c -> p (j c)")
+        whole_product(6, 0, 2, scalar_cast, spent_dom[:, 0:N])
 
         for c in range(2):
             weigh(1, c)
         quantise_weights(1, 0)
+        pair_of_products(5, 1, probs[1][0])
+        for m in range(2):
+            scalar_scatter(m, H, N, probs[1][0][:, half(m)])
         for c in range(2, PACK):
             weigh(1, c)
-        third = bank(4)
-        product(third[:, 0:H], 1, 0, half(0))
-        vector_cast(probs[1][PACK - 1][:, 0:H], third[:, 0:H])
+        half_product(4, 0, probs[1][PACK - 1][:, 0:H])
         quantise_weights(1, 1)
-        acc = bank(5)
-        product(acc[:, 0:H], 1, 1, half(0))
-        scalar_cast(dense[1][:, N : N + H], acc[:, 0:H])
-        scalar_scatter(1, N, N + H, dense[1][:, N : N + H])
 
         vector_scatter(0, N, N + H, probs[1][PACK - 1][:, 0:H])
-        acc = bank(3)
-        product(acc[:, 0:H], 1, 0, half(1))
-        vector_cast(dense[1][:, 0:H], acc[:, 0:H])
-        vector_scatter(0, N + H, SLOTS, dense[1][:, 0:H])
+        half_product(7, 1, probs[1][PACK - 1][:, H:N])
+        whole_product(0, 1, 1, scalar_cast, probs[1][1])
+        whole_product(1, 1, 2, vector_cast, spent_dom[:, N:SLOTS])
+        whole_product(2, 1, 3, scalar_cast, dense3[:, N:SLOTS])
+        vector_scatter(0, N + H, SLOTS, probs[1][PACK - 1][:, H:N])
         nc.sync.dma_start(out=out[block(0), :], in_=window[0][:])
 
-        acc = bank(0)
-        product(acc[:], 1, 2, slice(0, N))
-        scalar_cast(probs[1][PACK - 1], acc[:])
-        acc = bank(6)
-        product(acc[:, 0:H], 1, 1, half(1))
-        scalar_cast(dense[1][:, N + H : SLOTS], acc[:, 0:H])
-        acc = bank(1)
-        product(acc[:], 1, 3, slice(0, N))
-        scalar_cast(dense[3][:, N:SLOTS], acc[:])
-        scalar_scatter(1, N + H, SLOTS, dense[1][:, N + H : SLOTS])
+        for h in range(2):
+            scalar_scatter(1, N + h * H, N + (h + 1) * H, probs[1][1][:, half(h)])
         nc.scalar.dma_start(out=out[block(1), :], in_=window[1][:])
 
-        vector_scatter(2, N, SLOTS, probs[1][PACK - 1])
-        vector_scatter(2, 0, N, dense[2][:, 0:N])
+        vector_scatter(2, N, SLOTS, spent_dom[:, N:SLOTS])
+        vector_scatter(2, 0, N, spent_dom[:, 0:N])
         nc.sync.dma_start(out=out[block(2), :], in_=window[2][:])
 
         for lo, hi in ((640, SLOTS), (H, 640), (0, H)):
-            scalar_scatter(3, lo, hi, dense[3][:, lo:hi])
+            scalar_scatter(3, lo, hi, dense3[:, lo:hi])
         nc.scalar.dma_start(out=out[block(3), :], in_=window[3][:])

@@ -232,12 +232,12 @@ def tile_attend_gat_sig_v_kernel(tc, qT, kT, rw, dom, offs, out):
         for m in range(2):
             cast_grad(scalar_cast, 0, m)
         gather(1, 1, 0, N)
-        quantise_grads(0, 0)
 
         for c in range(PACK):
             sigmoid(0, c, c % 3)
         for c in range(2):
             weigh(0, c)
+        quantise_grads(0, 0)
         quantise_weights(0, 0)
         for m in range(2, BLOCKS):
             cast_grad(scalar_cast, 0, m)
@@ -265,12 +265,12 @@ def tile_attend_gat_sig_v_kernel(tc, qT, kT, rw, dom, offs, out):
 
         for c in range(2, PACK):
             weigh(0, c)
-        quantise_weights(0, 1)
         vector_cast(picked[1], pair_rows.rearrange("p u n -> p n u"))
-        quantise_keys(1, 0, N)
+        quantise_weights(0, 1)
         quantise_grads(0, 1)
         for h in range(2):
             cast_queries(vector_cast, 1, h, 0, GROUPS)
+        quantise_keys(1, 0, N)
         quantise(queries[1], slice(0, R), q_grouped[1].rearrange("p t m j -> p (t m j)"), E4M3)
         for c in range(PACK):
             sigmoid(1, c, c)
@@ -279,8 +279,6 @@ def tile_attend_gat_sig_v_kernel(tc, qT, kT, rw, dom, offs, out):
         for m in range(BLOCKS):
             cast_grad(vector_cast, 1, m)
         quantise(grads[1], slice(0, DV), room[:].bitcast(BF16), E5M2)
-        spent_dom = dom_raw[1, 1].rearrange("p j c -> p (j c)")
-        whole_product(6, 0, 2, scalar_cast, spent_dom[:, 0:N])
 
         for c in range(2):
             weigh(1, c)
@@ -295,9 +293,10 @@ def tile_attend_gat_sig_v_kernel(tc, qT, kT, rw, dom, offs, out):
 
         vector_scatter(0, N, N + H, probs[1][PACK - 1][:, 0:H])
         half_product(7, 1, probs[1][PACK - 1][:, H:N])
+        whole_product(1, 1, 2, vector_cast, first[:])
         whole_product(0, 1, 1, scalar_cast, probs[1][1])
-        whole_product(1, 1, 2, vector_cast, spent_dom[:, N:SLOTS])
         whole_product(2, 1, 3, scalar_cast, dense3[:, N:SLOTS])
+        whole_product(6, 0, 2, scalar_cast, probs[1][0])
         vector_scatter(0, N + H, SLOTS, probs[1][PACK - 1][:, H:N])
         nc.sync.dma_start(out=out[block(0), :], in_=window[0][:])
 
@@ -305,10 +304,10 @@ def tile_attend_gat_sig_v_kernel(tc, qT, kT, rw, dom, offs, out):
             scalar_scatter(1, N + h * H, N + (h + 1) * H, probs[1][1][:, half(h)])
         nc.scalar.dma_start(out=out[block(1), :], in_=window[1][:])
 
-        vector_scatter(2, N, SLOTS, spent_dom[:, N:SLOTS])
-        vector_scatter(2, 0, N, spent_dom[:, 0:N])
+        vector_scatter(2, N, SLOTS, first[:])
+        vector_scatter(2, 0, N, probs[1][0])
         nc.sync.dma_start(out=out[block(2), :], in_=window[2][:])
 
         for lo, hi in ((640, SLOTS), (H, 640), (0, H)):
             scalar_scatter(3, lo, hi, dense3[:, lo:hi])
-        nc.scalar.dma_start(out=out[block(3), :], in_=window[3][:])
+        nc.sync.dma_start(out=out[block(3), :], in_=window[3][:])

@@ -26,6 +26,7 @@ SLOTS = B * N
 KEY_LOADS = (((1536, 704), (512, 128)), ((1024, 768), (768, 256), (256, 96)))
 GROUPS = H // PACK
 SCALAR_GROUPS = 28
+EARLY = 288
 
 
 def tile_attend_gat_sig_v_kernel(tc, qT, kT, rw, dom, offs, out):
@@ -148,12 +149,11 @@ def tile_attend_gat_sig_v_kernel(tc, qT, kT, rw, dom, offs, out):
             (1, 0): room[:, 0:N].bitcast(BF16),
             (1, 1): room[:, N : 2 * N].bitcast(BF16),
         }
-        pw1 = tile("pw1", [P, PACK * N], BF16)
         pw = {
             (0, 0): lane[:, 3 * N : 5 * N],
             (0, 1): lane[:, 4 * N : 6 * N],
-            (1, 0): pw1[:, 0 : 2 * N],
-            (1, 1): pw1[:, 2 * N : 4 * N],
+            (1, 0): room[:, 0:N].bitcast(BF16),
+            (1, 1): probs[1][1].bitcast(BF16),
         }
 
         def query_tile(b, t):
@@ -200,8 +200,8 @@ def tile_attend_gat_sig_v_kernel(tc, qT, kT, rw, dom, offs, out):
                 out=probs[b][c].rearrange("p (n t) -> p n t", t=PACK), in_=scores.rearrange("p t n -> p n t"), func=SIGMOID
             )
 
-        def weigh(b, c):
-            nc.vector.tensor_tensor(
+        def weigh(b, c, engine=nc.vector):
+            engine.tensor_tensor(
                 out=chunk(pw[b, c // 2], c % 2).rearrange("p (n t) -> p n t", t=PACK),
                 in0=probs[b][c].rearrange("p (n t) -> p n t", t=PACK),
                 in1=gate[b][:].broadcast_to([P, P, PACK]),
@@ -242,24 +242,24 @@ def tile_attend_gat_sig_v_kernel(tc, qT, kT, rw, dom, offs, out):
         for m in range(2, BLOCKS):
             cast_grad(scalar_cast, 0, m)
 
-        def pair_of_products(where, h, dense):
+        def pair_of_products(where, h, cast, dense):
             acc = bank(where)
             for m in range(2):
                 product(acc[:, half(m)], 0, m, half(h))
-            scalar_cast(dense, acc[:])
+            cast(dense, acc[:])
 
         def whole_product(where, b, m, cast, dense):
             acc = bank(where)
             product(acc[:], b, m, slice(0, N))
             cast(dense, acc[:])
 
-        def half_product(where, h, dense):
+        def half_product(where, m, h, cast, dense):
             acc = bank(where)
-            product(acc[:, 0:H], 1, 0, half(h))
-            vector_cast(dense, acc[:, 0:H])
+            product(acc[:, 0:H], 1, m, half(h))
+            cast(dense, acc[:, 0:H])
 
         first = tile("first", [P, N], F32)
-        pair_of_products(4, 0, first[:])
+        pair_of_products(4, 0, scalar_cast, first[:])
         for m in range(2):
             scalar_scatter(m, 0, H, first[:, half(m)])
 
@@ -280,32 +280,35 @@ def tile_attend_gat_sig_v_kernel(tc, qT, kT, rw, dom, offs, out):
             cast_grad(vector_cast, 1, m)
         quantise(grads[1], slice(0, DV), room[:].bitcast(BF16), E5M2)
 
+        dense2 = dom_raw[1, 1].rearrange("p j c -> p (j c)")
+        whole_product(6, 0, 2, vector_cast, dense2[:, 0:N])
+        pair_of_products(5, 1, vector_cast, room[:, N : 2 * N])
+        vector_scatter(2, 0, EARLY, dense2[:, 0:EARLY])
+
         for c in range(2):
-            weigh(1, c)
+            weigh(1, c, nc.gpsimd)
         quantise_weights(1, 0)
-        pair_of_products(5, 1, probs[1][0])
         for m in range(2):
-            scalar_scatter(m, H, N, probs[1][0][:, half(m)])
+            scalar_scatter(m, H, N, room[:, N + m * H : N + (m + 1) * H])
         for c in range(2, PACK):
             weigh(1, c)
-        half_product(4, 0, probs[1][PACK - 1][:, 0:H])
+        half_product(4, 0, 0, vector_cast, probs[1][PACK - 1][:, 0:H])
         quantise_weights(1, 1)
+        half_product(0, 1, 0, scalar_cast, first[:, 0:H])
+        scalar_scatter(1, N, N + H, first[:, 0:H])
 
         vector_scatter(0, N, N + H, probs[1][PACK - 1][:, 0:H])
-        half_product(7, 1, probs[1][PACK - 1][:, H:N])
-        whole_product(1, 1, 2, vector_cast, first[:])
-        whole_product(0, 1, 1, scalar_cast, probs[1][1])
+        half_product(7, 0, 1, vector_cast, probs[1][PACK - 1][:, H:N])
+        whole_product(1, 1, 2, vector_cast, dense2[:, N:SLOTS])
+        half_product(3, 1, 1, scalar_cast, first[:, H:N])
         whole_product(2, 1, 3, scalar_cast, dense3[:, N:SLOTS])
-        whole_product(6, 0, 2, scalar_cast, probs[1][0])
         vector_scatter(0, N + H, SLOTS, probs[1][PACK - 1][:, H:N])
         nc.sync.dma_start(out=out[block(0), :], in_=window[0][:])
 
-        for h in range(2):
-            scalar_scatter(1, N + h * H, N + (h + 1) * H, probs[1][1][:, half(h)])
+        scalar_scatter(1, N + H, SLOTS, first[:, H:N])
         nc.scalar.dma_start(out=out[block(1), :], in_=window[1][:])
 
-        vector_scatter(2, N, SLOTS, first[:])
-        vector_scatter(2, 0, N, probs[1][0])
+        vector_scatter(2, EARLY, SLOTS, dense2[:, EARLY:SLOTS])
         nc.sync.dma_start(out=out[block(2), :], in_=window[2][:])
 
         for lo, hi in ((640, SLOTS), (H, 640), (0, H)):

@@ -116,6 +116,7 @@ def tile_attend_gat_sig_v_kernel(tc, qT, kT, rw, dom, offs, out):
             nc.sync.dma_start(out=raw, in_=src.rearrange("(p j) c -> p j c", j=PACK)[:, :, half(h)])
             return raw
 
+        dense3 = tile("dense3", [P, SLOTS], F32)
         q_raw = {}
         dom_raw = {}
         for b in range(B):
@@ -126,7 +127,11 @@ def tile_attend_gat_sig_v_kernel(tc, qT, kT, rw, dom, offs, out):
                     raw = tile("q_raw%d_%d" % (b, h), [P, PACK, H], F32)[:]
                 q_raw[b, h] = load_half(raw, qT[b], h)
             for h in range(2):
-                dom_raw[b, h] = load_half(tile("dom_raw%d_%d" % (b, h), [P, PACK, H], F32)[:], dom[b], h)
+                if (b, h) == (1, 1):
+                    raw = dense3[:].rearrange("p (j c) -> p j c", j=PACK)
+                else:
+                    raw = tile("dom_raw%d_%d" % (b, h), [P, PACK, H], F32)[:]
+                dom_raw[b, h] = load_half(raw, dom[b], h)
 
         def operand(name, words):
             return tile(name + "_codes", [P, words], U32), tile(name + "_scales", [P, words], U8)
@@ -136,12 +141,15 @@ def tile_attend_gat_sig_v_kernel(tc, qT, kT, rw, dom, offs, out):
         queries = [operand("query%d" % b, R) for b in range(B)]
         weights = [operand("weight%d" % b, N) for b in range(B)]
         grads = [operand("grad%d" % b, DV) for b in range(B)]
-        room = tile("room", [P, 2 * N], F32)
+        wide_room = tile("room", [P, 2 * SLOTS], F32)
+        room = wide_room[:, H : H + 2 * N]
+        second = wide_room[:, 0:N]
+        dense2 = wide_room[:, SLOTS:]
         probs = [[tile("prob%d_%d" % (b, c), [P, N], F32)[:] for c in range(PACK)] for b in range(B)]
         probs[0][2] = room[:, 0:N]
         q_grouped = [
             tile("q_grouped0", [P, PACK, P, PACK], BF16)[:],
-            room[:].bitcast(BF16).rearrange("p (t m j) -> p t m j", t=PACK, j=PACK),
+            room.bitcast(BF16).rearrange("p (t m j) -> p t m j", t=PACK, j=PACK),
         ]
         dom_grouped = {
             (0, 0): tile("dom_grouped0", [P, 2 * N], BF16)[:],
@@ -152,7 +160,7 @@ def tile_attend_gat_sig_v_kernel(tc, qT, kT, rw, dom, offs, out):
         pw = {
             (0, 0): lane[:, 3 * N : 5 * N],
             (0, 1): lane[:, 4 * N : 6 * N],
-            (1, 0): room[:, 0:N].bitcast(BF16),
+            (1, 0): wide_room[:, N:SLOTS].bitcast(BF16),
             (1, 1): probs[1][1].bitcast(BF16),
         }
 
@@ -242,10 +250,10 @@ def tile_attend_gat_sig_v_kernel(tc, qT, kT, rw, dom, offs, out):
         for m in range(2, BLOCKS):
             cast_grad(scalar_cast, 0, m)
 
-        def pair_of_products(where, h, cast, dense):
+        def pair_of_products(where, b, h, cast, dense):
             acc = bank(where)
             for m in range(2):
-                product(acc[:, half(m)], 0, m, half(h))
+                product(acc[:, half(m)], b, m, half(h))
             cast(dense, acc[:])
 
         def whole_product(where, b, m, cast, dense):
@@ -253,13 +261,13 @@ def tile_attend_gat_sig_v_kernel(tc, qT, kT, rw, dom, offs, out):
             product(acc[:], b, m, slice(0, N))
             cast(dense, acc[:])
 
-        def half_product(where, m, h, cast, dense):
+        def half_product(where, b, m, h, cast, dense):
             acc = bank(where)
-            product(acc[:, 0:H], 1, m, half(h))
+            product(acc[:, 0:H], b, m, half(h))
             cast(dense, acc[:, 0:H])
 
         first = tile("first", [P, N], F32)
-        pair_of_products(4, 0, scalar_cast, first[:])
+        pair_of_products(4, 0, 0, scalar_cast, first[:])
         for m in range(2):
             scalar_scatter(m, 0, H, first[:, half(m)])
 
@@ -272,37 +280,38 @@ def tile_attend_gat_sig_v_kernel(tc, qT, kT, rw, dom, offs, out):
             cast_queries(vector_cast, 1, h, 0, GROUPS)
         quantise_keys(1, 0, N)
         quantise(queries[1], slice(0, R), q_grouped[1].rearrange("p t m j -> p (t m j)"), E4M3)
-        for c in range(PACK):
+        for c in range(2):
             sigmoid(1, c, c)
-        dense3 = tile("dense3", [P, SLOTS], F32)
-        whole_product(7, 0, 3, scalar_cast, dense3[:, 0:N])
         for m in range(BLOCKS):
             cast_grad(vector_cast, 1, m)
-        quantise(grads[1], slice(0, DV), room[:].bitcast(BF16), E5M2)
+        whole_product(7, 0, 3, scalar_cast, dense3[:, 0:N])
+        scalar_scatter(3, 0, H, dense3[:, 0:H])
+        for c in range(2, PACK):
+            sigmoid(1, c, c)
+        quantise(grads[1], slice(0, DV), room.bitcast(BF16), E5M2)
 
-        dense2 = dom_raw[1, 1].rearrange("p j c -> p (j c)")
         whole_product(6, 0, 2, vector_cast, dense2[:, 0:N])
-        pair_of_products(5, 1, vector_cast, room[:, N : 2 * N])
+        half_product(5, 0, 0, 1, vector_cast, second[:, N - H : N])
         vector_scatter(2, 0, EARLY, dense2[:, 0:EARLY])
 
         for c in range(2):
             weigh(1, c, nc.gpsimd)
         quantise_weights(1, 0)
-        for m in range(2):
-            scalar_scatter(m, H, N, room[:, N + m * H : N + (m + 1) * H])
+        half_product(0, 0, 1, 1, scalar_cast, probs[1][0][:, 0:H])
+        scalar_scatter(0, H, N, second[:, N - H : N])
+        scalar_scatter(1, H, N, probs[1][0][:, 0:H])
         for c in range(2, PACK):
             weigh(1, c)
-        half_product(4, 0, 0, vector_cast, probs[1][PACK - 1][:, 0:H])
+        pair_of_products(4, 1, 0, vector_cast, probs[1][PACK - 1])
         quantise_weights(1, 1)
-        half_product(0, 1, 0, scalar_cast, first[:, 0:H])
-        scalar_scatter(1, N, N + H, first[:, 0:H])
+        scalar_scatter(1, N, N + H, probs[1][PACK - 1][:, H:N])
 
         vector_scatter(0, N, N + H, probs[1][PACK - 1][:, 0:H])
-        half_product(7, 0, 1, vector_cast, probs[1][PACK - 1][:, H:N])
+        half_product(7, 1, 0, 1, vector_cast, first[:, 0:H])
         whole_product(1, 1, 2, vector_cast, dense2[:, N:SLOTS])
-        half_product(3, 1, 1, scalar_cast, first[:, H:N])
+        half_product(3, 1, 1, 1, scalar_cast, first[:, H:N])
         whole_product(2, 1, 3, scalar_cast, dense3[:, N:SLOTS])
-        vector_scatter(0, N + H, SLOTS, probs[1][PACK - 1][:, H:N])
+        vector_scatter(0, N + H, SLOTS, first[:, 0:H])
         nc.sync.dma_start(out=out[block(0), :], in_=window[0][:])
 
         scalar_scatter(1, N + H, SLOTS, first[:, H:N])
@@ -311,6 +320,6 @@ def tile_attend_gat_sig_v_kernel(tc, qT, kT, rw, dom, offs, out):
         vector_scatter(2, EARLY, SLOTS, dense2[:, EARLY:SLOTS])
         nc.sync.dma_start(out=out[block(2), :], in_=window[2][:])
 
-        for lo, hi in ((640, SLOTS), (H, 640), (0, H)):
+        for lo, hi in ((640, SLOTS), (H, 640)):
             scalar_scatter(3, lo, hi, dense3[:, lo:hi])
         nc.sync.dma_start(out=out[block(3), :], in_=window[3][:])

@@ -127,11 +127,7 @@ def tile_attend_gat_sig_v_kernel(tc, qT, kT, rw, dom, offs, out):
                     raw = tile("q_raw%d_%d" % (b, h), [P, PACK, H], F32)[:]
                 q_raw[b, h] = load_half(raw, qT[b], h)
             for h in range(2):
-                if (b, h) == (1, 1):
-                    raw = dense3[:].rearrange("p (j c) -> p j c", j=PACK)
-                else:
-                    raw = tile("dom_raw%d_%d" % (b, h), [P, PACK, H], F32)[:]
-                dom_raw[b, h] = load_half(raw, dom[b], h)
+                dom_raw[b, h] = load_half(tile("dom_raw%d_%d" % (b, h), [P, PACK, H], F32)[:], dom[b], h)
 
         def operand(name, words):
             return tile(name + "_codes", [P, words], U32), tile(name + "_scales", [P, words], U8)
@@ -147,6 +143,7 @@ def tile_attend_gat_sig_v_kernel(tc, qT, kT, rw, dom, offs, out):
         dense2 = wide_room[:, SLOTS:]
         probs = [[tile("prob%d_%d" % (b, c), [P, N], F32)[:] for c in range(PACK)] for b in range(B)]
         probs[0][2] = room[:, 0:N]
+        probs[1][0] = dense3[:, 0:N]
         q_grouped = [
             tile("q_grouped0", [P, PACK, P, PACK], BF16)[:],
             room.bitcast(BF16).rearrange("p (t m j) -> p t m j", t=PACK, j=PACK),
@@ -280,14 +277,12 @@ def tile_attend_gat_sig_v_kernel(tc, qT, kT, rw, dom, offs, out):
             cast_queries(vector_cast, 1, h, 0, GROUPS)
         quantise_keys(1, 0, N)
         quantise(queries[1], slice(0, R), q_grouped[1].rearrange("p t m j -> p (t m j)"), E4M3)
-        for c in range(2):
+        for c in range(PACK):
             sigmoid(1, c, c)
         for m in range(BLOCKS):
             cast_grad(vector_cast, 1, m)
-        whole_product(7, 0, 3, scalar_cast, dense3[:, 0:N])
-        scalar_scatter(3, 0, H, dense3[:, 0:H])
-        for c in range(2, PACK):
-            sigmoid(1, c, c)
+        quarter = dom_raw[1, 1].rearrange("p j c -> p (j c)")[:, 0:H]
+        half_product(4, 0, 1, 1, scalar_cast, quarter)
         quantise(grads[1], slice(0, DV), room.bitcast(BF16), E5M2)
 
         whole_product(6, 0, 2, vector_cast, dense2[:, 0:N])
@@ -297,25 +292,26 @@ def tile_attend_gat_sig_v_kernel(tc, qT, kT, rw, dom, offs, out):
         for c in range(2):
             weigh(1, c, nc.gpsimd)
         quantise_weights(1, 0)
-        half_product(0, 0, 1, 1, scalar_cast, probs[1][0][:, 0:H])
+        scalar_scatter(1, H, N, quarter)
+        whole_product(7, 0, 3, scalar_cast, dense3[:, 0:N])
         scalar_scatter(0, H, N, second[:, N - H : N])
-        scalar_scatter(1, H, N, probs[1][0][:, 0:H])
+        scalar_scatter(3, 0, H, dense3[:, 0:H])
         for c in range(2, PACK):
             weigh(1, c)
-        pair_of_products(4, 1, 0, vector_cast, probs[1][PACK - 1])
+        pair_of_products(0, 1, 0, vector_cast, probs[1][PACK - 1])
         quantise_weights(1, 1)
-        scalar_scatter(1, N, N + H, probs[1][PACK - 1][:, H:N])
+        scalar_scatter(0, N, N + H, probs[1][PACK - 1][:, 0:H])
 
-        vector_scatter(0, N, N + H, probs[1][PACK - 1][:, 0:H])
-        half_product(7, 1, 0, 1, vector_cast, first[:, 0:H])
+        vector_scatter(1, N, N + H, probs[1][PACK - 1][:, H:N])
+        half_product(5, 1, 1, 1, vector_cast, first[:, H:N])
         whole_product(1, 1, 2, vector_cast, dense2[:, N:SLOTS])
-        half_product(3, 1, 1, 1, scalar_cast, first[:, H:N])
+        half_product(3, 1, 0, 1, scalar_cast, first[:, 0:H])
         whole_product(2, 1, 3, scalar_cast, dense3[:, N:SLOTS])
-        vector_scatter(0, N + H, SLOTS, first[:, 0:H])
-        nc.sync.dma_start(out=out[block(0), :], in_=window[0][:])
+        vector_scatter(1, N + H, SLOTS, first[:, H:N])
+        nc.sync.dma_start(out=out[block(1), :], in_=window[1][:])
 
-        scalar_scatter(1, N + H, SLOTS, first[:, H:N])
-        nc.scalar.dma_start(out=out[block(1), :], in_=window[1][:])
+        scalar_scatter(0, N + H, SLOTS, first[:, 0:H])
+        nc.scalar.dma_start(out=out[block(0), :], in_=window[0][:])
 
         vector_scatter(2, EARLY, SLOTS, dense2[:, EARLY:SLOTS])
         nc.sync.dma_start(out=out[block(2), :], in_=window[2][:])

@@ -225,6 +225,11 @@ def tile_attend_gat_sig_v_kernel(tc, qT, kT, rw, dom, offs, out):
         def scalar_scatter(m, lo, hi, dense):
             nc.scalar.activation(out=listed(window[m], lo, hi), in_=dense, func=COPY)
 
+        def store(m, queues):
+            for h, queue in enumerate(queues):
+                cols = slice(h * T // 2, (h + 1) * T // 2)
+                queue.dma_start(out=out[block(m), cols], in_=window[m][:, cols])
+
         for h in range(2):
             gather(0, 1, h * H, (h + 1) * H)
         for h in range(2):
@@ -308,14 +313,14 @@ def tile_attend_gat_sig_v_kernel(tc, qT, kT, rw, dom, offs, out):
         half_product(3, 1, 0, 1, scalar_cast, first[:, 0:H])
         whole_product(2, 1, 3, scalar_cast, dense3[:, N:SLOTS])
         vector_scatter(1, N + H, SLOTS, first[:, H:N])
-        nc.sync.dma_start(out=out[block(1), :], in_=window[1][:])
+        store(1, (nc.sync, nc.sync))
 
         scalar_scatter(0, N + H, SLOTS, first[:, 0:H])
-        nc.scalar.dma_start(out=out[block(0), :], in_=window[0][:])
+        store(0, (nc.scalar, nc.scalar))
 
         vector_scatter(2, EARLY, SLOTS, dense2[:, EARLY:SLOTS])
-        nc.sync.dma_start(out=out[block(2), :], in_=window[2][:])
+        store(2, (nc.sync, nc.sync))
 
         for lo, hi in ((640, SLOTS), (H, 640)):
             scalar_scatter(3, lo, hi, dense3[:, lo:hi])
-        nc.sync.dma_start(out=out[block(3), :], in_=window[3][:])
+        store(3, (nc.sync, nc.scalar))

@@ -1,6 +1,7 @@
 from contextlib import ExitStack
 
 import concourse.mybir as mybir
+from concourse.masks import make_identity
 
 B, N, T, D, DV, R = 2, 512, 2048, 512, 512, 512
 FLOPS = 2 * B * R * N * D + 2 * B * DV * N * R
@@ -16,6 +17,7 @@ E5M2 = mybir.dt.float8_e5m2_x4
 COPY = mybir.ActivationFunctionType.Copy
 SIGMOID = mybir.ActivationFunctionType.Sigmoid
 MULT = mybir.AluOpType.mult
+ADD = mybir.AluOpType.add
 
 P = 128
 PACK = 4
@@ -26,7 +28,6 @@ SLOTS = B * N
 KEY_LOADS = (((1536, 704), (512, 128)), ((1024, 768), (768, 256), (256, 96)))
 GROUPS = H // PACK
 SCALAR_GROUPS = 28
-EARLY = 288
 
 
 def tile_attend_gat_sig_v_kernel(tc, qT, kT, rw, dom, offs, out):
@@ -62,9 +63,18 @@ def tile_attend_gat_sig_v_kernel(tc, qT, kT, rw, dom, offs, out):
         def listed(window, lo, hi):
             return window[:].indirect(offsets[:, lo // 16 : hi // 16])
 
-        gate = [tile("gate%d" % b, [P, 1, PACK], F32) for b in range(B)]
+        gates = tile("gates", [P, P], F32)
+        nc.gpsimd.memset(gates[:], 0.0)
         for b in range(B):
-            nc.scalar.dma_start(out=gate[b][:, 0, :], in_=rw[b].rearrange("(p t) o -> p (t o)", t=PACK))
+            nc.scalar.dma_start(out=gates[:, 8 * b : 8 * b + PACK], in_=rw[b].rearrange("(p t) o -> p (t o)", t=PACK))
+        identity = tile("identity", [P, P], F32)
+        make_identity(nc, identity[:])
+        turned = tile("turned", [P, P], F32)
+        once = bank(0)
+        nc.tensor.transpose(once[:, 0:P], gates[:], identity[:])
+        scalar_cast(turned[:], once[:, 0:P])
+        twice = bank(7)
+        nc.tensor.transpose(twice[:, 0:P], turned[:], identity[:])
 
         warm_in = tile("warm_in", [P, 1], F32)
         warm_out = tile("warm_out", [P, 1], F32)
@@ -137,28 +147,28 @@ def tile_attend_gat_sig_v_kernel(tc, qT, kT, rw, dom, offs, out):
         queries = [operand("query%d" % b, R) for b in range(B)]
         weights = [operand("weight%d" % b, N) for b in range(B)]
         grads = [operand("grad%d" % b, DV) for b in range(B)]
-        wide_room = tile("room", [P, 2 * SLOTS], F32)
-        room = wide_room[:, H : H + 2 * N]
-        second = wide_room[:, 0:N]
-        dense2 = wide_room[:, SLOTS:]
+        room = tile("room", [P, SLOTS], F32)[:]
+        dense2 = tile("dense2", [P, SLOTS], F32)
         probs = [[tile("prob%d_%d" % (b, c), [P, N], F32)[:] for c in range(PACK)] for b in range(B)]
-        probs[0][2] = room[:, 0:N]
-        probs[1][0] = dense3[:, 0:N]
+        probs[0][1] = room[:, 0:N]
+        probs[1][2] = dense3[:, 0:N]
+        probs[1][PACK - 1] = dense2[:, 0:N]
+        front = tile("front", [P, 6 * N], BF16)
         q_grouped = [
-            tile("q_grouped0", [P, PACK, P, PACK], BF16)[:],
+            front[:, 0 : 4 * N].rearrange("p (t m j) -> p t m j", t=PACK, j=PACK),
             room.bitcast(BF16).rearrange("p (t m j) -> p t m j", t=PACK, j=PACK),
         ]
         dom_grouped = {
-            (0, 0): tile("dom_grouped0", [P, 2 * N], BF16)[:],
-            (0, 1): probs[0][1].bitcast(BF16),
+            (0, 0): front[:, 4 * N : 6 * N],
+            (0, 1): front[:, 3 * N : 5 * N],
             (1, 0): room[:, 0:N].bitcast(BF16),
             (1, 1): room[:, N : 2 * N].bitcast(BF16),
         }
         pw = {
             (0, 0): lane[:, 3 * N : 5 * N],
             (0, 1): lane[:, 4 * N : 6 * N],
-            (1, 0): wide_room[:, N:SLOTS].bitcast(BF16),
-            (1, 1): probs[1][1].bitcast(BF16),
+            (1, 0): room[:, 0:N].bitcast(BF16),
+            (1, 1): room[:, N : 2 * N].bitcast(BF16),
         }
 
         def query_tile(b, t):
@@ -205,11 +215,11 @@ def tile_attend_gat_sig_v_kernel(tc, qT, kT, rw, dom, offs, out):
                 out=probs[b][c].rearrange("p (n t) -> p n t", t=PACK), in_=scores.rearrange("p t n -> p n t"), func=SIGMOID
             )
 
-        def weigh(b, c, engine=nc.vector):
+        def weigh(b, c, engine, held):
             engine.tensor_tensor(
                 out=chunk(pw[b, c // 2], c % 2).rearrange("p (n t) -> p n t", t=PACK),
                 in0=probs[b][c].rearrange("p (n t) -> p n t", t=PACK),
-                in1=gate[b][:].broadcast_to([P, P, PACK]),
+                in1=held[:, 8 * b : 8 * b + PACK].unsqueeze(1).broadcast_to([P, P, PACK]),
                 op=MULT,
             )
 
@@ -225,10 +235,8 @@ def tile_attend_gat_sig_v_kernel(tc, qT, kT, rw, dom, offs, out):
         def scalar_scatter(m, lo, hi, dense):
             nc.scalar.activation(out=listed(window[m], lo, hi), in_=dense, func=COPY)
 
-        def store(m, queues):
-            for h, queue in enumerate(queues):
-                cols = slice(h * T // 2, (h + 1) * T // 2)
-                queue.dma_start(out=out[block(m), cols], in_=window[m][:, cols])
+        def store(m, queue):
+            queue.dma_start(out=out[block(m), :], in_=window[m][:])
 
         for h in range(2):
             gather(0, 1, h * H, (h + 1) * H)
@@ -242,15 +250,23 @@ def tile_attend_gat_sig_v_kernel(tc, qT, kT, rw, dom, offs, out):
         for m in range(2):
             cast_grad(scalar_cast, 0, m)
         gather(1, 1, 0, N)
+        quantise_grads(0, 0)
+        for m in range(2):
+            nc.gpsimd.tensor_scalar(
+                out=chunk(dom_grouped[0, 1], m).rearrange("p (e j) -> p e j", j=PACK),
+                in0=dom_raw[0, 1][:, :, block(m)].rearrange("p j e -> p e j"),
+                scalar1=1.0,
+                scalar2=0.0,
+                op0=MULT,
+                op1=ADD,
+            )
 
         for c in range(PACK):
             sigmoid(0, c, c % 3)
         for c in range(2):
-            weigh(0, c)
-        quantise_grads(0, 0)
+            weigh(0, c, nc.vector, twice)
         quantise_weights(0, 0)
-        for m in range(2, BLOCKS):
-            cast_grad(scalar_cast, 0, m)
+        cast_queries(scalar_cast, 1, 0, 0, GROUPS)
 
         def pair_of_products(where, b, h, cast, dense):
             acc = bank(where)
@@ -268,59 +284,54 @@ def tile_attend_gat_sig_v_kernel(tc, qT, kT, rw, dom, offs, out):
             product(acc[:, 0:H], b, m, half(h))
             cast(dense, acc[:, 0:H])
 
+        def product_in_halves(where, m, dense):
+            acc = bank(where)
+            for h in range(2):
+                product(acc[:, half(h)], 1, m, half(h))
+            vector_cast(dense, acc[:])
+
         first = tile("first", [P, N], F32)
         pair_of_products(4, 0, 0, scalar_cast, first[:])
         for m in range(2):
             scalar_scatter(m, 0, H, first[:, half(m)])
 
         for c in range(2, PACK):
-            weigh(0, c)
+            weigh(0, c, nc.vector, twice)
         vector_cast(picked[1], pair_rows.rearrange("p u n -> p n u"))
         quantise_weights(0, 1)
         quantise_grads(0, 1)
-        for h in range(2):
-            cast_queries(vector_cast, 1, h, 0, GROUPS)
+        cast_queries(vector_cast, 1, 1, 0, GROUPS)
         quantise_keys(1, 0, N)
         quantise(queries[1], slice(0, R), q_grouped[1].rearrange("p t m j -> p (t m j)"), E4M3)
         for c in range(PACK):
             sigmoid(1, c, c)
         for m in range(BLOCKS):
             cast_grad(vector_cast, 1, m)
-        quarter = dom_raw[1, 1].rearrange("p j c -> p (j c)")[:, 0:H]
-        half_product(4, 0, 1, 1, scalar_cast, quarter)
         quantise(grads[1], slice(0, DV), room.bitcast(BF16), E5M2)
 
+        weigh(1, 0, nc.gpsimd, gates)
+        for c in range(1, PACK):
+            weigh(1, c, nc.vector, twice)
+        second = dom_raw[1, 0].rearrange("p j c -> p (j c)")[:, 0:N]
+        pair_of_products(5, 0, 1, vector_cast, second)
+        for h in range(2):
+            quantise_weights(1, h)
+        scalar_scatter(0, H, N, second[:, 0:H])
+        whole_product(0, 0, 3, scalar_cast, dense3[:, 0:N])
+        scalar_scatter(1, H, N, second[:, H:N])
+
         whole_product(6, 0, 2, vector_cast, dense2[:, 0:N])
-        half_product(5, 0, 0, 1, vector_cast, second[:, N - H : N])
-        vector_scatter(2, 0, EARLY, dense2[:, 0:EARLY])
-
-        for c in range(2):
-            weigh(1, c, nc.gpsimd)
-        quantise_weights(1, 0)
-        scalar_scatter(1, H, N, quarter)
-        whole_product(7, 0, 3, scalar_cast, dense3[:, 0:N])
-        scalar_scatter(0, H, N, second[:, N - H : N])
-        scalar_scatter(3, 0, H, dense3[:, 0:H])
-        for c in range(2, PACK):
-            weigh(1, c)
-        pair_of_products(0, 1, 0, vector_cast, probs[1][PACK - 1])
-        quantise_weights(1, 1)
-        scalar_scatter(0, N, N + H, probs[1][PACK - 1][:, 0:H])
-
-        vector_scatter(1, N, N + H, probs[1][PACK - 1][:, H:N])
-        half_product(5, 1, 1, 1, vector_cast, first[:, H:N])
-        whole_product(1, 1, 2, vector_cast, dense2[:, N:SLOTS])
-        half_product(3, 1, 0, 1, scalar_cast, first[:, 0:H])
-        whole_product(2, 1, 3, scalar_cast, dense3[:, N:SLOTS])
-        vector_scatter(1, N + H, SLOTS, first[:, H:N])
-        store(1, (nc.sync, nc.sync))
-
-        scalar_scatter(0, N + H, SLOTS, first[:, 0:H])
-        store(0, (nc.scalar, nc.scalar))
-
-        vector_scatter(2, EARLY, SLOTS, dense2[:, EARLY:SLOTS])
-        store(2, (nc.sync, nc.sync))
-
-        for lo, hi in ((640, SLOTS), (H, 640)):
+        product_in_halves(1, 0, probs[1][0])
+        product_in_halves(4, 2, dense2[:, N:SLOTS])
+        whole_product(2, 1, 1, scalar_cast, first[:])
+        whole_product(3, 1, 3, scalar_cast, dense3[:, N:SLOTS])
+        vector_scatter(0, N, SLOTS, probs[1][0])
+        store(0, nc.sync)
+        for h in range(2):
+            scalar_scatter(1, N + h * H, N + (h + 1) * H, first[:, half(h)])
+        store(1, nc.scalar)
+        vector_scatter(2, 0, SLOTS, dense2[:])
+        store(2, nc.sync)
+        for lo, hi in ((640, SLOTS), (H, 640), (0, H)):
             scalar_scatter(3, lo, hi, dense3[:, lo:hi])
-        store(3, (nc.sync, nc.scalar))
+        store(3, nc.sync)

@@ -24,10 +24,13 @@ PACK = 4
 H = N // 2
 BLOCKS = DV // P
 SLOTS = B * N
+GATE_STEP = 8
 
 KEY_LOADS = (((1536, 704), (512, 128)), ((1024, 768), (768, 256), (256, 96)))
 GROUPS = H // PACK
 SCALAR_GROUPS = 28
+SCALAR_COLS = 32
+LAST_PIECES = ((640, SLOTS), (H, 640), (0, H))
 
 
 def tile_attend_gat_sig_v_kernel(tc, qT, kT, rw, dom, offs, out):
@@ -60,21 +63,24 @@ def tile_attend_gat_sig_v_kernel(tc, qT, kT, rw, dom, offs, out):
 
         offsets = keep.tile([P, SLOTS // 16], U16, name="offsets")
 
-        def listed(window, lo, hi):
-            return window[:].indirect(offsets[:, lo // 16 : hi // 16])
+        def listed(indexed, lo, hi):
+            return indexed[:].indirect(offsets[:, lo // 16 : hi // 16])
 
         gates = tile("gates", [P, P], F32)
         nc.gpsimd.memset(gates[:], 0.0)
         for b in range(B):
-            nc.scalar.dma_start(out=gates[:, 8 * b : 8 * b + PACK], in_=rw[b].rearrange("(p t) o -> p (t o)", t=PACK))
+            loaded = tile("gate%d" % b, [P, PACK], F32)
+            nc.scalar.dma_start(out=loaded[:], in_=rw[b].rearrange("(p t) o -> p (t o)", t=PACK))
+            nc.gpsimd.tensor_copy(out=gates[:, GATE_STEP * b : GATE_STEP * b + PACK], in_=loaded[:])
+
         identity = tile("identity", [P, P], F32)
         make_identity(nc, identity[:])
         turned = tile("turned", [P, P], F32)
         once = bank(0)
         nc.tensor.transpose(once[:, 0:P], gates[:], identity[:])
         scalar_cast(turned[:], once[:, 0:P])
-        twice = bank(7)
-        nc.tensor.transpose(twice[:, 0:P], turned[:], identity[:])
+        psum_gates = bank(7)
+        nc.tensor.transpose(psum_gates[:, 0:P], turned[:], identity[:])
 
         warm_in = tile("warm_in", [P, 1], F32)
         warm_out = tile("warm_out", [P, 1], F32)
@@ -87,12 +93,12 @@ def tile_attend_gat_sig_v_kernel(tc, qT, kT, rw, dom, offs, out):
 
         key_rows = kT.rearrange("(p u e) t -> u p e t", u=2, e=2)
         key_pairs = [tile("key_pairs%d" % u, [P, T], U32) for u in range(2)]
-
-        lane = tile("lane", [P, 6 * N], BF16)
+        late = tile("late", [P, 4 * N], F32)
         picked = [
             tile("picked0", [P, N, 2], U32)[:],
-            lane[:, 0 : 4 * N].bitcast(U32).rearrange("p (n u) -> p n u", u=2),
+            late[:, 0 : 2 * N].bitcast(U32).rearrange("p (n u) -> p n u", u=2),
         ]
+
         shared = tile("shared", [P, 3, N], F32)
         pair_rows = shared[:, 0:2, :].rearrange("p u n -> p (u n)").bitcast(U32).rearrange("p (u n) -> p u n", u=2)
 
@@ -113,8 +119,7 @@ def tile_attend_gat_sig_v_kernel(tc, qT, kT, rw, dom, offs, out):
                     nc.sync.dma_start(offsets[:], offs)
                 by_token = raw[:].rearrange("p e t -> p t e")
                 scalar_cast(pairs[:, t0 : t0 + on_scalar, :], by_token[:, 0:on_scalar])
-                if on_scalar < width:
-                    vector_cast(pairs[:, t0 + on_scalar : t0 + width, :], by_token[:, on_scalar:width])
+                vector_cast(pairs[:, t0 + on_scalar : t0 + width, :], by_token[:, on_scalar:width])
                 t0 += width
             if u == 0:
                 window.append(placed.tile([P, T], F32, name="last_window", offset=0))
@@ -126,7 +131,6 @@ def tile_attend_gat_sig_v_kernel(tc, qT, kT, rw, dom, offs, out):
             nc.sync.dma_start(out=raw, in_=src.rearrange("(p j) c -> p j c", j=PACK)[:, :, half(h)])
             return raw
 
-        dense3 = tile("dense3", [P, SLOTS], F32)
         q_raw = {}
         dom_raw = {}
         for b in range(B):
@@ -147,29 +151,29 @@ def tile_attend_gat_sig_v_kernel(tc, qT, kT, rw, dom, offs, out):
         queries = [operand("query%d" % b, R) for b in range(B)]
         weights = [operand("weight%d" % b, N) for b in range(B)]
         grads = [operand("grad%d" % b, DV) for b in range(B)]
-        room = tile("room", [P, SLOTS], F32)[:]
-        dense2 = tile("dense2", [P, SLOTS], F32)
-        probs = [[tile("prob%d_%d" % (b, c), [P, N], F32)[:] for c in range(PACK)] for b in range(B)]
-        probs[0][1] = room[:, 0:N]
-        probs[1][2] = dense3[:, 0:N]
-        probs[1][PACK - 1] = dense2[:, 0:N]
+
         front = tile("front", [P, 6 * N], BF16)
+        lane = tile("lane", [P, 3 * N], BF16)
+        room = late[:, 2 * N : 4 * N]
+        dense2 = tile("dense2", [P, SLOTS], F32)
+        dense3 = tile("dense3", [P, SLOTS], F32)
+
+        probs = [
+            [
+                tile("prob0_0", [P, N], F32)[:],
+                late[:, 3 * H : 5 * H],
+                tile("prob0_2", [P, N], F32)[:],
+                tile("prob0_3", [P, N], F32)[:],
+            ],
+            [tile("prob1_0", [P, N], F32)[:], tile("prob1_1", [P, N], F32)[:], chunk(dense3, 0), chunk(dense2, 0)],
+        ]
         q_grouped = [
             front[:, 0 : 4 * N].rearrange("p (t m j) -> p t m j", t=PACK, j=PACK),
             room.bitcast(BF16).rearrange("p (t m j) -> p t m j", t=PACK, j=PACK),
         ]
-        dom_grouped = {
-            (0, 0): front[:, 4 * N : 6 * N],
-            (0, 1): front[:, 3 * N : 5 * N],
-            (1, 0): room[:, 0:N].bitcast(BF16),
-            (1, 1): room[:, N : 2 * N].bitcast(BF16),
-        }
-        pw = {
-            (0, 0): lane[:, 3 * N : 5 * N],
-            (0, 1): lane[:, 4 * N : 6 * N],
-            (1, 0): room[:, 0:N].bitcast(BF16),
-            (1, 1): room[:, N : 2 * N].bitcast(BF16),
-        }
+        room_halves = [chunk(room, h).bitcast(BF16) for h in range(2)]
+        dom_grouped = [[front[:, 4 * N : 6 * N], front[:, 3 * N : 5 * N]], room_halves]
+        pw = [[lane[:, 0 : 2 * N], lane[:, N : 3 * N]], room_halves]
 
         def query_tile(b, t):
             codes, scales = queries[b]
@@ -198,14 +202,26 @@ def tile_attend_gat_sig_v_kernel(tc, qT, kT, rw, dom, offs, out):
             dst = q_grouped[b].rearrange("p t m j -> p m j t")[:, GROUPS * h + lo : GROUPS * h + hi]
             cast(dst, q_raw[b, h].rearrange("p j (m t) -> p m j t", t=PACK)[:, lo:hi])
 
-        def cast_grad(cast, b, m):
-            cast(
-                chunk(dom_grouped[b, m // 2], m % 2).rearrange("p (c i j) -> p c j i", i=4, j=PACK),
-                dom_raw[b, m // 2][:, :, block(m % 2)].rearrange("p j (c i) -> p c j i", i=4),
+        def grad_columns(b, h, lo, hi):
+            return dom_grouped[b][h][:, PACK * lo : PACK * hi], dom_raw[b, h][:, :, lo:hi]
+
+        def cast_grad(cast, b, h, lo, hi):
+            dst, src = grad_columns(b, h, lo, hi)
+            cast(dst.rearrange("p (c i j) -> p c j i", i=4, j=PACK), src.rearrange("p j (c i) -> p c j i", i=4))
+
+        def gpsimd_cast_grad(b, h, lo, hi):
+            dst, src = grad_columns(b, h, lo, hi)
+            nc.gpsimd.tensor_scalar(
+                out=dst.rearrange("p (e j) -> p e j", j=PACK),
+                in0=src.rearrange("p j e -> p e j"),
+                scalar1=1.0,
+                scalar2=0.0,
+                op0=MULT,
+                op1=ADD,
             )
 
         def quantise_grads(b, h):
-            quantise(grads[b], half(h), dom_grouped[b, h], E5M2)
+            quantise(grads[b], half(h), dom_grouped[b][h], E5M2)
 
         def sigmoid(b, c, where):
             scores = bank(where)[:].rearrange("p (t n) -> p t n", t=PACK)
@@ -215,19 +231,25 @@ def tile_attend_gat_sig_v_kernel(tc, qT, kT, rw, dom, offs, out):
                 out=probs[b][c].rearrange("p (n t) -> p n t", t=PACK), in_=scores.rearrange("p t n -> p n t"), func=SIGMOID
             )
 
-        def weigh(b, c, engine, held):
+        def weigh(engine, held, b, c):
             engine.tensor_tensor(
-                out=chunk(pw[b, c // 2], c % 2).rearrange("p (n t) -> p n t", t=PACK),
+                out=chunk(pw[b][c // 2], c % 2).rearrange("p (n t) -> p n t", t=PACK),
                 in0=probs[b][c].rearrange("p (n t) -> p n t", t=PACK),
-                in1=held[:, 8 * b : 8 * b + PACK].unsqueeze(1).broadcast_to([P, P, PACK]),
+                in1=held[:, GATE_STEP * b : GATE_STEP * b + PACK].unsqueeze(1).broadcast_to([P, P, PACK]),
                 op=MULT,
             )
 
         def quantise_weights(b, h):
-            quantise(weights[b], half(h), pw[b, h], E4M3)
+            quantise(weights[b], half(h), pw[b][h], E4M3)
 
-        def product(acc, b, m, cols):
-            multiply(acc, grads[b], block(m), E5M2, weights[b], cols)
+        def copy_out(cast, dense, where, b, parts):
+            acc = bank(where)
+            lo = 0
+            for m, cols in parts:
+                hi = lo + cols.stop - cols.start
+                multiply(acc[:, lo:hi], grads[b], block(m), E5M2, weights[b], cols)
+                lo = hi
+            cast(dense, acc[:])
 
         def vector_scatter(m, lo, hi, dense):
             nc.vector.tensor_copy(listed(window[m], lo, hi), dense)
@@ -237,6 +259,8 @@ def tile_attend_gat_sig_v_kernel(tc, qT, kT, rw, dom, offs, out):
 
         def store(m, queue):
             queue.dma_start(out=out[block(m), :], in_=window[m][:])
+
+        every_slot = slice(0, N)
 
         for h in range(2):
             gather(0, 1, h * H, (h + 1) * H)
@@ -248,83 +272,55 @@ def tile_attend_gat_sig_v_kernel(tc, qT, kT, rw, dom, offs, out):
         for t in range(PACK):
             quantise(query_tile(0, t), block(0), q_grouped[0][:, t].rearrange("p m j -> p (m j)"), E4M3)
         for m in range(2):
-            cast_grad(scalar_cast, 0, m)
+            cast_grad(scalar_cast, 0, 0, m * P, (m + 1) * P)
         gather(1, 1, 0, N)
         quantise_grads(0, 0)
-        for m in range(2):
-            nc.gpsimd.tensor_scalar(
-                out=chunk(dom_grouped[0, 1], m).rearrange("p (e j) -> p e j", j=PACK),
-                in0=dom_raw[0, 1][:, :, block(m)].rearrange("p j e -> p e j"),
-                scalar1=1.0,
-                scalar2=0.0,
-                op0=MULT,
-                op1=ADD,
-            )
+        gpsimd_cast_grad(0, 1, SCALAR_COLS, P)
+        gpsimd_cast_grad(0, 1, P, H)
 
         for c in range(PACK):
             sigmoid(0, c, c % 3)
+        cast_grad(scalar_cast, 0, 1, 0, SCALAR_COLS)
         for c in range(2):
-            weigh(0, c, nc.vector, twice)
+            weigh(nc.vector, psum_gates, 0, c)
         quantise_weights(0, 0)
-        cast_queries(scalar_cast, 1, 0, 0, GROUPS)
-
-        def pair_of_products(where, b, h, cast, dense):
-            acc = bank(where)
-            for m in range(2):
-                product(acc[:, half(m)], b, m, half(h))
-            cast(dense, acc[:])
-
-        def whole_product(where, b, m, cast, dense):
-            acc = bank(where)
-            product(acc[:], b, m, slice(0, N))
-            cast(dense, acc[:])
-
-        def half_product(where, b, m, h, cast, dense):
-            acc = bank(where)
-            product(acc[:, 0:H], b, m, half(h))
-            cast(dense, acc[:, 0:H])
-
-        def product_in_halves(where, m, dense):
-            acc = bank(where)
-            for h in range(2):
-                product(acc[:, half(h)], 1, m, half(h))
-            vector_cast(dense, acc[:])
-
+        nc.scalar.copy(out=picked[1], in_=pair_rows.rearrange("p u n -> p n u"))
         first = tile("first", [P, N], F32)
-        pair_of_products(4, 0, 0, scalar_cast, first[:])
+        copy_out(scalar_cast, first[:], 4, 0, [(m, half(0)) for m in range(2)])
         for m in range(2):
             scalar_scatter(m, 0, H, first[:, half(m)])
 
         for c in range(2, PACK):
-            weigh(0, c, nc.vector, twice)
-        vector_cast(picked[1], pair_rows.rearrange("p u n -> p n u"))
-        quantise_weights(0, 1)
+            weigh(nc.vector, psum_gates, 0, c)
         quantise_grads(0, 1)
+        quantise_weights(0, 1)
+        for lo in (0, GROUPS // 2):
+            cast_queries(vector_cast, 1, 0, lo, lo + GROUPS // 2)
         cast_queries(vector_cast, 1, 1, 0, GROUPS)
         quantise_keys(1, 0, N)
-        quantise(queries[1], slice(0, R), q_grouped[1].rearrange("p t m j -> p (t m j)"), E4M3)
+        quantise(queries[1], slice(0, R), room.bitcast(BF16), E4M3)
         for c in range(PACK):
             sigmoid(1, c, c)
         for m in range(BLOCKS):
-            cast_grad(vector_cast, 1, m)
+            cast_grad(vector_cast, 1, m // 2, m % 2 * P, (m % 2 + 1) * P)
         quantise(grads[1], slice(0, DV), room.bitcast(BF16), E5M2)
 
-        weigh(1, 0, nc.gpsimd, gates)
+        weigh(nc.gpsimd, gates, 1, 0)
         for c in range(1, PACK):
-            weigh(1, c, nc.vector, twice)
+            weigh(nc.vector, psum_gates, 1, c)
         second = dom_raw[1, 0].rearrange("p j c -> p (j c)")[:, 0:N]
-        pair_of_products(5, 0, 1, vector_cast, second)
+        copy_out(vector_cast, second, 5, 0, [(m, half(1)) for m in range(2)])
         for h in range(2):
             quantise_weights(1, h)
-        scalar_scatter(0, H, N, second[:, 0:H])
-        whole_product(0, 0, 3, scalar_cast, dense3[:, 0:N])
-        scalar_scatter(1, H, N, second[:, H:N])
+        scalar_scatter(0, H, N, second[:, half(0)])
+        copy_out(scalar_cast, chunk(dense3, 0), 0, 0, [(3, every_slot)])
+        scalar_scatter(1, H, N, second[:, half(1)])
 
-        whole_product(6, 0, 2, vector_cast, dense2[:, 0:N])
-        product_in_halves(1, 0, probs[1][0])
-        product_in_halves(4, 2, dense2[:, N:SLOTS])
-        whole_product(2, 1, 1, scalar_cast, first[:])
-        whole_product(3, 1, 3, scalar_cast, dense3[:, N:SLOTS])
+        copy_out(vector_cast, chunk(dense2, 0), 6, 0, [(2, every_slot)])
+        copy_out(vector_cast, probs[1][0], 1, 1, [(0, half(h)) for h in range(2)])
+        copy_out(vector_cast, chunk(dense2, 1), 4, 1, [(2, half(h)) for h in range(2)])
+        copy_out(scalar_cast, first[:], 2, 1, [(1, every_slot)])
+        copy_out(scalar_cast, chunk(dense3, 1), 3, 1, [(3, every_slot)])
         vector_scatter(0, N, SLOTS, probs[1][0])
         store(0, nc.sync)
         for h in range(2):
@@ -332,6 +328,6 @@ def tile_attend_gat_sig_v_kernel(tc, qT, kT, rw, dom, offs, out):
         store(1, nc.scalar)
         vector_scatter(2, 0, SLOTS, dense2[:])
         store(2, nc.sync)
-        for lo, hi in ((640, SLOTS), (H, 640), (0, H)):
+        for lo, hi in LAST_PIECES:
             scalar_scatter(3, lo, hi, dense3[:, lo:hi])
         store(3, nc.sync)

@@ -28,7 +28,6 @@ GATE_STEP = 8
 
 KEY_LOADS = (((1536, 704), (512, 128)), ((1024, 768), (768, 256), (256, 96)))
 GROUPS = H // PACK
-SCALAR_GROUPS = 28
 SCALAR_COLS = 32
 LAST_PIECES = ((640, SLOTS), (H, 640), (0, H))
 
@@ -94,17 +93,22 @@ def tile_attend_gat_sig_v_kernel(tc, qT, kT, rw, dom, offs, out):
         key_rows = kT.rearrange("(p u e) t -> u p e t", u=2, e=2)
         key_pairs = [tile("key_pairs%d" % u, [P, T], U32) for u in range(2)]
         late = tile("late", [P, 4 * N], F32)
+        q_first = tile("q_first", [P, 2 * N], F32)
         picked = [
-            tile("picked0", [P, N, 2], U32)[:],
+            tile("picked0", [P, H, 2], U32)[:],
+            q_first[:, 0:N].bitcast(U32).rearrange("p (n u) -> p n u", u=2),
             late[:, 0 : 2 * N].bitcast(U32).rearrange("p (n u) -> p n u", u=2),
         ]
 
-        shared = tile("shared", [P, 3, N], F32)
-        pair_rows = shared[:, 0:2, :].rearrange("p u n -> p (u n)").bitcast(U32).rearrange("p (u n) -> p u n", u=2)
+        shared = tile("shared", [P, 4 * N], F32)
+        pair_rows = shared[:, 0 : 3 * N].bitcast(U32).rearrange("p (u n) -> p u n", u=2)
 
-        def gather(b, u, lo, hi):
-            dst = picked[0][:, lo:hi, u] if b == 0 else pair_rows[:, u, lo:hi]
-            nc.vector.tensor_copy(dst, listed(key_pairs[u], b * N + lo, b * N + hi))
+        def gather(u, lo, hi):
+            dst = picked[0][:, lo:hi, u] if lo < H else pair_rows[:, u, lo - H : hi - H]
+            nc.vector.tensor_copy(dst, listed(key_pairs[u], lo, hi))
+
+        def interleave(dst, lo, hi):
+            nc.scalar.copy(out=dst, in_=pair_rows[:, :, lo - H : hi - H].rearrange("p u n -> p n u"))
 
         for u in range(2):
             pairs = key_pairs[u][:].bitcast(BF16).rearrange("p (t e) -> p t e", e=2)
@@ -124,8 +128,8 @@ def tile_attend_gat_sig_v_kernel(tc, qT, kT, rw, dom, offs, out):
             if u == 0:
                 window.append(placed.tile([P, T], F32, name="last_window", offset=0))
                 nc.gpsimd.memset(window[BLOCKS - 1][:], 0.0)
-                for b in range(B):
-                    gather(b, 0, 0, N)
+                gather(0, 0, H)
+                gather(0, H, SLOTS)
 
         def load_half(raw, src, h):
             nc.sync.dma_start(out=raw, in_=src.rearrange("(p j) c -> p j c", j=PACK)[:, :, half(h)])
@@ -135,8 +139,8 @@ def tile_attend_gat_sig_v_kernel(tc, qT, kT, rw, dom, offs, out):
         dom_raw = {}
         for b in range(B):
             for h in range(2):
-                if (b, h) == (0, 1):
-                    raw = shared[:, 1:3, :].rearrange("p a (j c) -> p (a j) c", j=2)
+                if b == 0:
+                    raw = (q_first[:], shared[:, 2 * N : 4 * N])[h].rearrange("p (j c) -> p j c", j=PACK)
                 else:
                     raw = tile("q_raw%d_%d" % (b, h), [P, PACK, H], F32)[:]
                 q_raw[b, h] = load_half(raw, qT[b], h)
@@ -146,13 +150,14 @@ def tile_attend_gat_sig_v_kernel(tc, qT, kT, rw, dom, offs, out):
         def operand(name, words):
             return tile(name + "_codes", [P, words], U32), tile(name + "_scales", [P, words], U8)
 
-        planes = tile("planes", [P, N], U8)
-        keys = [(tile("key0_codes", [P, N], U32), planes[4:P, :]), operand("key1", N)]
+        planes = tile("planes", [P, 2 * N], U8)
+        keys = [(tile("key0_codes", [P, N], U32), planes[4:P, 0:N]), operand("key1", N)]
         queries = [operand("query%d" % b, R) for b in range(B)]
         weights = [operand("weight%d" % b, N) for b in range(B)]
-        grads = [operand("grad%d" % b, DV) for b in range(B)]
+        grads = [(tile("grad0_codes", [P, DV], U32), planes[:, N - 64 : 2 * N - 64]), operand("grad1", DV)]
 
-        front = tile("front", [P, 6 * N], BF16)
+        front32 = tile("front", [P, 7 * H], F32)
+        front = front32[:].bitcast(BF16)
         lane = tile("lane", [P, 3 * N], BF16)
         room = late[:, 2 * N : 4 * N]
         dense2 = tile("dense2", [P, SLOTS], F32)
@@ -160,25 +165,25 @@ def tile_attend_gat_sig_v_kernel(tc, qT, kT, rw, dom, offs, out):
 
         probs = [
             [
-                tile("prob0_0", [P, N], F32)[:],
+                front32[:, H + 32 : 3 * H + 32],
                 late[:, 3 * H : 5 * H],
                 tile("prob0_2", [P, N], F32)[:],
                 tile("prob0_3", [P, N], F32)[:],
             ],
-            [tile("prob1_0", [P, N], F32)[:], tile("prob1_1", [P, N], F32)[:], chunk(dense3, 0), chunk(dense2, 0)],
+            [tile("prob1_%d" % c, [P, N], F32)[:] for c in range(PACK - 1)] + [chunk(dense3, 0)],
         ]
         q_grouped = [
             front[:, 0 : 4 * N].rearrange("p (t m j) -> p t m j", t=PACK, j=PACK),
             room.bitcast(BF16).rearrange("p (t m j) -> p t m j", t=PACK, j=PACK),
         ]
-        room_halves = [chunk(room, h).bitcast(BF16) for h in range(2)]
-        dom_grouped = [[front[:, 4 * N : 6 * N], front[:, 3 * N : 5 * N]], room_halves]
-        pw = [[lane[:, 0 : 2 * N], lane[:, N : 3 * N]], room_halves]
+        back = tile("back", [P, 8 * N], BF16)
+        dom_grouped = [[front[:, 5 * N : 7 * N], front[:, 3 * N : 5 * N]], [back[:, 4 * N - 32 : 6 * N - 32], back[:, 6 * N - 32 : 8 * N - 32]]]
+        pw = [[lane[:, 0 : 2 * N], lane[:, N : 3 * N]], [back[:, 2 * N : 4 * N], back[:, 0 : 2 * N]]]
 
         def query_tile(b, t):
             codes, scales = queries[b]
             if (b, t) == (0, PACK - 1):
-                return codes[:, block(t)], planes[:, 3 * P // 2 : 5 * P // 2]
+                return codes[:, block(t)], planes[:, P : 2 * P]
             return codes[:, block(t)], scales[:, block(t)]
 
         def quantise(dst, cols, src, fmt):
@@ -195,8 +200,8 @@ def tile_attend_gat_sig_v_kernel(tc, qT, kT, rw, dom, offs, out):
                 stop=True,
             )
 
-        def quantise_keys(b, lo, hi):
-            quantise(keys[b], slice(lo, hi), picked[b][:, lo:hi, :].rearrange("p n u -> p (n u)").bitcast(BF16), E4M3)
+        def quantise_keys(b, cols, src):
+            quantise(keys[b], cols, src.rearrange("p n u -> p (n u)").bitcast(BF16), E4M3)
 
         def cast_queries(cast, b, h, lo, hi):
             dst = q_grouped[b].rearrange("p t m j -> p m j t")[:, GROUPS * h + lo : GROUPS * h + hi]
@@ -242,14 +247,16 @@ def tile_attend_gat_sig_v_kernel(tc, qT, kT, rw, dom, offs, out):
         def quantise_weights(b, h):
             quantise(weights[b], half(h), pw[b][h], E4M3)
 
-        def copy_out(cast, dense, where, b, parts):
+        def copy_out(cast, dense, where, b, parts, pieces=1):
             acc = bank(where)
             lo = 0
             for m, cols in parts:
                 hi = lo + cols.stop - cols.start
                 multiply(acc[:, lo:hi], grads[b], block(m), E5M2, weights[b], cols)
                 lo = hi
-            cast(dense, acc[:])
+            for i in range(pieces):
+                cols = slice(i * lo // pieces, (i + 1) * lo // pieces)
+                cast(dense[:, cols], acc[:, cols])
 
         def vector_scatter(m, lo, hi, dense):
             nc.vector.tensor_copy(listed(window[m], lo, hi), dense)
@@ -263,69 +270,70 @@ def tile_attend_gat_sig_v_kernel(tc, qT, kT, rw, dom, offs, out):
         every_slot = slice(0, N)
 
         for h in range(2):
-            gather(0, 1, h * H, (h + 1) * H)
-        for h in range(2):
-            quantise_keys(0, h * H, (h + 1) * H)
+            gather(1, h * H, (h + 1) * H)
+        quantise_keys(0, half(0), picked[0])
         cast_queries(scalar_cast, 0, 0, 0, GROUPS)
-        cast_queries(scalar_cast, 0, 1, 0, SCALAR_GROUPS)
-        cast_queries(vector_cast, 0, 1, SCALAR_GROUPS, GROUPS)
+        cast_queries(vector_cast, 0, 1, 0, GROUPS)
+        interleave(picked[1], H, N)
         for t in range(PACK):
             quantise(query_tile(0, t), block(0), q_grouped[0][:, t].rearrange("p m j -> p (m j)"), E4M3)
-        for m in range(2):
-            cast_grad(scalar_cast, 0, 0, m * P, (m + 1) * P)
-        gather(1, 1, 0, N)
-        quantise_grads(0, 0)
-        gpsimd_cast_grad(0, 1, SCALAR_COLS, P)
-        gpsimd_cast_grad(0, 1, P, H)
+        quantise_keys(0, half(1), picked[1])
+        cast_grad(scalar_cast, 0, 0, 0, H)
+        gather(1, N, SLOTS)
+        gpsimd_cast_grad(0, 1, SCALAR_COLS, H)
 
         for c in range(PACK):
             sigmoid(0, c, c % 3)
-        cast_grad(scalar_cast, 0, 1, 0, SCALAR_COLS)
         for c in range(2):
             weigh(nc.vector, psum_gates, 0, c)
+        cast_grad(scalar_cast, 0, 1, 0, SCALAR_COLS)
+        quantise_grads(0, 0)
         quantise_weights(0, 0)
-        nc.scalar.copy(out=picked[1], in_=pair_rows.rearrange("p u n -> p n u"))
+        interleave(picked[2], N, SLOTS)
         first = tile("first", [P, N], F32)
-        copy_out(scalar_cast, first[:], 4, 0, [(m, half(0)) for m in range(2)])
+        for m in range(2):
+            copy_out(scalar_cast, first[:, half(m)], 4 + 2 * m, 0, [(m, half(0))])
         for m in range(2):
             scalar_scatter(m, 0, H, first[:, half(m)])
 
-        for c in range(2, PACK):
-            weigh(nc.vector, psum_gates, 0, c)
+        for h in range(2):
+            cast_queries(vector_cast, 1, h, 0, GROUPS)
         quantise_grads(0, 1)
-        quantise_weights(0, 1)
-        for lo in (0, GROUPS // 2):
-            cast_queries(vector_cast, 1, 0, lo, lo + GROUPS // 2)
-        cast_queries(vector_cast, 1, 1, 0, GROUPS)
-        quantise_keys(1, 0, N)
         quantise(queries[1], slice(0, R), room.bitcast(BF16), E4M3)
+        quantise_keys(1, every_slot, picked[2])
+        for h in range(2):
+            weigh(nc.vector, psum_gates, 0, 2 + h)
+            cast_grad(vector_cast, 1, h, 0, H)
         for c in range(PACK):
             sigmoid(1, c, c)
-        for m in range(BLOCKS):
-            cast_grad(vector_cast, 1, m // 2, m % 2 * P, (m % 2 + 1) * P)
-        quantise(grads[1], slice(0, DV), room.bitcast(BF16), E5M2)
+        quantise_weights(0, 1)
+        quantise(grads[1], slice(0, DV), back[:, 4 * N - 32 : 8 * N - 32], E5M2)
 
-        weigh(nc.gpsimd, gates, 1, 0)
-        for c in range(1, PACK):
+        weigh(nc.vector, psum_gates, 1, 0)
+        weigh(nc.gpsimd, gates, 1, 1)
+        copy_out(vector_cast, chunk(dense2, 0), 5, 0, [(2, every_slot)])
+        for c in range(2, PACK):
             weigh(nc.vector, psum_gates, 1, c)
-        second = dom_raw[1, 0].rearrange("p j c -> p (j c)")[:, 0:N]
-        copy_out(vector_cast, second, 5, 0, [(m, half(1)) for m in range(2)])
+        second = tile("second", [P, N], F32)
+        copy_out(scalar_cast, second[:], 1, 0, [(m, half(1)) for m in range(2)], 2)
         for h in range(2):
             quantise_weights(1, h)
-        scalar_scatter(0, H, N, second[:, half(0)])
-        copy_out(scalar_cast, chunk(dense3, 0), 0, 0, [(3, every_slot)])
-        scalar_scatter(1, H, N, second[:, half(1)])
+        for m in range(2):
+            scalar_scatter(m, H, N, second[:, half(m)])
 
-        copy_out(vector_cast, chunk(dense2, 0), 6, 0, [(2, every_slot)])
-        copy_out(vector_cast, probs[1][0], 1, 1, [(0, half(h)) for h in range(2)])
-        copy_out(vector_cast, chunk(dense2, 1), 4, 1, [(2, half(h)) for h in range(2)])
+        copy_out(vector_cast, chunk(dense3, 0), 0, 0, [(3, every_slot)])
+        copy_out(vector_cast, probs[1][0][:, half(0)], 6, 1, [(0, half(0))])
+        copy_out(vector_cast, chunk(dense2, 1)[:, half(0)], 5, 1, [(2, half(0))])
+        copy_out(vector_cast, probs[1][0][:, half(1)], 4, 1, [(0, half(1))])
         copy_out(scalar_cast, first[:], 2, 1, [(1, every_slot)])
         copy_out(scalar_cast, chunk(dense3, 1), 3, 1, [(3, every_slot)])
-        vector_scatter(0, N, SLOTS, probs[1][0])
+        copy_out(scalar_cast, chunk(dense2, 1)[:, half(1)], 1, 1, [(2, half(1))])
+        for h in range(2):
+            vector_scatter(0, N + h * H, N + (h + 1) * H, probs[1][0][:, half(h)])
         store(0, nc.sync)
         for h in range(2):
             scalar_scatter(1, N + h * H, N + (h + 1) * H, first[:, half(h)])
-        store(1, nc.scalar)
+        store(1, nc.sync)
         vector_scatter(2, 0, SLOTS, dense2[:])
         store(2, nc.sync)
         for lo, hi in LAST_PIECES:

@@ -24,11 +24,12 @@ PACK = 4
 H = N // 2
 BLOCKS = DV // P
 SLOTS = B * N
-GATE_STEP = 8
 
 KEY_LOADS = (((1536, 704), (512, 128)), ((1024, 768), (768, 256), (256, 96)))
 GROUPS = H // PACK
-SCALAR_COLS = 32
+EARLY_COLS = 240
+GPSIMD_COLS = 192
+FIRST_GROUPS = 48
 LAST_PIECES = ((640, SLOTS), (H, 640), (0, H))
 
 
@@ -65,25 +66,20 @@ def tile_attend_gat_sig_v_kernel(tc, qT, kT, rw, dom, offs, out):
         def listed(indexed, lo, hi):
             return indexed[:].indirect(offsets[:, lo // 16 : hi // 16])
 
-        gates = tile("gates", [P, P], F32)
-        nc.gpsimd.memset(gates[:], 0.0)
-        for b in range(B):
-            loaded = tile("gate%d" % b, [P, PACK], F32)
-            nc.scalar.dma_start(out=loaded[:], in_=rw[b].rearrange("(p t) o -> p (t o)", t=PACK))
-            nc.gpsimd.tensor_copy(out=gates[:, GATE_STEP * b : GATE_STEP * b + PACK], in_=loaded[:])
-
+        gate_rows = tile("gate_rows", [P, R], F32)
+        loaded = tile("loaded", [B, R], F32)
+        nc.scalar.dma_start(out=loaded[:], in_=rw.rearrange("b r o -> b (r o)"))
+        nc.gpsimd.memset(gate_rows[:], 0.0)
+        nc.gpsimd.tensor_scalar(out=gate_rows[0:B, :], in0=loaded[:], scalar1=1.0, scalar2=0.0, op0=MULT, op1=ADD)
         identity = tile("identity", [P, P], F32)
         make_identity(nc, identity[:])
-        turned = tile("turned", [P, P], F32)
-        once = bank(0)
-        nc.tensor.transpose(once[:, 0:P], gates[:], identity[:])
-        scalar_cast(turned[:], once[:, 0:P])
         psum_gates = bank(7)
-        nc.tensor.transpose(psum_gates[:, 0:P], turned[:], identity[:])
+        for t in range(PACK):
+            nc.tensor.transpose(psum_gates[:, B * t : B * t + P], gate_rows[:, t:R:PACK], identity[:])
 
         warm_in = tile("warm_in", [P, 1], F32)
         warm_out = tile("warm_out", [P, 1], F32)
-        nc.gpsimd.memset(warm_in[:], 0.0)
+        nc.vector.memset(warm_in[:], 0.0)
         nc.scalar.activation(out=warm_out[:], in_=warm_in[:], func=SIGMOID)
 
         window = [tile("window%d" % m, [P, T], F32) for m in range(BLOCKS - 1)]
@@ -93,7 +89,7 @@ def tile_attend_gat_sig_v_kernel(tc, qT, kT, rw, dom, offs, out):
         key_rows = kT.rearrange("(p u e) t -> u p e t", u=2, e=2)
         key_pairs = [tile("key_pairs%d" % u, [P, T], U32) for u in range(2)]
         late = tile("late", [P, 4 * N], F32)
-        q_first = tile("q_first", [P, 2 * N], F32)
+        q_first = tile("q_first", [P, 3 * N], F32)
         picked = [
             tile("picked0", [P, H, 2], U32)[:],
             q_first[:, 0:N].bitcast(U32).rearrange("p (n u) -> p n u", u=2),
@@ -140,12 +136,15 @@ def tile_attend_gat_sig_v_kernel(tc, qT, kT, rw, dom, offs, out):
         for b in range(B):
             for h in range(2):
                 if b == 0:
-                    raw = (q_first[:], shared[:, 2 * N : 4 * N])[h].rearrange("p (j c) -> p j c", j=PACK)
+                    raw = (q_first[:, N - 64 : 3 * N - 64], shared[:, 2 * N : 4 * N])[h].rearrange("p (j c) -> p j c", j=PACK)
                 else:
                     raw = tile("q_raw%d_%d" % (b, h), [P, PACK, H], F32)[:]
                 q_raw[b, h] = load_half(raw, qT[b], h)
+            cuts = (0, EARLY_COLS if b == 0 else H, DV)
             for h in range(2):
-                dom_raw[b, h] = load_half(tile("dom_raw%d_%d" % (b, h), [P, PACK, H], F32)[:], dom[b], h)
+                dom_raw[b, h] = tile("dom_raw%d_%d" % (b, h), [P, PACK, cuts[h + 1] - cuts[h]], F32)[:]
+                rows = dom[b].rearrange("(p j) c -> p j c", j=PACK)
+                nc.sync.dma_start(out=dom_raw[b, h], in_=rows[:, :, cuts[h] : cuts[h + 1]])
 
         def operand(name, words):
             return tile(name + "_codes", [P, words], U32), tile(name + "_scales", [P, words], U8)
@@ -165,7 +164,7 @@ def tile_attend_gat_sig_v_kernel(tc, qT, kT, rw, dom, offs, out):
 
         probs = [
             [
-                front32[:, H + 32 : 3 * H + 32],
+                front32[:, 2 * N - 32 : 3 * N - 32],
                 late[:, 3 * H : 5 * H],
                 tile("prob0_2", [P, N], F32)[:],
                 tile("prob0_3", [P, N], F32)[:],
@@ -173,16 +172,16 @@ def tile_attend_gat_sig_v_kernel(tc, qT, kT, rw, dom, offs, out):
             [tile("prob1_%d" % c, [P, N], F32)[:] for c in range(PACK - 1)] + [chunk(dense3, 0)],
         ]
         q_grouped = [
-            front[:, 0 : 4 * N].rearrange("p (t m j) -> p t m j", t=PACK, j=PACK),
+            front[:, 9 * P : 9 * P + 4 * N].rearrange("p (t m j) -> p t m j", t=PACK, j=PACK),
             room.bitcast(BF16).rearrange("p (t m j) -> p t m j", t=PACK, j=PACK),
         ]
         back = tile("back", [P, 8 * N], BF16)
-        dom_grouped = [[front[:, 5 * N : 7 * N], front[:, 3 * N : 5 * N]], [back[:, 4 * N - 32 : 6 * N - 32], back[:, 6 * N - 32 : 8 * N - 32]]]
+        dom_grouped = [[front[:, 0 : 4 * N], front[:, PACK * EARLY_COLS : 4 * N]], [back[:, 4 * N - 32 : 6 * N - 32], back[:, 6 * N - 32 : 8 * N - 32]]]
         pw = [[lane[:, 0 : 2 * N], lane[:, N : 3 * N]], [back[:, 2 * N : 4 * N], back[:, 0 : 2 * N]]]
 
         def query_tile(b, t):
             codes, scales = queries[b]
-            if (b, t) == (0, PACK - 1):
+            if (b, t) == (0, 0):
                 return codes[:, block(t)], planes[:, P : 2 * P]
             return codes[:, block(t)], scales[:, block(t)]
 
@@ -203,9 +202,9 @@ def tile_attend_gat_sig_v_kernel(tc, qT, kT, rw, dom, offs, out):
         def quantise_keys(b, cols, src):
             quantise(keys[b], cols, src.rearrange("p n u -> p (n u)").bitcast(BF16), E4M3)
 
-        def cast_queries(cast, b, h, lo, hi):
-            dst = q_grouped[b].rearrange("p t m j -> p m j t")[:, GROUPS * h + lo : GROUPS * h + hi]
-            cast(dst, q_raw[b, h].rearrange("p j (m t) -> p m j t", t=PACK)[:, lo:hi])
+        def cast_queries(cast, b, h, lo, hi, tiles=slice(0, PACK)):
+            dst = q_grouped[b].rearrange("p t m j -> p m j t")[:, GROUPS * h + lo : GROUPS * h + hi, :, tiles]
+            cast(dst, q_raw[b, h].rearrange("p j (m t) -> p m j t", t=PACK)[:, lo:hi, :, tiles])
 
         def grad_columns(b, h, lo, hi):
             return dom_grouped[b][h][:, PACK * lo : PACK * hi], dom_raw[b, h][:, :, lo:hi]
@@ -226,11 +225,11 @@ def tile_attend_gat_sig_v_kernel(tc, qT, kT, rw, dom, offs, out):
             )
 
         def quantise_grads(b, h):
-            quantise(grads[b], half(h), dom_grouped[b][h], E5M2)
+            quantise(grads[b], half(h), dom_grouped[b][0][:, 2 * N * h : 2 * N * (h + 1)], E5M2)
 
         def sigmoid(b, c, where):
             scores = bank(where)[:].rearrange("p (t n) -> p t n", t=PACK)
-            for t in range(PACK):
+            for t in reversed(range(PACK)):
                 multiply(scores[:, t, :], query_tile(b, t), block(0), E4M3, keys[b], block(c))
             nc.scalar.activation(
                 out=probs[b][c].rearrange("p (n t) -> p n t", t=PACK), in_=scores.rearrange("p t n -> p n t"), func=SIGMOID
@@ -240,7 +239,7 @@ def tile_attend_gat_sig_v_kernel(tc, qT, kT, rw, dom, offs, out):
             engine.tensor_tensor(
                 out=chunk(pw[b][c // 2], c % 2).rearrange("p (n t) -> p n t", t=PACK),
                 in0=probs[b][c].rearrange("p (n t) -> p n t", t=PACK),
-                in1=held[:, GATE_STEP * b : GATE_STEP * b + PACK].unsqueeze(1).broadcast_to([P, P, PACK]),
+                in1=held[:, b : B * PACK : B].unsqueeze(1).broadcast_to([P, P, PACK]),
                 op=MULT,
             )
 
@@ -272,21 +271,25 @@ def tile_attend_gat_sig_v_kernel(tc, qT, kT, rw, dom, offs, out):
         for h in range(2):
             gather(1, h * H, (h + 1) * H)
         quantise_keys(0, half(0), picked[0])
-        cast_queries(scalar_cast, 0, 0, 0, GROUPS)
-        cast_queries(vector_cast, 0, 1, 0, GROUPS)
+        cast_queries(scalar_cast, 0, 0, 0, FIRST_GROUPS)
+        cast_queries(scalar_cast, 0, 0, FIRST_GROUPS, GROUPS)
+        cast_queries(vector_cast, 0, 1, 0, GROUPS, slice(2, PACK))
+        cast_queries(vector_cast, 0, 1, 0, GROUPS, slice(0, 2))
         interleave(picked[1], H, N)
-        for t in range(PACK):
+        gates = q_first[:, N : N + B * PACK]
+        scalar_cast(gates, psum_gates[:, 0 : B * PACK])
+        for t in reversed(range(PACK)):
             quantise(query_tile(0, t), block(0), q_grouped[0][:, t].rearrange("p m j -> p (m j)"), E4M3)
         quantise_keys(0, half(1), picked[1])
-        cast_grad(scalar_cast, 0, 0, 0, H)
+        cast_grad(scalar_cast, 0, 0, 0, EARLY_COLS)
         gather(1, N, SLOTS)
-        gpsimd_cast_grad(0, 1, SCALAR_COLS, H)
+        gpsimd_cast_grad(0, 1, 0, GPSIMD_COLS)
 
         for c in range(PACK):
             sigmoid(0, c, c % 3)
         for c in range(2):
             weigh(nc.vector, psum_gates, 0, c)
-        cast_grad(scalar_cast, 0, 1, 0, SCALAR_COLS)
+        cast_grad(scalar_cast, 0, 1, GPSIMD_COLS, DV - EARLY_COLS)
         quantise_grads(0, 0)
         quantise_weights(0, 0)
         interleave(picked[2], N, SLOTS)

@@ -28,7 +28,7 @@ SLOTS = B * N
 KEY_LOADS = (((1536, 704), (512, 128)), ((1024, 768), (768, 256), (256, 96)))
 GROUPS = H // PACK
 EARLY_COLS = 240
-GPSIMD_COLS = 192
+GPSIMD_COLS = 208
 FIRST_GROUPS = 48
 LAST_PIECES = ((640, SLOTS), (H, 640), (0, H))
 
@@ -88,11 +88,12 @@ def tile_attend_gat_sig_v_kernel(tc, qT, kT, rw, dom, offs, out):
 
         key_rows = kT.rearrange("(p u e) t -> u p e t", u=2, e=2)
         key_pairs = [tile("key_pairs%d" % u, [P, T], U32) for u in range(2)]
-        late = tile("late", [P, 4 * N], F32)
-        q_first = tile("q_first", [P, 3 * N], F32)
+        late = tile("late", [P, 3 * N], F32)
+        front32 = tile("front", [P, 4 * N], F32)
+        woven = 2 * EARLY_COLS
         picked = [
             tile("picked0", [P, H, 2], U32)[:],
-            q_first[:, 0:N].bitcast(U32).rearrange("p (n u) -> p n u", u=2),
+            front32[:, woven : woven + N].bitcast(U32).rearrange("p (n u) -> p n u", u=2),
             late[:, 0 : 2 * N].bitcast(U32).rearrange("p (n u) -> p n u", u=2),
         ]
 
@@ -136,7 +137,7 @@ def tile_attend_gat_sig_v_kernel(tc, qT, kT, rw, dom, offs, out):
         for b in range(B):
             for h in range(2):
                 if b == 0:
-                    raw = (q_first[:, N - 64 : 3 * N - 64], shared[:, 2 * N : 4 * N])[h].rearrange("p (j c) -> p j c", j=PACK)
+                    raw = (front32[:, woven + N - 64 : woven + 3 * N - 64], shared[:, 2 * N : 4 * N])[h].rearrange("p (j c) -> p j c", j=PACK)
                 else:
                     raw = tile("q_raw%d_%d" % (b, h), [P, PACK, H], F32)[:]
                 q_raw[b, h] = load_half(raw, qT[b], h)
@@ -155,29 +156,28 @@ def tile_attend_gat_sig_v_kernel(tc, qT, kT, rw, dom, offs, out):
         weights = [operand("weight%d" % b, N) for b in range(B)]
         grads = [(tile("grad0_codes", [P, DV], U32), planes[:, N - 64 : 2 * N - 64]), operand("grad1", DV)]
 
-        front32 = tile("front", [P, 7 * H], F32)
         front = front32[:].bitcast(BF16)
-        lane = tile("lane", [P, 3 * N], BF16)
-        room = late[:, 2 * N : 4 * N]
+        lane = tile("lane", [P, 6 * N], BF16)
+        room = lane[:, 2 * N - 32 : 6 * N - 32]
         dense2 = tile("dense2", [P, SLOTS], F32)
         dense3 = tile("dense3", [P, SLOTS], F32)
 
         probs = [
             [
                 front32[:, 2 * N - 32 : 3 * N - 32],
-                late[:, 3 * H : 5 * H],
+                late[:, 2 * N - 32 : 3 * N - 32],
                 tile("prob0_2", [P, N], F32)[:],
                 tile("prob0_3", [P, N], F32)[:],
             ],
             [tile("prob1_%d" % c, [P, N], F32)[:] for c in range(PACK - 1)] + [chunk(dense3, 0)],
         ]
         q_grouped = [
-            front[:, 9 * P : 9 * P + 4 * N].rearrange("p (t m j) -> p t m j", t=PACK, j=PACK),
-            room.bitcast(BF16).rearrange("p (t m j) -> p t m j", t=PACK, j=PACK),
+            tile("q_grouped0", [P, 4 * N], BF16)[:].rearrange("p (t m j) -> p t m j", t=PACK, j=PACK),
+            room.rearrange("p (t m j) -> p t m j", t=PACK, j=PACK),
         ]
         back = tile("back", [P, 8 * N], BF16)
         dom_grouped = [[front[:, 0 : 4 * N], front[:, PACK * EARLY_COLS : 4 * N]], [back[:, 4 * N - 32 : 6 * N - 32], back[:, 6 * N - 32 : 8 * N - 32]]]
-        pw = [[lane[:, 0 : 2 * N], lane[:, N : 3 * N]], [back[:, 2 * N : 4 * N], back[:, 0 : 2 * N]]]
+        pw = [[lane[:, 0 : 2 * N], lane[:, 0 : 2 * N]], [back[:, 2 * N : 4 * N], back[:, 0 : 2 * N]]]
 
         def query_tile(b, t):
             codes, scales = queries[b]
@@ -276,7 +276,7 @@ def tile_attend_gat_sig_v_kernel(tc, qT, kT, rw, dom, offs, out):
         cast_queries(vector_cast, 0, 1, 0, GROUPS, slice(2, PACK))
         cast_queries(vector_cast, 0, 1, 0, GROUPS, slice(0, 2))
         interleave(picked[1], H, N)
-        gates = q_first[:, N : N + B * PACK]
+        gates = front32[:, 3 * N : 3 * N + B * PACK]
         scalar_cast(gates, psum_gates[:, 0 : B * PACK])
         for t in reversed(range(PACK)):
             quantise(query_tile(0, t), block(0), q_grouped[0][:, t].rearrange("p m j -> p (m j)"), E4M3)
@@ -302,7 +302,7 @@ def tile_attend_gat_sig_v_kernel(tc, qT, kT, rw, dom, offs, out):
         for h in range(2):
             cast_queries(vector_cast, 1, h, 0, GROUPS)
         quantise_grads(0, 1)
-        quantise(queries[1], slice(0, R), room.bitcast(BF16), E4M3)
+        quantise(queries[1], slice(0, R), room, E4M3)
         quantise_keys(1, every_slot, picked[2])
         for h in range(2):
             weigh(nc.vector, psum_gates, 0, 2 + h)

@@ -27,7 +27,7 @@ SLOTS = B * N
 
 KEY_LOADS = (((1536, 704), (512, 128)), ((1024, 768), (768, 256), (256, 96)))
 GROUPS = H // PACK
-EARLY_COLS = 240
+EARLY_COLS = 224
 GPSIMD_COLS = 208
 FIRST_GROUPS = 48
 LAST_PIECES = ((640, SLOTS), (H, 640), (0, H))
@@ -88,8 +88,8 @@ def tile_attend_gat_sig_v_kernel(tc, qT, kT, rw, dom, offs, out):
 
         key_rows = kT.rearrange("(p u e) t -> u p e t", u=2, e=2)
         key_pairs = [tile("key_pairs%d" % u, [P, T], U32) for u in range(2)]
-        late = tile("late", [P, 3 * N], F32)
-        front32 = tile("front", [P, 4 * N], F32)
+        front32 = tile("front", [P, 5 * N], F32)
+        late = front32[:, 2 * N - 16 : 5 * N - 16]
         woven = 2 * EARLY_COLS
         picked = [
             tile("picked0", [P, H, 2], U32)[:],
@@ -164,7 +164,7 @@ def tile_attend_gat_sig_v_kernel(tc, qT, kT, rw, dom, offs, out):
 
         probs = [
             [
-                front32[:, 2 * N - 32 : 3 * N - 32],
+                tile("prob0_0", [P, N], F32)[:],
                 late[:, 2 * N - 32 : 3 * N - 32],
                 tile("prob0_2", [P, N], F32)[:],
                 tile("prob0_3", [P, N], F32)[:],
@@ -176,8 +176,8 @@ def tile_attend_gat_sig_v_kernel(tc, qT, kT, rw, dom, offs, out):
             room.rearrange("p (t m j) -> p t m j", t=PACK, j=PACK),
         ]
         back = tile("back", [P, 8 * N], BF16)
-        dom_grouped = [[front[:, 0 : 4 * N], front[:, PACK * EARLY_COLS : 4 * N]], [back[:, 4 * N - 32 : 6 * N - 32], back[:, 6 * N - 32 : 8 * N - 32]]]
-        pw = [[lane[:, 0 : 2 * N], lane[:, 0 : 2 * N]], [back[:, 2 * N : 4 * N], back[:, 0 : 2 * N]]]
+        dom_grouped = [[front[:, 0 : 4 * N], front[:, PACK * EARLY_COLS : 4 * N]], [back[:, 0 : 2 * N], back[:, 2 * N : 4 * N]]]
+        pw = [[lane[:, 0 : 2 * N], lane[:, 0 : 2 * N]], [back[:, 4 * N - 32 : 6 * N - 32], back[:, 6 * N - 32 : 8 * N - 32]]]
 
         def query_tile(b, t):
             codes, scales = queries[b]
@@ -246,16 +246,14 @@ def tile_attend_gat_sig_v_kernel(tc, qT, kT, rw, dom, offs, out):
         def quantise_weights(b, h):
             quantise(weights[b], half(h), pw[b][h], E4M3)
 
-        def copy_out(cast, dense, where, b, parts, pieces=1):
+        def copy_out(cast, dense, where, b, parts):
             acc = bank(where)
             lo = 0
             for m, cols in parts:
                 hi = lo + cols.stop - cols.start
                 multiply(acc[:, lo:hi], grads[b], block(m), E5M2, weights[b], cols)
                 lo = hi
-            for i in range(pieces):
-                cols = slice(i * lo // pieces, (i + 1) * lo // pieces)
-                cast(dense[:, cols], acc[:, cols])
+            cast(dense, acc[:, 0:lo])
 
         def vector_scatter(m, lo, hi, dense):
             nc.vector.tensor_copy(listed(window[m], lo, hi), dense)
@@ -276,7 +274,7 @@ def tile_attend_gat_sig_v_kernel(tc, qT, kT, rw, dom, offs, out):
         cast_queries(vector_cast, 0, 1, 0, GROUPS, slice(2, PACK))
         cast_queries(vector_cast, 0, 1, 0, GROUPS, slice(0, 2))
         interleave(picked[1], H, N)
-        gates = front32[:, 3 * N : 3 * N + B * PACK]
+        gates = shared[:, 3 * N : 3 * N + B * PACK]
         scalar_cast(gates, psum_gates[:, 0 : B * PACK])
         for t in reversed(range(PACK)):
             quantise(query_tile(0, t), block(0), q_grouped[0][:, t].rearrange("p m j -> p (m j)"), E4M3)
@@ -289,7 +287,6 @@ def tile_attend_gat_sig_v_kernel(tc, qT, kT, rw, dom, offs, out):
             sigmoid(0, c, c % 3)
         for c in range(2):
             weigh(nc.vector, psum_gates, 0, c)
-        cast_grad(scalar_cast, 0, 1, GPSIMD_COLS, DV - EARLY_COLS)
         quantise_grads(0, 0)
         quantise_weights(0, 0)
         interleave(picked[2], N, SLOTS)
@@ -301,38 +298,39 @@ def tile_attend_gat_sig_v_kernel(tc, qT, kT, rw, dom, offs, out):
 
         for h in range(2):
             cast_queries(vector_cast, 1, h, 0, GROUPS)
-        quantise_grads(0, 1)
-        quantise(queries[1], slice(0, R), room, E4M3)
         quantise_keys(1, every_slot, picked[2])
-        for h in range(2):
-            weigh(nc.vector, psum_gates, 0, 2 + h)
-            cast_grad(vector_cast, 1, h, 0, H)
+        quantise(queries[1], slice(0, R), room, E4M3)
+        gpsimd_cast_grad(0, 1, GPSIMD_COLS, DV - EARLY_COLS)
+        for c in range(2, PACK):
+            weigh(nc.vector, psum_gates, 0, c)
         for c in range(PACK):
             sigmoid(1, c, c)
+        cast_grad(vector_cast, 1, 0, 0, H)
         quantise_weights(0, 1)
-        quantise(grads[1], slice(0, DV), back[:, 4 * N - 32 : 8 * N - 32], E5M2)
+        cast_grad(vector_cast, 1, 1, 0, H)
+        quantise_grads(0, 1)
+        quantise(grads[1], slice(0, DV), back[:, 0 : 4 * N], E5M2)
 
-        weigh(nc.vector, psum_gates, 1, 0)
-        weigh(nc.gpsimd, gates, 1, 1)
-        copy_out(vector_cast, chunk(dense2, 0), 5, 0, [(2, every_slot)])
-        for c in range(2, PACK):
-            weigh(nc.vector, psum_gates, 1, c)
+        weigh(nc.gpsimd, gates, 1, 0)
         second = tile("second", [P, N], F32)
-        copy_out(scalar_cast, second[:], 1, 0, [(m, half(1)) for m in range(2)], 2)
+        copy_out(vector_cast, second[:], 5, 0, [(m, half(1)) for m in range(2)])
+        for c in range(1, PACK):
+            weigh(nc.vector, psum_gates, 1, c)
+        copy_out(scalar_cast, chunk(dense2, 0), 1, 0, [(2, every_slot)])
         for h in range(2):
             quantise_weights(1, h)
         for m in range(2):
             scalar_scatter(m, H, N, second[:, half(m)])
 
         copy_out(vector_cast, chunk(dense3, 0), 0, 0, [(3, every_slot)])
-        copy_out(vector_cast, probs[1][0][:, half(0)], 6, 1, [(0, half(0))])
+        copy_out(vector_cast, probs[1][1][:, half(0)], 6, 1, [(0, half(0))])
         copy_out(vector_cast, chunk(dense2, 1)[:, half(0)], 5, 1, [(2, half(0))])
-        copy_out(vector_cast, probs[1][0][:, half(1)], 4, 1, [(0, half(1))])
+        copy_out(vector_cast, probs[1][1][:, half(1)], 4, 1, [(0, half(1))])
         copy_out(scalar_cast, first[:], 2, 1, [(1, every_slot)])
         copy_out(scalar_cast, chunk(dense3, 1), 3, 1, [(3, every_slot)])
         copy_out(scalar_cast, chunk(dense2, 1)[:, half(1)], 1, 1, [(2, half(1))])
         for h in range(2):
-            vector_scatter(0, N + h * H, N + (h + 1) * H, probs[1][0][:, half(h)])
+            vector_scatter(0, N + h * H, N + (h + 1) * H, probs[1][1][:, half(h)])
         store(0, nc.sync)
         for h in range(2):
             scalar_scatter(1, N + h * H, N + (h + 1) * H, first[:, half(h)])

@@ -88,9 +88,10 @@ def tile_attend_gat_sig_v_kernel(tc, qT, kT, rw, dom, offs, out):
 
         key_rows = kT.rearrange("(p u e) t -> u p e t", u=2, e=2)
         key_pairs = [tile("key_pairs%d" % u, [P, T], U32) for u in range(2)]
-        front32 = tile("front", [P, 5 * N], F32)
-        late = front32[:, 2 * N - 16 : 5 * N - 16]
-        woven = 2 * EARLY_COLS
+        front32 = tile("front", [P, 6 * N], F32)
+        late = tile("late", [P, 3 * N], F32)
+        grad0_at = 2 * N - 16
+        woven = grad0_at + 2 * EARLY_COLS
         picked = [
             tile("picked0", [P, H, 2], U32)[:],
             front32[:, woven : woven + N].bitcast(U32).rearrange("p (n u) -> p n u", u=2),
@@ -135,7 +136,7 @@ def tile_attend_gat_sig_v_kernel(tc, qT, kT, rw, dom, offs, out):
         q_raw = {}
         dom_raw = {}
         for b in range(B):
-            for h in range(2):
+            for h in (b, 1 - b):
                 if b == 0:
                     raw = (front32[:, woven + N - 64 : woven + 3 * N - 64], shared[:, 2 * N : 4 * N])[h].rearrange("p (j c) -> p j c", j=PACK)
                 else:
@@ -157,8 +158,9 @@ def tile_attend_gat_sig_v_kernel(tc, qT, kT, rw, dom, offs, out):
         grads = [(tile("grad0_codes", [P, DV], U32), planes[:, N - 64 : 2 * N - 64]), operand("grad1", DV)]
 
         front = front32[:].bitcast(BF16)
-        lane = tile("lane", [P, 6 * N], BF16)
-        room = lane[:, 2 * N - 32 : 6 * N - 32]
+        room = front[:, 0 : 4 * N]
+        grad0_room = front[:, 4 * N - 32 : 8 * N - 32]
+        lane = front[:, 8 * N - 64 : 12 * N - 64]
         dense2 = tile("dense2", [P, SLOTS], F32)
         dense3 = tile("dense3", [P, SLOTS], F32)
 
@@ -176,8 +178,8 @@ def tile_attend_gat_sig_v_kernel(tc, qT, kT, rw, dom, offs, out):
             room.rearrange("p (t m j) -> p t m j", t=PACK, j=PACK),
         ]
         back = tile("back", [P, 8 * N], BF16)
-        dom_grouped = [[front[:, 0 : 4 * N], front[:, PACK * EARLY_COLS : 4 * N]], [back[:, 0 : 2 * N], back[:, 2 * N : 4 * N]]]
-        pw = [[lane[:, 0 : 2 * N], lane[:, 0 : 2 * N]], [back[:, 4 * N - 32 : 6 * N - 32], back[:, 6 * N - 32 : 8 * N - 32]]]
+        dom_grouped = [[grad0_room, grad0_room[:, PACK * EARLY_COLS : 4 * N]], [back[:, 0 : 2 * N], back[:, 2 * N : 4 * N]]]
+        pw = [[lane[:, 0 : 2 * N], lane[:, 2 * N - 32 : 4 * N - 32]], [back[:, 4 * N - 32 : 6 * N - 32], back[:, 6 * N - 32 : 8 * N - 32]]]
 
         def query_tile(b, t):
             codes, scales = queries[b]
@@ -296,18 +298,19 @@ def tile_attend_gat_sig_v_kernel(tc, qT, kT, rw, dom, offs, out):
         for m in range(2):
             scalar_scatter(m, 0, H, first[:, half(m)])
 
-        for h in range(2):
-            cast_queries(vector_cast, 1, h, 0, GROUPS)
-        quantise_keys(1, every_slot, picked[2])
-        quantise(queries[1], slice(0, R), room, E4M3)
+        cast_queries(vector_cast, 1, 1, 0, GROUPS)
         gpsimd_cast_grad(0, 1, GPSIMD_COLS, DV - EARLY_COLS)
         for c in range(2, PACK):
             weigh(nc.vector, psum_gates, 0, c)
+        cast_queries(vector_cast, 1, 0, 0, GROUPS)
+        quantise_weights(0, 1)
+        quantise(queries[1], slice(0, R), room, E4M3)
+        for h in range(2):
+            quantise_keys(1, half(h), picked[2][:, half(h)])
         for c in range(PACK):
             sigmoid(1, c, c)
-        cast_grad(vector_cast, 1, 0, 0, H)
-        quantise_weights(0, 1)
-        cast_grad(vector_cast, 1, 1, 0, H)
+        for h in range(2):
+            cast_grad(vector_cast, 1, h, 0, H)
         quantise_grads(0, 1)
         quantise(grads[1], slice(0, DV), back[:, 0 : 4 * N], E5M2)
 
@@ -316,11 +319,11 @@ def tile_attend_gat_sig_v_kernel(tc, qT, kT, rw, dom, offs, out):
         copy_out(vector_cast, second[:], 5, 0, [(m, half(1)) for m in range(2)])
         for c in range(1, PACK):
             weigh(nc.vector, psum_gates, 1, c)
-        copy_out(scalar_cast, chunk(dense2, 0), 1, 0, [(2, every_slot)])
         for h in range(2):
             quantise_weights(1, h)
-        for m in range(2):
-            scalar_scatter(m, H, N, second[:, half(m)])
+        scalar_scatter(0, H, N, second[:, half(0)])
+        copy_out(scalar_cast, chunk(dense2, 0), 1, 0, [(2, every_slot)])
+        scalar_scatter(1, H, N, second[:, half(1)])
 
         copy_out(vector_cast, chunk(dense3, 0), 0, 0, [(3, every_slot)])
         copy_out(vector_cast, probs[1][1][:, half(0)], 6, 1, [(0, half(0))])

@@ -27,9 +27,10 @@ SLOTS = B * N
 
 KEY_LOADS = (((1536, 704), (512, 128)), ((1024, 768), (768, 256), (256, 96)))
 GROUPS = H // PACK
-EARLY_COLS = 224
-GPSIMD_COLS = 208
-FIRST_GROUPS = 48
+EARLY_COLS = 240
+GPSIMD_COLS = (176, 96)
+HELD_COLS = 16
+SCALAR_GROUPS = 28
 LAST_PIECES = ((640, SLOTS), (H, 640), (0, H))
 
 
@@ -88,87 +89,88 @@ def tile_attend_gat_sig_v_kernel(tc, qT, kT, rw, dom, offs, out):
 
         key_rows = kT.rearrange("(p u e) t -> u p e t", u=2, e=2)
         key_pairs = [tile("key_pairs%d" % u, [P, T], U32) for u in range(2)]
-        front32 = tile("front", [P, 6 * N], F32)
         late = tile("late", [P, 3 * N], F32)
-        grad0_at = 2 * N - 16
+        front32 = tile("front", [P, 9 * N], F32)
+        grad0_at = N
         woven = grad0_at + 2 * EARLY_COLS
         picked = [
             tile("picked0", [P, H, 2], U32)[:],
             front32[:, woven : woven + N].bitcast(U32).rearrange("p (n u) -> p n u", u=2),
             late[:, 0 : 2 * N].bitcast(U32).rearrange("p (n u) -> p n u", u=2),
         ]
-
-        shared = tile("shared", [P, 4 * N], F32)
-        pair_rows = shared[:, 0 : 3 * N].bitcast(U32).rearrange("p (u n) -> p u n", u=2)
+        q_at = woven + N - 64
+        rows_at = q_at + 4 * N - 64
+        pair_rows = [
+            tile("pair_rows0", [P, 2, H], U32)[:],
+            front32[:, rows_at : rows_at + 2 * N].bitcast(U32).rearrange("p (u n) -> p u n", u=2),
+        ]
 
         def gather(u, lo, hi):
-            dst = picked[0][:, lo:hi, u] if lo < H else pair_rows[:, u, lo - H : hi - H]
+            dst = picked[0][:, :, u] if lo < H else pair_rows[lo // N][:, u, :]
             nc.vector.tensor_copy(dst, listed(key_pairs[u], lo, hi))
 
-        def interleave(dst, lo, hi):
-            nc.scalar.copy(out=dst, in_=pair_rows[:, :, lo - H : hi - H].rearrange("p u n -> p n u"))
+        def interleave(b):
+            nc.scalar.copy(out=picked[1 + b], in_=pair_rows[b].rearrange("p u n -> p n u"))
 
-        for u in range(2):
+        for step, u in enumerate((1, 0)):
             pairs = key_pairs[u][:].bitcast(BF16).rearrange("p (t e) -> p t e", e=2)
             t0 = 0
-            for i, (width, on_scalar) in enumerate(KEY_LOADS[u]):
-                if (u, i) == (0, 1):
+            for i, (width, on_scalar) in enumerate(KEY_LOADS[step]):
+                if (step, i) == (0, 1):
                     raw = placed.tile([P, 2, width], F32, name="key_raw0_1", offset=0)
                 else:
                     raw = tile("key_raw%d_%d" % (u, i), [P, 2, width], F32)
                 nc.sync.dma_start(out=raw[:], in_=key_rows[u][:, :, t0 : t0 + width])
-                if (u, i) == (0, 0):
+                if (step, i) == (0, 0):
                     nc.sync.dma_start(offsets[:], offs)
                 by_token = raw[:].rearrange("p e t -> p t e")
                 scalar_cast(pairs[:, t0 : t0 + on_scalar, :], by_token[:, 0:on_scalar])
                 vector_cast(pairs[:, t0 + on_scalar : t0 + width, :], by_token[:, on_scalar:width])
                 t0 += width
-            if u == 0:
+            if step == 0:
                 window.append(placed.tile([P, T], F32, name="last_window", offset=0))
                 nc.gpsimd.memset(window[BLOCKS - 1][:], 0.0)
-                gather(0, 0, H)
-                gather(0, H, SLOTS)
+                for lo, hi in ((0, H), (H, N), (N, SLOTS)):
+                    gather(u, lo, hi)
 
-        def load_half(raw, src, h):
-            nc.sync.dma_start(out=raw, in_=src.rearrange("(p j) c -> p j c", j=PACK)[:, :, half(h)])
+        def load(raw, src, lo, hi):
+            nc.sync.dma_start(out=raw, in_=src.rearrange("(p j) c -> p j c", j=PACK)[:, :, lo:hi])
             return raw
 
-        q_raw = {}
-        dom_raw = {}
-        for b in range(B):
-            for h in (b, 1 - b):
-                if b == 0:
-                    raw = (front32[:, woven + N - 64 : woven + 3 * N - 64], shared[:, 2 * N : 4 * N])[h].rearrange("p (j c) -> p j c", j=PACK)
-                else:
-                    raw = tile("q_raw%d_%d" % (b, h), [P, PACK, H], F32)[:]
-                q_raw[b, h] = load_half(raw, qT[b], h)
-            cuts = (0, EARLY_COLS if b == 0 else H, DV)
-            for h in range(2):
-                dom_raw[b, h] = tile("dom_raw%d_%d" % (b, h), [P, PACK, cuts[h + 1] - cuts[h]], F32)[:]
-                rows = dom[b].rearrange("(p j) c -> p j c", j=PACK)
-                nc.sync.dma_start(out=dom_raw[b, h], in_=rows[:, :, cuts[h] : cuts[h + 1]])
+        def raw_tile(name, width):
+            return tile(name, [P, PACK, width], F32)[:]
+
+        q_raw = [load(front32[:, q_at : q_at + 4 * N].rearrange("p (j c) -> p j c", j=PACK), qT[0], 0, R)]
+        dom_raw = {
+            (0, 0): load(raw_tile("dom_raw0_0", EARLY_COLS), dom[0], 0, EARLY_COLS),
+            (0, 1): load(raw_tile("dom_raw0_1", DV - EARLY_COLS), dom[0], EARLY_COLS, DV),
+        }
+        q_raw.append(load(raw_tile("q_raw1", R), qT[1], 0, R))
+        dom_raw[1, 0] = load(raw_tile("dom_raw1", DV), dom[1], 0, DV)
 
         def operand(name, words):
             return tile(name + "_codes", [P, words], U32), tile(name + "_scales", [P, words], U8)
 
-        planes = tile("planes", [P, 2 * N], U8)
+        planes = tile("planes", [P, N], U8)
         keys = [(tile("key0_codes", [P, N], U32), planes[4:P, 0:N]), operand("key1", N)]
         queries = [operand("query%d" % b, R) for b in range(B)]
         weights = [operand("weight%d" % b, N) for b in range(B)]
-        grads = [(tile("grad0_codes", [P, DV], U32), planes[:, N - 64 : 2 * N - 64]), operand("grad1", DV)]
+        grads = [operand("grad%d" % b, DV) for b in range(B)]
 
         front = front32[:].bitcast(BF16)
-        room = front[:, 0 : 4 * N]
-        grad0_room = front[:, 4 * N - 32 : 8 * N - 32]
-        lane = front[:, 8 * N - 64 : 12 * N - 64]
+        grad0_room = front[:, 2 * N : 6 * N]
+        lane_at = PACK * (EARLY_COLS + sum(GPSIMD_COLS) - 8)
+        lane = front[:, 2 * N + lane_at : 4 * N + lane_at]
+        middle = tile("middle", [P, 3 * N], F32)
+        room = middle[:, N - 16 : 3 * N - 16].bitcast(BF16)
         dense2 = tile("dense2", [P, SLOTS], F32)
         dense3 = tile("dense3", [P, SLOTS], F32)
 
         probs = [
             [
-                tile("prob0_0", [P, N], F32)[:],
+                front32[:, grad0_at + 2 * HELD_COLS - N : grad0_at + 2 * HELD_COLS],
                 late[:, 2 * N - 32 : 3 * N - 32],
-                tile("prob0_2", [P, N], F32)[:],
+                middle[:, 0:N],
                 tile("prob0_3", [P, N], F32)[:],
             ],
             [tile("prob1_%d" % c, [P, N], F32)[:] for c in range(PACK - 1)] + [chunk(dense3, 0)],
@@ -178,8 +180,8 @@ def tile_attend_gat_sig_v_kernel(tc, qT, kT, rw, dom, offs, out):
             room.rearrange("p (t m j) -> p t m j", t=PACK, j=PACK),
         ]
         back = tile("back", [P, 8 * N], BF16)
-        dom_grouped = [[grad0_room, grad0_room[:, PACK * EARLY_COLS : 4 * N]], [back[:, 0 : 2 * N], back[:, 2 * N : 4 * N]]]
-        pw = [[lane[:, 0 : 2 * N], lane[:, 2 * N - 32 : 4 * N - 32]], [back[:, 4 * N - 32 : 6 * N - 32], back[:, 6 * N - 32 : 8 * N - 32]]]
+        dom_grouped = [[grad0_room, grad0_room[:, PACK * EARLY_COLS : 4 * N]], [back[:, 0 : 4 * N]]]
+        pw = [[lane, grad0_room[:, 0 : 2 * N]], [back[:, 4 * N - 32 : 6 * N - 32], back[:, 6 * N - 32 : 8 * N - 32]]]
 
         def query_tile(b, t):
             codes, scales = queries[b]
@@ -204,9 +206,9 @@ def tile_attend_gat_sig_v_kernel(tc, qT, kT, rw, dom, offs, out):
         def quantise_keys(b, cols, src):
             quantise(keys[b], cols, src.rearrange("p n u -> p (n u)").bitcast(BF16), E4M3)
 
-        def cast_queries(cast, b, h, lo, hi, tiles=slice(0, PACK)):
-            dst = q_grouped[b].rearrange("p t m j -> p m j t")[:, GROUPS * h + lo : GROUPS * h + hi, :, tiles]
-            cast(dst, q_raw[b, h].rearrange("p j (m t) -> p m j t", t=PACK)[:, lo:hi, :, tiles])
+        def cast_queries(cast, b, lo, hi, tiles):
+            dst = q_grouped[b].rearrange("p t m j -> p m j t")[:, lo:hi, :, tiles]
+            cast(dst, q_raw[b].rearrange("p j (m t) -> p m j t", t=PACK)[:, lo:hi, :, tiles])
 
         def grad_columns(b, h, lo, hi):
             return dom_grouped[b][h][:, PACK * lo : PACK * hi], dom_raw[b, h][:, :, lo:hi]
@@ -269,48 +271,48 @@ def tile_attend_gat_sig_v_kernel(tc, qT, kT, rw, dom, offs, out):
         every_slot = slice(0, N)
 
         for h in range(2):
-            gather(1, h * H, (h + 1) * H)
+            gather(0, h * H, (h + 1) * H)
         quantise_keys(0, half(0), picked[0])
-        cast_queries(scalar_cast, 0, 0, 0, FIRST_GROUPS)
-        cast_queries(scalar_cast, 0, 0, FIRST_GROUPS, GROUPS)
-        cast_queries(vector_cast, 0, 1, 0, GROUPS, slice(2, PACK))
-        cast_queries(vector_cast, 0, 1, 0, GROUPS, slice(0, 2))
-        interleave(picked[1], H, N)
-        gates = shared[:, 3 * N : 3 * N + B * PACK]
+        cast_queries(scalar_cast, 0, 0, 16, slice(0, PACK))
+        cast_queries(scalar_cast, 0, 16, SCALAR_GROUPS, slice(0, PACK))
+        cast_queries(vector_cast, 0, SCALAR_GROUPS, P, slice(2, PACK))
+        cast_queries(vector_cast, 0, SCALAR_GROUPS, P, slice(0, 2))
+        interleave(0)
+        gates = front32[:, 6 * N : 6 * N + B * PACK]
         scalar_cast(gates, psum_gates[:, 0 : B * PACK])
         for t in reversed(range(PACK)):
             quantise(query_tile(0, t), block(0), q_grouped[0][:, t].rearrange("p m j -> p (m j)"), E4M3)
         quantise_keys(0, half(1), picked[1])
-        cast_grad(scalar_cast, 0, 0, 0, EARLY_COLS)
-        gather(1, N, SLOTS)
-        gpsimd_cast_grad(0, 1, 0, GPSIMD_COLS)
+        cast_grad(scalar_cast, 0, 0, HELD_COLS, EARLY_COLS)
+        gather(0, N, SLOTS)
+        gpsimd_cast_grad(0, 1, 0, GPSIMD_COLS[0])
 
-        for c in range(PACK):
-            sigmoid(0, c, c % 3)
+        for c in range(PACK - 1):
+            sigmoid(0, c, c)
         for c in range(2):
             weigh(nc.vector, psum_gates, 0, c)
+        cast_grad(scalar_cast, 0, 0, 0, HELD_COLS)
+        sigmoid(0, PACK - 1, 0)
         quantise_grads(0, 0)
         quantise_weights(0, 0)
-        interleave(picked[2], N, SLOTS)
+        interleave(1)
         first = tile("first", [P, N], F32)
         for m in range(2):
             copy_out(scalar_cast, first[:, half(m)], 4 + 2 * m, 0, [(m, half(0))])
         for m in range(2):
             scalar_scatter(m, 0, H, first[:, half(m)])
 
-        cast_queries(vector_cast, 1, 1, 0, GROUPS)
-        gpsimd_cast_grad(0, 1, GPSIMD_COLS, DV - EARLY_COLS)
+        gpsimd_cast_grad(0, 1, GPSIMD_COLS[0], sum(GPSIMD_COLS))
         for c in range(2, PACK):
             weigh(nc.vector, psum_gates, 0, c)
-        cast_queries(vector_cast, 1, 0, 0, GROUPS)
+        cast_queries(vector_cast, 1, 0, P, slice(0, PACK))
         quantise_weights(0, 1)
         quantise(queries[1], slice(0, R), room, E4M3)
         for h in range(2):
             quantise_keys(1, half(h), picked[2][:, half(h)])
         for c in range(PACK):
             sigmoid(1, c, c)
-        for h in range(2):
-            cast_grad(vector_cast, 1, h, 0, H)
+        cast_grad(vector_cast, 1, 0, 0, DV)
         quantise_grads(0, 1)
         quantise(grads[1], slice(0, DV), back[:, 0 : 4 * N], E5M2)
 

@@ -25,10 +25,10 @@ H = N // 2
 BLOCKS = DV // P
 SLOTS = B * N
 
-KEY_LOADS = (((1536, 704), (512, 128)), ((1024, 768), (768, 256), (256, 96)))
+KEY_LOADS = (((T, 704),), ((1024, 1024), (768, 176), (256, 112)))
 GROUPS = H // PACK
-EARLY_COLS = 240
-GPSIMD_COLS = (176, 96)
+EARLY_COLS = H
+GPSIMD_COLS = (192, 64)
 HELD_COLS = 16
 SCALAR_GROUPS = 28
 LAST_PIECES = ((640, SLOTS), (H, 640), (0, H))
@@ -116,8 +116,8 @@ def tile_attend_gat_sig_v_kernel(tc, qT, kT, rw, dom, offs, out):
             pairs = key_pairs[u][:].bitcast(BF16).rearrange("p (t e) -> p t e", e=2)
             t0 = 0
             for i, (width, on_scalar) in enumerate(KEY_LOADS[step]):
-                if (step, i) == (0, 1):
-                    raw = placed.tile([P, 2, width], F32, name="key_raw0_1", offset=0)
+                if step == 0:
+                    raw = placed.tile([P, 2, width], F32, name="first_pair", offset=0)
                 else:
                     raw = tile("key_raw%d_%d" % (u, i), [P, 2, width], F32)
                 nc.sync.dma_start(out=raw[:], in_=key_rows[u][:, :, t0 : t0 + width])
@@ -125,7 +125,8 @@ def tile_attend_gat_sig_v_kernel(tc, qT, kT, rw, dom, offs, out):
                     nc.sync.dma_start(offsets[:], offs)
                 by_token = raw[:].rearrange("p e t -> p t e")
                 scalar_cast(pairs[:, t0 : t0 + on_scalar, :], by_token[:, 0:on_scalar])
-                vector_cast(pairs[:, t0 + on_scalar : t0 + width, :], by_token[:, on_scalar:width])
+                if on_scalar < width:
+                    vector_cast(pairs[:, t0 + on_scalar : t0 + width, :], by_token[:, on_scalar:width])
                 t0 += width
             if step == 0:
                 window.append(placed.tile([P, T], F32, name="last_window", offset=0))

@@ -330,13 +330,13 @@ def tile_attend_gat_sig_v_kernel(tc, qT, kT, rw, dom, offs, out):
 
         copy_out(vector_cast, chunk(dense3, 0), 0, 0, [(3, every_slot)])
         copy_out(vector_cast, probs[1][1][:, half(0)], 6, 1, [(0, half(0))])
-        copy_out(vector_cast, chunk(dense2, 1)[:, half(0)], 5, 1, [(2, half(0))])
         copy_out(vector_cast, probs[1][1][:, half(1)], 4, 1, [(0, half(1))])
+        vector_scatter(0, N, N + H, probs[1][1][:, half(0)])
+        copy_out(vector_cast, chunk(dense2, 1)[:, half(0)], 6, 1, [(2, half(0))])
         copy_out(scalar_cast, first[:], 2, 1, [(1, every_slot)])
         copy_out(scalar_cast, chunk(dense3, 1), 3, 1, [(3, every_slot)])
         copy_out(scalar_cast, chunk(dense2, 1)[:, half(1)], 1, 1, [(2, half(1))])
-        for h in range(2):
-            vector_scatter(0, N + h * H, N + (h + 1) * H, probs[1][1][:, half(h)])
+        vector_scatter(0, N + H, SLOTS, probs[1][1][:, half(1)])
         store(0, nc.sync)
         for h in range(2):
             scalar_scatter(1, N + h * H, N + (h + 1) * H, first[:, half(h)])

from contextlib import ExitStack

import concourse.mybir as mybir
from concourse.masks import make_identity

B, N, T, D, DV, R = 2, 512, 2048, 512, 512, 512
FLOPS = 2 * B * R * N * D + 2 * B * DV * N * R

F32 = mybir.dt.float32
BF16 = mybir.dt.bfloat16
U32 = mybir.dt.uint32
I32 = mybir.dt.int32
U16 = mybir.dt.uint16
U8 = mybir.dt.uint8
E4M3 = mybir.dt.float8_e4m3fn_x4
E5M2 = mybir.dt.float8_e5m2_x4
COPY = mybir.ActivationFunctionType.Copy
SIGMOID = mybir.ActivationFunctionType.Sigmoid
MULT = mybir.AluOpType.mult
ADD = mybir.AluOpType.add

P = 128
PACK = 4
H = N // 2
BLOCKS = DV // P
SLOTS = B * N

KEY_LOADS = (((T, 704),), ((1024, 1024), (768, 176), (256, 112)))
GROUPS = H // PACK
EARLY_COLS = H
GPSIMD_COLS = (192, 64)
HELD_COLS = 16
SCALAR_GROUPS = 28
LAST_PIECES = ((640, SLOTS), (H, 640), (0, H))


def tile_attend_gat_sig_v_kernel(tc, qT, kT, rw, dom, offs, out):
    nc = tc.nc
    with ExitStack() as ctx:
        keep = ctx.enter_context(tc.tile_pool(name="keep", bufs=1))
        placed = ctx.enter_context(tc.tile_pool(name="placed", bufs=1))
        psum = ctx.enter_context(tc.psum_pool(name="psum", bufs=1))

        def tile(name, shape, dtype):
            return keep.tile(shape, dtype, name=name, align_bytes=64)

        def bank(i):
            return psum.tile([P, N], F32, name="bank%d" % i)

        def scalar_cast(dst, src):
            nc.scalar.activation(out=dst, in_=src, func=COPY)

        def vector_cast(dst, src):
            nc.vector.tensor_copy(out=dst, in_=src)

        def half(h):
            return slice(h * H, (h + 1) * H)

        def block(c):
            return slice(c * P, (c + 1) * P)

        def chunk(wide, c):
            return wide[:, c * N : (c + 1) * N]

        offsets = keep.tile([P, SLOTS // 16], U16, name="offsets")

        def listed(indexed, lo, hi):
            return indexed[:].indirect(offsets[:, lo // 16 : hi // 16])

        gate_rows = tile("gate_rows", [P, R], F32)
        loaded = tile("loaded", [B, R], F32)
        nc.scalar.dma_start(out=loaded[:], in_=rw.rearrange("b r o -> b (r o)"))
        nc.gpsimd.memset(gate_rows[:], 0.0)
        nc.gpsimd.tensor_scalar(out=gate_rows[0:B, :], in0=loaded[:], scalar1=1.0, scalar2=0.0, op0=MULT, op1=ADD)
        identity = tile("identity", [P, P], F32)
        make_identity(nc, identity[:])
        psum_gates = bank(7)
        for t in range(PACK):
            nc.tensor.transpose(psum_gates[:, B * t : B * t + P], gate_rows[:, t:R:PACK], identity[:])

        warm_in = tile("warm_in", [P, 1], F32)
        warm_out = tile("warm_out", [P, 1], F32)
        nc.vector.memset(warm_in[:], 0.0)
        nc.scalar.activation(out=warm_out[:], in_=warm_in[:], func=SIGMOID)

        window = [tile("window%d" % m, [P, T], F32) for m in range(BLOCKS - 1)]
        for m in range(BLOCKS - 1):
            nc.vector.memset(window[m][:].bitcast(I32), 0)

        key_rows = kT.rearrange("(p u e) t -> u p e t", u=2, e=2)
        key_pairs = [tile("key_pairs%d" % u, [P, T], U32) for u in range(2)]
        late = tile("late", [P, 3 * N], F32)
        front32 = tile("front", [P, 9 * N], F32)
        grad0_at = N
        woven = grad0_at + 2 * EARLY_COLS
        picked = [
            tile("picked0", [P, H, 2], U32)[:],
            front32[:, woven : woven + N].bitcast(U32).rearrange("p (n u) -> p n u", u=2),
            late[:, 0 : 2 * N].bitcast(U32).rearrange("p (n u) -> p n u", u=2),
        ]
        q_at = woven + N - 64
        rows_at = q_at + 4 * N - 64
        pair_rows = [
            tile("pair_rows0", [P, 2, H], U32)[:],
            front32[:, rows_at : rows_at + 2 * N].bitcast(U32).rearrange("p (u n) -> p u n", u=2),
        ]

        def gather(u, lo, hi):
            dst = picked[0][:, :, u] if lo < H else pair_rows[lo // N][:, u, :]
            nc.vector.tensor_copy(dst, listed(key_pairs[u], lo, hi))

        def interleave(b):
            nc.scalar.copy(out=picked[1 + b], in_=pair_rows[b].rearrange("p u n -> p n u"))

        for step, u in enumerate((1, 0)):
            pairs = key_pairs[u][:].bitcast(BF16).rearrange("p (t e) -> p t e", e=2)
            t0 = 0
            for i, (width, on_scalar) in enumerate(KEY_LOADS[step]):
                if step == 0:
                    raw = placed.tile([P, 2, width], F32, name="first_pair", offset=0)
                else:
                    raw = tile("key_raw%d_%d" % (u, i), [P, 2, width], F32)
                nc.sync.dma_start(out=raw[:], in_=key_rows[u][:, :, t0 : t0 + width])
                if (step, i) == (0, 0):
                    nc.sync.dma_start(offsets[:], offs)
                by_token = raw[:].rearrange("p e t -> p t e")
                scalar_cast(pairs[:, t0 : t0 + on_scalar, :], by_token[:, 0:on_scalar])
                if on_scalar < width:
                    vector_cast(pairs[:, t0 + on_scalar : t0 + width, :], by_token[:, on_scalar:width])
                t0 += width
            if step == 0:
                window.append(placed.tile([P, T], F32, name="last_window", offset=0))
                nc.gpsimd.memset(window[BLOCKS - 1][:], 0.0)
                for lo, hi in ((0, H), (H, N), (N, SLOTS)):
                    gather(u, lo, hi)

        def load(raw, src, lo, hi):
            nc.sync.dma_start(out=raw, in_=src.rearrange("(p j) c -> p j c", j=PACK)[:, :, lo:hi])
            return raw

        def raw_tile(name, width):
            return tile(name, [P, PACK, width], F32)[:]

        q_raw = [load(front32[:, q_at : q_at + 4 * N].rearrange("p (j c) -> p j c", j=PACK), qT[0], 0, R)]
        dom_raw = {
            (0, 0): load(raw_tile("dom_raw0_0", EARLY_COLS), dom[0], 0, EARLY_COLS),
            (0, 1): load(raw_tile("dom_raw0_1", DV - EARLY_COLS), dom[0], EARLY_COLS, DV),
        }
        q_raw.append(load(raw_tile("q_raw1", R), qT[1], 0, R))
        dom_raw[1, 0] = load(raw_tile("dom_raw1", DV), dom[1], 0, DV)

        def operand(name, words):
            return tile(name + "_codes", [P, words], U32), tile(name + "_scales", [P, words], U8)

        planes = tile("planes", [P, N], U8)
        keys = [(tile("key0_codes", [P, N], U32), planes[4:P, 0:N]), operand("key1", N)]
        queries = [operand("query%d" % b, R) for b in range(B)]
        weights = [operand("weight%d" % b, N) for b in range(B)]
        grads = [operand("grad%d" % b, DV) for b in range(B)]

        front = front32[:].bitcast(BF16)
        grad0_room = front[:, 2 * N : 6 * N]
        lane_at = PACK * (EARLY_COLS + sum(GPSIMD_COLS) - 8)
        lane = front[:, 2 * N + lane_at : 4 * N + lane_at]
        middle = tile("middle", [P, 3 * N], F32)
        room = middle[:, N - 16 : 3 * N - 16].bitcast(BF16)
        dense2 = tile("dense2", [P, SLOTS], F32)
        dense3 = tile("dense3", [P, SLOTS], F32)

        probs = [
            [
                front32[:, grad0_at + 2 * HELD_COLS - N : grad0_at + 2 * HELD_COLS],
                late[:, 2 * N - 32 : 3 * N - 32],
                middle[:, 0:N],
                tile("prob0_3", [P, N], F32)[:],
            ],
            [tile("prob1_%d" % c, [P, N], F32)[:] for c in range(PACK - 1)] + [chunk(dense3, 0)],
        ]
        q_grouped = [
            tile("q_grouped0", [P, 4 * N], BF16)[:].rearrange("p (t m j) -> p t m j", t=PACK, j=PACK),
            room.rearrange("p (t m j) -> p t m j", t=PACK, j=PACK),
        ]
        back = tile("back", [P, 8 * N], BF16)
        dom_grouped = [[grad0_room, grad0_room[:, PACK * EARLY_COLS : 4 * N]], [back[:, 0 : 4 * N]]]
        pw = [[lane, grad0_room[:, 0 : 2 * N]], [back[:, 4 * N - 32 : 6 * N - 32], back[:, 6 * N - 32 : 8 * N - 32]]]

        def query_tile(b, t):
            codes, scales = queries[b]
            if (b, t) == (0, 0):
                return codes[:, block(t)], planes[:, P : 2 * P]
            return codes[:, block(t)], scales[:, block(t)]

        def quantise(dst, cols, src, fmt):
            nc.vector.quantize_mx(out=dst[0][:, cols].bitcast(fmt), scales=dst[1][:, cols], in_=src)

        def multiply(acc, lhs, lhs_cols, lhs_fmt, rhs, rhs_cols):
            nc.tensor.matmul_mx(
                out=acc,
                lhsT=lhs[0][:, lhs_cols].bitcast(lhs_fmt),
                lhsT_scale=lhs[1][:, lhs_cols],
                rhs=rhs[0][:, rhs_cols].bitcast(E4M3),
                rhs_scale=rhs[1][:, rhs_cols],
                start=True,
                stop=True,
            )

        def quantise_keys(b, cols, src):
            quantise(keys[b], cols, src.rearrange("p n u -> p (n u)").bitcast(BF16), E4M3)

        def cast_queries(cast, b, lo, hi, tiles):
            dst = q_grouped[b].rearrange("p t m j -> p m j t")[:, lo:hi, :, tiles]
            cast(dst, q_raw[b].rearrange("p j (m t) -> p m j t", t=PACK)[:, lo:hi, :, tiles])

        def grad_columns(b, h, lo, hi):
            return dom_grouped[b][h][:, PACK * lo : PACK * hi], dom_raw[b, h][:, :, lo:hi]

        def cast_grad(cast, b, h, lo, hi):
            dst, src = grad_columns(b, h, lo, hi)
            cast(dst.rearrange("p (c i j) -> p c j i", i=4, j=PACK), src.rearrange("p j (c i) -> p c j i", i=4))

        def gpsimd_cast_grad(b, h, lo, hi):
            dst, src = grad_columns(b, h, lo, hi)
            nc.gpsimd.tensor_scalar(
                out=dst.rearrange("p (e j) -> p e j", j=PACK),
                in0=src.rearrange("p j e -> p e j"),
                scalar1=1.0,
                scalar2=0.0,
                op0=MULT,
                op1=ADD,
            )

        def quantise_grads(b, h):
            quantise(grads[b], half(h), dom_grouped[b][0][:, 2 * N * h : 2 * N * (h + 1)], E5M2)

        def sigmoid(b, c, where):
            scores = bank(where)[:].rearrange("p (t n) -> p t n", t=PACK)
            for t in reversed(range(PACK)):
                multiply(scores[:, t, :], query_tile(b, t), block(0), E4M3, keys[b], block(c))
            nc.scalar.activation(
                out=probs[b][c].rearrange("p (n t) -> p n t", t=PACK), in_=scores.rearrange("p t n -> p n t"), func=SIGMOID
            )

        def weigh(engine, held, b, c):
            engine.tensor_tensor(
                out=chunk(pw[b][c // 2], c % 2).rearrange("p (n t) -> p n t", t=PACK),
                in0=probs[b][c].rearrange("p (n t) -> p n t", t=PACK),
                in1=held[:, b : B * PACK : B].unsqueeze(1).broadcast_to([P, P, PACK]),
                op=MULT,
            )

        def quantise_weights(b, h):
            quantise(weights[b], half(h), pw[b][h], E4M3)

        def copy_out(cast, dense, where, b, parts):
            acc = bank(where)
            lo = 0
            for m, cols in parts:
                hi = lo + cols.stop - cols.start
                multiply(acc[:, lo:hi], grads[b], block(m), E5M2, weights[b], cols)
                lo = hi
            cast(dense, acc[:, 0:lo])

        def vector_scatter(m, lo, hi, dense):
            nc.vector.tensor_copy(listed(window[m], lo, hi), dense)

        def scalar_scatter(m, lo, hi, dense):
            nc.scalar.activation(out=listed(window[m], lo, hi), in_=dense, func=COPY)

        def store(m, queue):
            queue.dma_start(out=out[block(m), :], in_=window[m][:])

        every_slot = slice(0, N)

        for h in range(2):
            gather(0, h * H, (h + 1) * H)
        quantise_keys(0, half(0), picked[0])
        cast_queries(scalar_cast, 0, 0, 16, slice(0, PACK))
        cast_queries(scalar_cast, 0, 16, SCALAR_GROUPS, slice(0, PACK))
        cast_queries(vector_cast, 0, SCALAR_GROUPS, P, slice(2, PACK))
        cast_queries(vector_cast, 0, SCALAR_GROUPS, P, slice(0, 2))
        interleave(0)
        gates = front32[:, 6 * N : 6 * N + B * PACK]
        scalar_cast(gates, psum_gates[:, 0 : B * PACK])
        for t in reversed(range(PACK)):
            quantise(query_tile(0, t), block(0), q_grouped[0][:, t].rearrange("p m j -> p (m j)"), E4M3)
        quantise_keys(0, half(1), picked[1])
        cast_grad(scalar_cast, 0, 0, HELD_COLS, EARLY_COLS)
        gather(0, N, SLOTS)
        gpsimd_cast_grad(0, 1, 0, GPSIMD_COLS[0])

        for c in range(PACK - 1):
            sigmoid(0, c, c)
        for c in range(2):
            weigh(nc.vector, psum_gates, 0, c)
        cast_grad(scalar_cast, 0, 0, 0, HELD_COLS)
        sigmoid(0, PACK - 1, 0)
        quantise_grads(0, 0)
        quantise_weights(0, 0)
        interleave(1)
        first = tile("first", [P, N], F32)
        for m in range(2):
            copy_out(scalar_cast, first[:, half(m)], 4 + 2 * m, 0, [(m, half(0))])
        for m in range(2):
            scalar_scatter(m, 0, H, first[:, half(m)])

        gpsimd_cast_grad(0, 1, GPSIMD_COLS[0], sum(GPSIMD_COLS))
        for c in range(2, PACK):
            weigh(nc.vector, psum_gates, 0, c)
        cast_queries(vector_cast, 1, 0, P, slice(0, PACK))
        quantise_weights(0, 1)
        quantise(queries[1], slice(0, R), room, E4M3)
        for h in range(2):
            quantise_keys(1, half(h), picked[2][:, half(h)])
        for c in range(PACK):
            sigmoid(1, c, c)
        cast_grad(vector_cast, 1, 0, 0, DV)
        quantise_grads(0, 1)
        quantise(grads[1], slice(0, DV), back[:, 0 : 4 * N], E5M2)

        weigh(nc.gpsimd, gates, 1, 0)
        second = tile("second", [P, N], F32)
        copy_out(vector_cast, second[:], 5, 0, [(m, half(1)) for m in range(2)])
        for c in range(1, PACK):
            weigh(nc.vector, psum_gates, 1, c)
        for h in range(2):
            quantise_weights(1, h)
        scalar_scatter(0, H, N, second[:, half(0)])
        copy_out(scalar_cast, chunk(dense2, 0), 1, 0, [(2, every_slot)])
        scalar_scatter(1, H, N, second[:, half(1)])

        copy_out(vector_cast, chunk(dense3, 0), 0, 0, [(3, every_slot)])
        copy_out(vector_cast, probs[1][1][:, half(0)], 6, 1, [(0, half(0))])
        copy_out(vector_cast, probs[1][1][:, half(1)], 4, 1, [(0, half(1))])
        vector_scatter(0, N, N + H, probs[1][1][:, half(0)])
        copy_out(vector_cast, chunk(dense2, 1)[:, half(0)], 6, 1, [(2, half(0))])
        copy_out(scalar_cast, first[:], 2, 1, [(1, every_slot)])
        copy_out(scalar_cast, chunk(dense3, 1), 3, 1, [(3, every_slot)])
        copy_out(scalar_cast, chunk(dense2, 1)[:, half(1)], 1, 1, [(2, half(1))])
        vector_scatter(0, N + H, SLOTS, probs[1][1][:, half(1)])
        store(0, nc.sync)
        for h in range(2):
            scalar_scatter(1, N + h * H, N + (h + 1) * H, first[:, half(h)])
        store(1, nc.sync)
        vector_scatter(2, 0, SLOTS, dense2[:])
        store(2, nc.sync)
        for lo, hi in LAST_PIECES:
            scalar_scatter(3, lo, hi, dense3[:, lo:hi])
        store(3, nc.sync)
